import numpy as np, ml_dtypes
CORES = [2,3,42,43,82,83,122,123]
N = 8
BF = ml_dtypes.bfloat16
V, HV, LV, K, T, S, EPS, LK = 4096, 2048, 12, 192, 4, 3, 60, 8
def pick(tab, ix):
    return np.take_along_axis(tab, ix[:, :, None, :], 3)
def parts(rng):
    px = np.clip(rng.integers(0, 256, (1, 8, 16, V)) + rng.integers(-48, 49, (N, 8, 16, V)), 0, 255)
    vi = rng.integers(0, V, (N, 8, 16, V))
    few = rng.integers(0, V, (N, 8, 16))
    v = np.where(rng.random((N, 8, K)) < 0.25, np.take_along_axis(few, rng.integers(0, 16, (N, 8, K)), 2), rng.integers(0, V, (N, 8, K)))
    near = np.clip(pick(px, v) + rng.integers(-120, 121, (N, 8, 16, K)), 0, 255)
    z = np.where(rng.random((N, 8, 1, K)) < 0.4, near, rng.integers(0, 256, (N, 8, 16, K)))
    f = rng.integers(0, V, (N, 8, 16, K)); d = rng.integers(0, 4, (N, 8, K))
    return px, vi, z, f, v, d, rng.integers(0, 256, (N, 8, 16)), rng.integers(0, 4096, (N, 8, 16))
def pack(px, vi, z, f, v, d, w, k):
    return {"px": np.ascontiguousarray(px.reshape(N, 128, V)).astype(np.float32).astype(BF), "vw": (vi[..., :HV] + V * vi[..., HV:]).reshape(N, 128, HV).astype(np.int32),
            "z0": z.reshape(N, 128, K).astype(np.float32).astype(BF), "f0": f.reshape(N, 128, K).astype(np.int32), "v0": v.astype(np.int32), "d0": d.astype(np.int32),
            "wt": w.reshape(N, 128, 1).astype(np.int32), "kap": k.reshape(N, 128, 1).astype(np.int32)}
def setup_inputs(rng):
    return pack(*parts(rng))
def setup_inputs_corners(rng):
    px, vi, z, f, v, d, w, k = parts(rng); own = np.arange(V)[None, :]; lane = np.arange(16); i = np.arange(K); one = 0 * i
    for r in range(N):
        for g in range(8):
            m = r + g
            d[r, g] = (one, one + 1, one + 3, 3 * (i & 1))[m & 3]
            v[r, g] = (one + (0, V - 1, HV)[m % 3], rng.permutation(V)[:K], (V - 1) * (i & 1), V - K + i)[(r + (g >> 1)) & 3]
            vi[r, g] = (own + 0 * lane[:, None], V - 1 - own + 0 * lane[:, None], (own + 1 + lane[:, None]) & (V - 1), (V - 1) * rng.integers(0, 2, (16, V)))[g & 3]
            f[r, g] = vi[r, g][:, v[r, g]] if m & 1 else (V - 1) * rng.integers(0, 2, (16, K))
            w[r, g] = (0 * lane, 0 * lane + 255, 255 * (lane == 15), w[r, g])[(m >> 1) & 3]
            k[r, g] = (0 * lane, 0 * lane + 4095, 4095 * (lane == 15), k[r, g])[(r + 3 * g) & 3]
            likes = (i >= 0, i < 0, (i & 1) == 0, (i & 1) == 1, rng.random(K) < 0.5)[(r + 2 * g) % 5]
            x = px[r, g][:, v[r, g]]; z[r, g] = np.where(likes[None, :], x, (x + 128) & 255)
    return pack(px, vi, z, f, v, d, w, k)
def setup_inputs_ends(rng):
    def bits(*shape):
        return rng.integers(0, 2, shape)
    pat = 255 * bits(N, 8, 16, 6); pat[..., 0] = 0; pat[..., 1] = 255; pat[..., 3] = 255 - pat[..., 2]
    px = np.take_along_axis(pat, rng.integers(0, 6, (N, 8, 1, V)), 3)
    px[..., 0] = 0; px[..., V - 1] = 255; px[..., V - 613] = 255
    vi = (V - 1) * bits(N, 8, 16, HV); vi = np.concatenate([vi, vi], axis=3)
    z = 255 * bits(N, 8, 16, K); f = (V - 1) * bits(N, 8, 16, K); v = (V - 1) * bits(N, 8, K); d = 3 * bits(N, 8, K)
    w = 255 * bits(N, 8, 16); w[:, 1::2] = 255; k = 4095 * bits(N, 8, 16); k[..., 15] = 4095
    for h in (0, K - 4):
        z[..., h] = 255; v[..., h] = V - 1
        z[..., h + 1] = 255; v[..., h + 1] = 0; d[..., h + 1] = 3
        z[..., h + 2] = 0; z[:, :, 0, h + 2] = 255; z[:, :, 1, h + 2] = 2; v[..., h + 2] = V - 1
        z[..., h + 3] = 0; v[..., h + 3] = V - 1
    return pack(px, vi, z, f, v, d, w, k)
def setup_inputs_spread(rng):
    px = np.minimum((np.exp2(8 * rng.random((N, 8, 1, V))) * rng.random((N, 8, 16, V))).astype(np.int64), 255)
    z = np.minimum((np.exp2(8 * rng.random((N, 8, 1, K))) * rng.random((N, 8, 16, K))).astype(np.int64), 255)
    vi = np.minimum((V * rng.random((N, 8, 16, V)) ** 3).astype(np.int64), V - 1)
    f = np.minimum((V * rng.random((N, 8, 16, K)) ** 4).astype(np.int64), V - 1)
    v = np.minimum((V * rng.random((N, 8, K)) ** 2).astype(np.int64), V - 1)
    d = np.minimum((4 * rng.random((N, 8, K)) ** 2).astype(np.int64), 3)
    w = np.minimum(np.exp2(8 * rng.random((N, 8, 16))).astype(np.int64), 255); k = np.minimum(np.exp2(12 * rng.random((N, 8, 16))).astype(np.int64), 4095)
    return pack(px, vi, z, f, v, d, w, k)
def setup_inputs_ties(rng):
    px, vi, z, f, v, d, w, k = parts(rng)
    pat = np.broadcast_to(rng.integers(0, 256, (1, 8, 16, 8)), (N, 8, 16, 8))
    px = np.take_along_axis(pat, rng.integers(0, 8, (N, 8, 1, V)), 3)
    v = np.take_along_axis(rng.integers(0, V, (N, 8, 24)), rng.integers(0, 24, (N, 8, K)), 2)
    x = pick(px, v); n = LK - rng.integers(0, 2, (N, 8, 1, K)); o = np.argsort(rng.random((N, 8, 16, K)), axis=2)
    far = EPS + (o >= n).astype(np.int64); z = np.where(x + far <= 255, x + far, x - far)
    vi = np.where(rng.random((N, 8, 16, V)) < 0.2, np.arange(V), vi)
    return pack(px, vi, z, f, v, d, w, k)
def check_inputs(d):
    bad = []
    for a, lo, hi in (("px", 0, 255), ("vw", 0, V * V - 1), ("z0", 0, 255), ("f0", 0, V - 1), ("v0", 0, V - 1), ("d0", 0, 3), ("wt", 0, 255), ("kap", 0, 4095)):
        x = np.asarray(d[a]).astype(np.float64)
        if not (np.min(x) >= lo and np.max(x) <= hi): bad.append("range of " + a)
        if not np.all(x == np.rint(x)): bad.append("whole numbers of " + a)
    return bad
def distances(X, ix, q):
    flat = ix.reshape(N, 8, 16 * K); out = np.zeros((N, 8, 16, K), np.int64)
    for i in range(16):
        out += np.abs(np.take_along_axis(X[:, :, i], flat, 2).reshape(N, 8, 16, K) - q[:, :, i][:, :, None, :])
    return out
def place(view, k):
    return np.take_along_axis(view, k[:, :, None, :], 2)[:, :, 0]
def reference(px, vw, z0, f0, v0, d0, wt, kap):
    X = px.astype(np.int64).reshape(N, 8, 16, V); packed = vw.astype(np.int64).reshape(N, 8, 16, HV)
    vi = np.concatenate([packed & (V - 1), packed >> LV], axis=3)
    z = z0.astype(np.int64).reshape(N, 8, 16, K); f = f0.astype(np.int64).reshape(N, 8, 16, K); v = v0.astype(np.int64); dl = d0.astype(np.int64); A = np.zeros((N, 8, K), np.int64)
    wl = wt.astype(np.int64).reshape(N, 8, 16, 1); kl = kap.astype(np.int64).reshape(N, 8, 16, 1); other = np.arange(K) ^ 1
    for t in range(T):
        x = pick(X, v); e = pick(vi, v)
        like = np.add.reduce((np.abs(x - z) <= EPS).astype(np.int64), axis=2) >= LK + (A & 1); L = like[:, :, None, :]
        u = np.add.reduce(wl * z, axis=2) & (V - 1)
        h = np.where(L, f, (((u[:, :, None, :] * kl) >> 5) + 613 * v[:, :, None, :]) & (V - 1))
        de = distances(X, e, x); dh = distances(X, h, np.where(L, x, z))
        e = np.where(L & (dh < de), h, e)
        for r in range(N):
            for g in range(8):
                j = np.flatnonzero(like[r, g]); users, first = np.unique(v[r, g, j], return_index=True)
                vi[r, g][:, users] = e[r, g][:, j[first]]
        z = np.where(L, (z + x) >> 1, z); A = A + like.astype(np.int64); dl = np.where(like, 0, dl + 1)
        s = np.add.reduce(z, axis=2)
        v = np.where(like, place(e, (s + t) & 15), place(h, np.argmin(dh, axis=2)))
        f = e; second = place(e, (s + t + 8) & 15)
        over = like[:, :, other] & (dl >= 2); O = over[:, :, None, :]
        z = np.where(O, z[..., other], z); f = np.where(O, f[..., other], f); A = np.where(over, A[..., other], A)
        v = np.where(over, second[..., other], v); dl = np.where(over, 0, dl)
        if t < T - 1: z, f, v, A, dl = [np.roll(a, S, axis=0) for a in (z, f, v, A, dl)]
    return {"yw": (vi[..., :HV] + V * vi[..., HV:]).reshape(N, 128, HV).astype(np.float32), "yz": z.reshape(N, 128, K).astype(np.float32), "yf": f.reshape(N, 128, K).astype(np.float32),
            "yv": v.astype(np.float32), "yc": (16 * A + dl).astype(np.float32)}

@@ -1,0 +1,745 @@
+from concourse.mybir import AluOpType as OP, ActivationFunctionType as AF
+
+import numpy as np
+
+NB, n = 2, 96
+M6, BIGM = 6, 12582912.0
+DT = {"F": "float32", "H": "bfloat16", "J": "int32", "U": "uint16"}
+EPE = True
+ABS_E, ABS_H = "SSS", "SSS"
+
+
+def ap(buf, c0, c1, st=1, r0=0, r1=128):
+    return ("ap", buf, r0, r1, c0, c1, st)
+
+
+def sub(a, c0, c1, st=1):
+    return ("ap", a[1], a[2], a[3], a[4] + c0, a[4] + c1, st)
+
+
+def rows(a, r0, r1):
+    return ("ap", a[1], r0, r1, a[4], a[5], a[6])
+
+
+def width(a):
+    return -(-(a[5] - a[4]) // a[6])
+
+
+def build():
+    ops, size, tiles, psn = [], {"F": 0, "H": 0, "J": 0, "U": 0}, {}, [0]
+    cur = [None, -1, "setup"]
+
+    def tile(pool, key, w):
+        k = (pool, key)
+        if k not in tiles:
+            tiles[k] = ap(pool, size[pool], size[pool] + w)
+            size[pool] += -(-w // 16) * 16
+        return tiles[k]
+
+    def ps():
+        psn[0] += 1
+        return ap(("ps", psn[0]), 0, 512)
+
+    def add(e, ins, rd, wr, **kw):
+        o = dict(e=e, ins=ins, x=cur[0], t=cur[1], sec=cur[2], rd=[r for r in rd if isinstance(r, tuple)], wr=wr, i=len(ops))
+        o.update(kw)
+        ops.append(o)
+
+    def two(x):
+        return list(x[1:]) if x[0] == "I" else [x]
+
+    def tt(out, a, b, op):
+        add("V", [("tt", out, a, b, op)], two(a) + [b], two(out))
+
+    def ts(out, a, s1, s2, op0, op1=None):
+        add("V", [("ts", out, a, s1, s2, op0, op1)], two(a) + [s1, s2], two(out))
+
+    def cp(out, a):
+        add("V", [("cp", out, a)], two(a) + ([out[2]] if out[0] == "I" else []), [out[1]] if out[0] == "I" else [out])
+
+    def ms(out, v):
+        add("V", [("ms", out, v)], [], [out])
+
+    def scan(out, d0, d1, init, op0, op1):
+        add("V", [("scan", out, d0, d1, init, op0, op1)], [d0, d1], [out])
+
+    def tr(out, a):
+        add("V", [("tr", out, a)], [a], [out])
+
+    def act(out, a, func, bias=0.0, scale=1.0):
+        add("S", [("act", out, a, func, bias, scale)], two(a) + [bias, scale], [out])
+
+    def mm(group):
+        k = len(group)
+        add("P", [("mm", o, l, r, j == 0, j == k - 1) for j, (o, l, r) in enumerate(group)],
+            [x for _, l, r in group for x in (l, r)], [group[0][0]])
+
+    def iota(out, pattern, base, cm):
+        add("G", [("iota", out, pattern, base, cm)], [], [out])
+
+    def asel(out, a, pattern, cmp, fill, base, cm):
+        add("G", [("asel", out, a, pattern, cmp, fill, base, cm)], [a], [out])
+
+    def dma(out, a, eng="Y"):
+        add(eng, [("dma", out, a)], [a], [out], dma=1)
+
+    def send(out, a, key):
+        add("G", [("rd", out, a, key)], [a], [out], dma=1, remote=1)
+
+    D = lambda nm, c1, r1=128: ap(nm, 0, c1, 1, 0, r1)
+    px, vw, vtab, T613, code = ap("pxs", 0, 4096), ap("vws", 0, 2048), ap("vtab", 0, 4096 + n), ap("t613", 0, 4096), ap("code", 0, 4096)
+    v0i, d0i, f0i = tile("J", "v0i", 192), tile("J", "d0i", 192), tile("J", "f0i", 192)
+    wi, ki, z0s = tile("J", "wi", 1), tile("J", "ki", 1), tile("H", "z0s", 192)
+    ms(v0i, 0)
+    ms(d0i, 0)
+    dma(("ap", "J", 0, 128, v0i[4], v0i[5], 1, 16), D("v0", 192, 8))
+    dma(z0s, D("z0", 192), "S")
+    dma(px, D("px", 4096))
+    dma(("ap", "J", 0, 128, d0i[4], d0i[5], 1, 16), D("d0", 192, 8), "S")
+    dma(wi, D("wt", 1), "S")
+    dma(ki, D("kap", 1), "S")
+    dma(f0i, D("f0", 192), "S")
+    dma(vw, D("vw", 2048))
+    ones, B, I = tile("H", "ones", 512), tile("H", "B", 128), tile("H", "I", 128)
+    ms(ones, 1.0)
+    pi = tile("J", "pi", 1)
+    iota(pi, [[0, 1]], 0, 1)
+    kkf = tile("F", "kkf", n)
+    iota(kkf, [[0, 6], [1, 16]], 0, 0)
+    iota(sub(T613, 0, 64), [[25856, 8], [19616, 8]], 0, 0)
+    t = tile("H", "Bt", 128)
+    asel(t, sub(ones, 0, 128), [[-16, 8], [0, 16]], "is_ge", 0.0, 0, 1)
+    asel(B, t, [[16, 8], [0, 16]], "is_ge", 0.0, 15, -1)
+    asel(I, sub(ones, 0, 128), [[-1, 128]], "is_equal", 0.0, 0, 1)
+    r6 = tile("F", "r6", 6)
+    iota(r6, [[16, 6]], 0, 0)
+    EXP = tile("H", "EXP", 512)
+    for c in range(3):
+        asel(rows(EXP, 32 * c, 32 * c + 32), rows(ones, 32 * c, 32 * c + 32), [[-1, 32], [0, 16]], "is_equal", 0.0, 0, 1)
+    for j in range(6, 12):
+        act(sub(T613, 1 << j, 2 << j), sub(T613, 0, 1 << j), "Copy", float(3232 << j))
+    lane_i, lane = tile("J", "lane", 1), tile("F", "lane", 1)
+    ts(lane_i, pi, 15, None, "bitwise_and")
+    cp(lane, lane_i)
+    MASK, RST, RSTM = tile("F", "MASK", n), tile("F", "RST", n), tile("F", "RSTM", n)
+    ts(MASK, kkf, lane, None, "is_equal")
+    ts(RSTM, kkf, 0.0, None, "not_equal")
+    B32 = tile("F", "B32", 128)
+    cp(B32, B)
+    v0f = tile("F", "v0f", 192)
+    cp(v0f, v0i)
+    vL, vLf = {}, {}
+
+    def pack_v(x, t_next, P):
+        a, b = tile("F", ("pv", x, t_next), n), tile("F", ("pw", x, t_next), n)
+        tt(a, MASK, P, "mult")
+        scan(b, RSTM, a, 0.0, "mult", "add")
+        return sub(b, 15, n, 16)
+
+    def list_v(x, t, v):
+        vL[x], vLf[x] = tile("U", ("vL", x, t), M6), v
+        cp(vL[x], v)
+
+    for x in range(NB):
+        P = ps()
+        mm([(sub(P, 0, n), B32, sub(v0f, x * n, x * n + n))])
+        list_v(x, 0, pack_v(x, 0, sub(P, 0, n)))
+    def scaled(base, s, key):
+        o = tile("H", key, width(base))
+        ts(o, base, float(s), None, "mult")
+        return o
+    SEL, LAST, GR = tile("H", "SEL", 2048), tile("F", "LAST", 128), tile("H", "GR", 1024)
+    nI, Ih, I8, In8, IBIG, In16, In64, I16, I8192 = [scaled(I, s, ("Is", s)) for s in (-1, .5, 8, -8, 131072, -16, -64, 16, 8192)]
+    B2 = scaled(B, 2, "B2")
+    wf, kf, wB = tile("F", "wf", 1), tile("F", "kf", 1), tile("H", "wB", 128)
+    cp(wf, wi)
+    cp(kf, ki)
+    ts(wB, B, wf, None, "mult")
+    Fin, Z, AD = {}, {}, {}
+    d0f = tile("H", "d0f", 192)
+    cp(d0f, d0i)
+    for x in range(NB):
+        Fin[x] = tile("F", ("f0", x), n)
+        cp(Fin[x], sub(f0i, x * n, x * n + n))
+        Z[x] = sub(z0s, x * n, x * n + n)
+        AD[x] = tile("H", ("ad0", x), 2 * n)
+        ms(sub(AD[x], 0, n), 0.0)
+        P = ps()
+        mm([(sub(P, 0, n), B, sub(d0f, x * n, x * n + n))])
+        act(sub(AD[x], n, 2 * n), sub(P, 0, n), "Copy")
+    c0, c1, FL = tile("F", "c0", 1), tile("F", "c1", 1), tile("F", "FL", 16)
+    ts(c0, lane, 12.0, -1.0, "is_lt", "mult")
+    ts(c1, lane, 12.0, None, "is_equal")
+    tt(sub(code, 0, 1), c0, c1, "add")
+    ts(FL, sub(MASK, 0, 16), -2.0, 1.0, "mult", "add")
+    for j in range(12):
+        if j < 10:
+            ts(sub(code, 1 << j, 2 << j), sub(code, 0, 1 << j), sub(FL, j, j + 1), None, "mult")
+        else:
+            act(sub(code, 1 << j, 2 << j), sub(code, 0, 1 << j), "Copy", 0.0, sub(FL, j, j + 1))
+    p16, mo, me = tile("J", "p16", 1), tile("F", "mo", 1), tile("F", "me", 1)
+    ts(p16, pi, 4, 1, "logical_shift_right", "bitwise_and")
+    cp(mo, p16)
+    ts(me, mo, -1.0, 1.0, "mult", "add")
+    m12, m12n = tile("F", "m12", 1), tile("F", "m12n", 1)
+    ts(m12, c1, 64.0, None, "mult")
+    ts(m12n, c1, -64.0, None, "mult")
+    kcol = tile("F", "kcol", 16)
+    for q in range(4):
+        ts(sub(kcol, q, q + 1), lane, -2.0, 2.0 * q + 1, "mult", "add")
+    sc, S16, dmp = tile("F", "sc", 6), tile("H", "S16", 6), tile("F", "dmp", 6)
+    ts(sc, r6, lane, None, "add")
+    ts(S16, sc, 16.0, None, "mult")
+    ts(dmp, sc, 4096.0, None, "add")
+    ts(RST, kkf, 0.0, 1e6, "is_equal", "mult")
+    C80, C1, Cq = tile("H", "C80", n), tile("H", "C1", n), tile("H", "Cq", n)
+    ms(C80, 80.0)
+    ms(C1, 1.0)
+    ms(Cq, -0.25)
+    ts(sub(vtab, 0, 2048), vw, 4095, None, "bitwise_and")
+    ts(sub(vtab, 2048, 4096), vw, 12, None, "logical_shift_right")
+    ms(SEL, 0.0)
+    for b in range(16):
+        cp(sub(SEL, b * 128 + b, b * 128 + 128, 16), sub(B, b, 128, 16))
+    NSEL = tile("H", "NSEL", 2048)
+    act(NSEL, SEL, "Copy", 0.0, -1.0)
+    ts(LAST, B32, sub(MASK, 15, 16), None, "mult")
+    ms(GR, 0.0)
+    for q in range(8):
+        ms(sub(GR, q * 144, q * 144 + 16), 1.0)
+    mat = lambda A, b: sub(A, b * 128, b * 128 + 128)
+    outz, outf, outv, outc = [tile("F", k, 192) for k in ("oz", "of", "ov", "oc")]
+
+    Csave = {}
+    for t in range(4):
+        L, Cx, NLx, over, y, xb, Elist, e0, h, hm, en, src, W, vfs, nxT, nqT, OH1, OH2 = [{} for _ in range(18)]
+        for x in range(NB):
+            cur[:] = [x, t, "like"]
+            sent = ("zad", "zland", "vland", "ff", "fland")
+            k = lambda s: (s, x, t if s in sent else t & 1)
+            z = Z[x]
+            y[x], xb[x] = sub(ps(), 0, n), tile("H", k("x"), n)
+            act(xb[x], ("I", px, vL[x]), "Copy")
+            mm([(y[x], nI, z), (y[x], I, xb[x])])
+            a, b = tile("H", k("c1"), n), tile("H", k("c2"), n)
+            ts(a, y[x], 60.0, None, "is_le")
+            ts(b, y[x], -60.0, None, "is_ge")
+            P = ps()
+            grp = []
+            if t == 1:
+                grp = [(sub(P, 0, n), nI, sub(AD[x], 0, n))]
+            elif t > 1:
+                for q in (1.0, 3.0)[:t - 1]:
+                    par = tile("H", k(("par", q)), n)
+                    ts(par, sub(AD[x], 0, n), q, None, "is_equal")
+                    grp.append((sub(P, 0, n), nI, par))
+            mm(grp + [(sub(P, 0, n), B, a), (sub(P, 0, n), B, b)])
+            L[x] = tile("H", k("L"), n)
+            ts(L[x], sub(P, 0, n), 24.0, None, "is_ge")
+            cur[2] = "hash"
+            U = ps()
+            mm([(sub(U, 0, n), wB, z)])
+            ui, uj, uh, us = [tile("J", k(("u", q)), n) for q in range(4)]
+            up = tile("F", k("up"), n)
+            cp(ui, sub(U, 0, n))
+            ts(uj, ui, 4095, None, "bitwise_and")
+            ts(up, uj, kf, -15728640.0, "mult", "add")
+            tt(uh, ("I", T613, vL[x]), up, "add")
+            ts(us, uh, 5, 4095, "arith_shift_right", "bitwise_and")
+            vp = "vps%d" % x
+            hf, m = ap(vp, 384, 384 + n), ap(vp, 0, n)
+            tt(hf, Fin[x], us, "subtract")
+            tt(m, hf, L[x], "mult")
+            h[x] = tile("F", k("h"), n)
+            tt(h[x], us, m, "add")
+            Hl = tile("U", k("Hl"), n)
+            cp(Hl, h[x])
+            cur[2] = "E"
+            Elist[x] = tile("U", k("El"), n)
+            cp(Elist[x], ("I", vtab, vL[x]))
+            e0[x] = ap(vp, 96, 96 + n)
+            cp(e0[x], Elist[x])
+            cur[2] = "q"
+            Ly = tile("H", k("Ly"), n)
+            tt(Ly, y[x], L[x], "mult")
+            P = ps()
+            mm([(rows(sub(P, 0, 128), 0, n), z, I), (rows(sub(P, 0, 128), 0, n), Ly, I)])
+            nqT[x] = tile("H", k("nqT"), 128)
+            act(rows(nqT[x], 0, n), rows(sub(P, 0, 128), 0, n), "Copy", 0.0, -1.0)
+            P = ps()
+            mm([(rows(sub(P, 0, 128), 0, n), xb[x], I)])
+            nxT[x] = tile("H", k("nxT"), 128)
+            act(rows(nxT[x], 0, n), rows(sub(P, 0, 128), 0, n), "Copy", 0.0, -1.0)
+            da, de = tile("H", ("da", x), 16 * n), tile("H", ("de", x), 16 * n)
+            for which, lst, nT, dist, eng, abse in (("E", Elist[x], nxT[x], de, "V", ABS_E), ("H", Hl, nqT[x], da, "S", ABS_H)):
+                cur[2] = which
+                raw = tile("H", ("raw", which, x), 16 * n)
+                for c in range(3):
+                    r, dd = sub(raw, 512 * c, 512 * c + 512), sub(dist, 512 * c, 512 * c + 512)
+                    win = ("I", px, sub(lst, 32 * c, 32 * c + 32))
+                    if eng == "V":
+                        cp(r, win)
+                    else:
+                        act(r, win, "Copy")
+                    P = ps()
+                    mm([(P, I, r), (P, rows(nT, 32 * c, 32 * c + 32), rows(EXP, 32 * c, 32 * c + 32))])
+                    act(dd, P, "Abs")
+            Dp = ps()
+            mm([(sub(Dp, 0, n), I8192, L[x])] + [(sub(Dp, 0, n), mat(SEL, q), sub(de, q, 16 * n, 16)) for q in range(16)])
+            Ds = tile("F", k("Ds"), n)
+            act(Ds, sub(Dp, 0, n), "Copy", -8192.0)
+            Dh = ps()
+            mm([(sub(Dh, 0, n), mat(SEL, q), sub(da, q, 16 * n, 16)) for q in range(16)])
+            cur[2] = "count"
+            P = ps()
+            mm([(sub(P, 0, 2 * n), I, AD[x]), (sub(P, 0, n), I, L[x]), (sub(P, n, 2 * n), In16, L[x]), (sub(P, n, 2 * n), I, C1)])
+            AD1 = tile("H", k("AD1"), 2 * n)
+            act(AD1, sub(P, 0, 2 * n), "Relu")
+            P = ps()
+            mm([(sub(P, 0, n), I, sub(AD1, n, 2 * n)), (sub(P, 0, n, 2), I8, sub(L[x], 1, n, 2)), (sub(P, 1, n, 2), I8, sub(L[x], 0, n, 2))])
+            over[x] = tile("H", k("ov"), n)
+            ts(over[x], sub(P, 0, n), 10.0, None, "is_ge")
+            P = ps()
+            mm([(sub(P, 0, 6), I, S16)] + [(sub(P, 0, 6), mat(NSEL if q & 1 else SEL, q), sub(over[x], q, n, 16)) for q in range(16)])
+            src[x] = tile("U", k("src"), 6)
+            ts(src[x], sub(P, 0, 6), 0.0625, None, "mult")
+            P = ps()
+            mm([(sub(P, 0, n), I, Cq), (sub(P, 0, n), I, z), (sub(P, 0, n), Ih, Ly)])
+            z1 = tile("H", k("z1"), n)
+            ts(z1, sub(P, 0, n), BIGM, BIGM, "add", "subtract")
+            zad = tile("H", k("zad"), 3 * n)
+            if t < 3:
+                act(sub(zad, 0, n), ("I", z1, src[x]), "Copy")
+            else:
+                act(sub(outz, x * n, x * n + n), ("I", z1, src[x]), "Copy")
+            act(sub(zad, n, 2 * n), ("I", sub(AD1, 0, n), src[x]), "Copy")
+            act(sub(zad, 2 * n, 3 * n), ("I", sub(AD1, n, 2 * n), src[x]), "Copy")
+            if t < 3:
+                land = tile("H", k("zland"), 3 * n)
+                send(land, zad, ("z", x, t))
+                Z[x], AD[x] = sub(land, 0, n), sub(land, n, 3 * n)
+            else:
+                P = ps()
+                mm([(sub(P, 0, n), I16, sub(zad, n, 2 * n)), (sub(P, 0, n), I, sub(zad, 2 * n, 3 * n))])
+                act(sub(outc, x * n, x * n + n), sub(P, 0, n), "Copy")
+            cur[2] = "place"
+            P = ps()
+            mm([(sub(P, 0, n), B2, z1), (sub(P, 0, n), nI, L[x])])
+            wi_, w31 = tile("J", k("wi"), n), tile("J", k("w31"), n)
+            ts(wi_, sub(P, 0, n), sub(kcol, t, t + 1), None, "add")
+            ts(w31, wi_, 31, None, "bitwise_and")
+            OH1[x], OH2[x] = ap(vp, 192, 192 + n), ap(vp, 288, 288 + n)
+            ts(OH1[x], w31, 0.0, None, "is_equal")
+            P = ps()
+            mm([(sub(P, 0, n), I, C80), (sub(P, 0, n, 2), In64, sub(over[x], 1, n, 2)), (sub(P, 1, n, 2), In64, sub(over[x], 0, n, 2))])
+            tt(OH2[x], w31, sub(P, 0, n), "is_equal")
+            cur[2] = "e"
+            hmx = tile("F", k("hm"), n)
+            tt(hmx, h[x], e0[x], "subtract")
+            cc, chm = ap(vp, 0, n), tile("F", k("chm"), n)
+            tt(cc, sub(Dh, 0, n), Ds, "is_lt")
+            tt(chm, hmx, cc, "mult")
+            en[x] = tile("F", k("en"), n)
+            tt(en[x], chm, e0[x], "add")
+            W1, W2, W3 = [tile("F", k(("W", q)), n) for q in range(3)]
+            cur[2] = "least"
+            key, k1, k2, k3 = [tile("F", k(("key", q)), n) for q in range(4)]
+            ts(key, sub(Dh, 0, n), 16.0, lane, "mult", "add")
+            tr(k1, key)
+            scan(k2, RST, k1, 1e6, "add", "min")
+            tr(k3, k2)
+            P = ps()
+            mm([(sub(P, 0, n), IBIG, L[x]), (sub(P, 0, n), IBIG, over[x]), (sub(P, 0, n), LAST, k3)])
+            oh3 = ap(vp, 0, n)
+            tt(oh3, key, sub(P, 0, n), "is_equal")
+            tt(W3, h[x], oh3, "mult")
+            tt(W1, OH1[x], en[x], "mult")
+            tt(sub(W2, 0, n, 2), sub(OH2[x], 1, n, 2), sub(en[x], 1, n, 2), "mult")
+            tt(sub(W2, 1, n, 2), sub(OH2[x], 0, n, 2), sub(en[x], 0, n, 2), "mult")
+            P = ps()
+            mm([(sub(P, 0, n), B32, w) for w in (W1, W2, W3)])
+            vold, vfold = vL[x], vLf[x]
+            if t < 3:
+                ff, land = sub(tile("F", k("ff"), n + 16), 0, n + M6), sub(tile("F", k("fland"), n + 16), 0, n + M6)
+                act(sub(ff, 0, n), ("I", en[x], src[x]), "Copy")
+                cp(sub(ff, n, n + M6), pack_v(x, t + 1, sub(P, 0, n)))
+                send(land, ff, ("f", x, t))
+                Fin[x] = sub(land, 0, n)
+                list_v(x, t + 1, sub(land, n, n + M6))
+            else:
+                act(sub(outv, x * n, x * n + n), sub(P, 0, n), "Copy")
+                act(sub(outf, x * n, x * n + n), ("I", en[x], src[x]), "Copy")
+            cur[2] = "write"
+            C, Ce, Co = [tile("H", k(("C", q)), n) for q in range(3)]
+            nl = ap(vp, 384, 384 + n)
+            act(C, ("I", code, vold), "Copy")
+            ts(Ce, C, me, None, "mult")
+            ts(Co, C, mo, None, "mult")
+            ts(nl, L[x], m12, m12n, "mult", "add")
+            Cn = tile("H", k("Cn"), n)
+            tt(Cn, C, nl, "add")
+            Csave[x] = (Cn,)
+            cnt = []
+            for x2 in range(x + 1):
+                E = tile("H", k(("E", x2)), 8 * n)
+                for pb in range(4):
+                    P = ps()
+                    o = rows(sub(P, 0, 2 * n), 0, n)
+                    same = x2 == x
+                    grp = []
+                    for q in range(2):
+                        oo = rows(sub(P, n * q, n * q + n), 0, n)
+                        r = rows(Co if q else Ce, 32 * pb, 32 * pb + 32)
+                        for w, l in enumerate(Csave[x2]):
+                            grp.append(("mm", oo, rows(l, 32 * pb, 32 * pb + 32), r, True, True))
+                    add("P", grp, [Ce, Co] + list(Csave[x2]), [o])
+                    act(rows(sub(E, 2 * n * pb, 2 * n * pb + 2 * n), 0, n), o, "Relu", -12.0)
+                if same:
+                    asel(rows(E, 0, n), rows(E, 0, n), [[0, 8], [1, n]], "is_ge", 0.0, -1, -1)
+                cnt += [(rows(mat(GR, q), 0, n), rows(sub(E, n * q, n * q + n), 0, n)) for q in range(8)]
+            P = ps()
+            mm([(sub(P, 0, n), In8, L[x])] + [(sub(P, 0, n), l, r) for l, r in cnt])
+            win = tile("H", k("win"), n)
+            ts(win, sub(P, 0, n), -7.5, 0.0625, "is_lt", "mult")
+            P = ps()
+            mm([(sub(P, 0, 6), mat(SEL, q), sub(win, q, n, 16)) for q in range(16)])
+            vmd, tq, off = [tile("F", k(("o", q)), 6) for q in range(3)]
+            tt(vmd, vfold, dmp, "subtract")
+            tt(tq, vmd, sub(P, 0, 6), "mult")
+            tt(off, tq, dmp, "add")
+            W[x] = tile("U", k("off"), 6)
+            cp(W[x], off)
+        for x in range(NB):
+            cur[:] = [x, t, "write"]
+            cp(("I", vtab, W[x]), en[x])
+    cur[:] = [None, 4, "out"]
+    for o, nm in ((outz, "yz"), (outf, "yf")):
+        dma(D(nm, 192), o)
+    for o, nm in ((outv, "yv"), (outc, "yc")):
+        dma(D(nm, 192, 8), ("ap", "F", 0, 128, o[4], o[5], 1, 16))
+    for c in range(4):
+        q = ap("vps%d" % (c & 1), 0, 512)
+        o = tile("F", ("yw", c), 512)
+        ts(q, sub(vtab, 2048 + 512 * c, 2560 + 512 * c), 4096.0, None, "mult")
+        tt(o, sub(vtab, 512 * c, 512 * c + 512), q, "add")
+        dma(ap("yw", 512 * c, 512 * c + 512), o, "YS"[c & 1])
+    return ops, size
+
+
+def pat(a):
+    return a[7] if len(a) > 7 else 1
+
+
+def cost(o):
+    c = 0.0
+    for i in o["ins"]:
+        k = i[0]
+        if k == "mm":
+            f = 4 if i[2][1] == "F" else 1
+            c += f * max(64, width(i[3])) * .42e-3
+        elif k in ("iota", "asel"):
+            c += .15 + 1.7e-3 * width(i[1])
+        elif k == "dma":
+            c += .06
+        elif k == "rd":
+            c += .8
+        else:
+            out = i[1][1] if i[1][0] == "I" else i[1]
+            w = width(i[2][2]) * 16 if k != "ms" and i[2][0] == "I" else width(out)
+            b16 = lambda a: a[0] != "I" and a[1] in ("H", "U", "code")
+            if i[1][0] == "I":
+                w = 3.5 * width(i[1][2]) * 16
+            elif k != "ms" and i[2][0] == "I":
+                w = 1.5 * w
+            elif k == "tt":
+                ps_ = any(isinstance(a[1], tuple) or a[1] in ("vps0", "vps1") for a in i[2:4])
+                w = w * (1 if ps_ else 2)
+            elif k in ("cp", "ts") and b16(i[1]) and b16(i[2]) or k == "ms" and b16(i[1]):
+                w = w * .5
+            c += max(64, w) * .83e-3 + (.01 if i[2:] else 0)
+    return c
+
+
+WAKE, OWN, NET, LOADT = .12, .06, 2.6, 2.0
+SCALE = 1.2
+SECT = {("E", 0): 2.6, ("H", 0): 2.9, ("count", 0): 7.3, ("e", 0): 3.0, ("hash", 0): 3.0, ("least", 0): 1.9, ("like", 0): 3.0, ("place", 0): 4.3,
+        ("q", 0): 3.0, ("write", 0): 3.0, ("hash", 1): -0.5, ("E", 1): -2.5, ("H", 1): -2.0, ("out", None): -20.2, ("q", 1): 0.7, ("like", 1): 4.2,
+        ("place", 1): 4.6, ("count", 1): 0.5}
+SEEDS = [(977194, 0.004, 8.0), (73801, 0.004, 8.0), (621379, 0.03, 3.0), (792181, 0.004, 1.0), (493328, 0.004, 3.0), (139368, 0.01, 1.0),
+         (828585, 0.01, 3.0), (445549, 0.03, 1.0), (186910, 0.03, 1.0), (256747, 0.004, 3.0), (625478, 0.01, 1.0), (890177, 0.01, 1.0)]
+
+
+def analyse():
+    ops, size = build()
+    N = len(ops)
+    hist = {}
+    deps = [set() for _ in range(N)]
+    tile_ops = {}
+    for o in ops:
+        i = o["i"] = ops.index(o) if ops[o["i"]] is not o else o["i"]
+    for o in ops:
+        i = o["i"]
+        for kind, lst in (("r", o["rd"]), ("w", o["wr"])):
+            for a in lst:
+                buf = a[1]
+                if isinstance(buf, tuple):
+                    tile_ops.setdefault(buf, [])
+                    if i not in tile_ops[buf]:
+                        tile_ops[buf].append(i)
+                for (lo, hi, k2, j, st) in hist.setdefault(buf, []):
+                    if j != i and (k2 == "w" or kind == "w") and lo < a[5] and a[4] < hi:
+                        if st == a[6] > 1 and (lo - a[4]) % st:
+                            continue
+                        deps[i].add(j)
+        for kind, lst in (("r", o["rd"]), ("w", o["wr"])):
+            for a in lst:
+                hh = hist[a[1]]
+                if kind == "w":
+                    hist[a[1]] = hh = [e for e in hh if not (a[6] == 1 and a[2] == 0 and a[3] == 128 and pat(a) == 1 and a[4] <= e[0] and e[1] <= a[5] and a[1] != "vtab")]
+                hh.append((a[4], a[5], kind, i, a[6]))
+    pool = [o["i"] for o in ops if o["e"] == "G" and not o.get("dma")]
+    for a, b in zip(pool, pool[1:]):
+        deps[b].add(a)
+    cst = [cost(o) * (1.0 if o.get("dma") else SCALE) for o in ops]
+    lat = []
+    for o in ops:
+        if o.get("remote"):
+            lat.append(NET)
+        elif o.get("dma"):
+            w = max(width(a) for a in o["wr"])
+            lat.append(LOADT + w * 1.1e-3)
+        else:
+            lat.append(0.0)
+    prio = [0.0] * N
+    succ = [[] for _ in range(N)]
+    for i in range(N):
+        for j in deps[i]:
+            succ[j].append(i)
+    for i in range(N - 1, -1, -1):
+        prio[i] = cst[i] + lat[i] + max([prio[s] + .1 for s in succ[i]] + [0.0])
+    for i in range(N):
+        prio[i] += SECT.get((ops[i]["sec"], ops[i]["x"]), 0.0)
+    return dict(ops=ops, size=size, deps=deps, succ=succ, tile_ops=tile_ops, cst=cst, lat=lat, prio=prio)
+
+
+def nudge(prio, seeds):
+    prio = list(prio)
+    for s, frac, sig in seeds:
+        r = np.random.default_rng(s)
+        hit, by = r.random(len(prio)) < frac, r.normal(size=len(prio)) * sig
+        prio = [float(p + b) if h else p for p, h, b in zip(prio, hit, by)]
+    return prio
+
+
+def schedule(an, prio):
+    ops, deps, succ, tile_ops, cst, lat = an["ops"], an["deps"], an["succ"], an["tile_ops"], an["cst"], an["lat"]
+    N = len(ops)
+    ptile = [next((a[1] for a in o["wr"] if isinstance(a[1], tuple)), None) for o in ops]
+    ptouch = [set(a[1] for a in o["rd"] + o["wr"] if isinstance(a[1], tuple)) for o in ops]
+    eng = [o["e"] for o in ops]
+    isdma = [bool(o.get("dma")) for o in ops]
+    bank_tiles = [[] for _ in range(6)]
+    bank_of, left = {}, {b: len(v) for b, v in tile_ops.items()}
+    fin, free = [None] * N, {}
+    start = [None] * N
+    order = {e: [] for e in "VSPGY"}
+    ndep = [len(d) for d in deps]
+    ready = [i for i in range(N) if ndep[i] == 0]
+    rt = {i: 0.0 for i in ready}
+    extra = [set() for _ in range(N)]
+    done = 0
+    while done < N:
+        best = None
+        for i in ready:
+            s = max(free.get(eng[i], 0.0), rt[i])
+            bk = None
+            if best is not None and round(s / .04) > best[0][0]:
+                continue
+            if ptile[i] is not None and ptile[i] not in bank_of:
+                cand = []
+                for b in range(6):
+                    bt = bank_tiles[b]
+                    if not bt or left[bt[-1]] == 0:
+                        f = max([fin[j] for j in tile_ops[bt[-1]]]) + WAKE if bt else 0.0
+                        cand.append((f, b))
+                if not cand:
+                    continue
+                f, bk = min(cand)
+                s = max(s, f)
+            key = (round(s / .04), -prio[i], i)
+            if best is None or key < best[0]:
+                best = (key, s, i, bk)
+        key, s, i, bk = best
+        o = ops[i]
+        ready.remove(i)
+        if bk is not None:
+            tb = ptile[i]
+            if bank_tiles[bk]:
+                extra[i] |= set(tile_ops[bank_tiles[bk][-1]])
+            bank_tiles[bk].append(tb)
+            bank_of[tb] = bk
+        for tb in ptouch[i]:
+            left[tb] -= 1
+        start[i], fin[i] = s, s + cst[i] + lat[i]
+        free[o["e"]] = s + cst[i]
+        order[o["e"]].append(i)
+        done += 1
+        for q in succ[i]:
+            w = OWN if eng[q] == eng[i] and not isdma[i] else WAKE
+            rt[q] = max(rt.get(q, 0.0), fin[i] + w)
+            ndep[q] -= 1
+            if ndep[q] == 0:
+                ready.append(q)
+    return dict(order=order, start=start, fin=fin, extra=extra, bank_of=bank_of, span=max(fin))
+
+
+def plan():
+    an = analyse()
+    sc = schedule(an, nudge(an["prio"], SEEDS))
+    ops, deps, order, extra, fin = an["ops"], an["deps"], sc["order"], sc["extra"], sc["fin"]
+    N = len(ops)
+    cnt = {e: 0 for e in "VSPG"}
+    end, K, clk, waits = {}, {e: {} for e in "VSPGY"}, [None] * N, [None] * N
+    ndma = 0
+    for e in "VSPGY":
+        pos = {i: p for p, i in enumerate(order[e])}
+        for i in order[e]:
+            if ops[i].get("dma"):
+                end[i] = (("d", ndma), 0)
+                ndma += 1
+            else:
+                cnt[e] += len(ops[i]["ins"])
+                end[i] = (e, cnt[e])
+    todo = {e: list(order[e]) for e in order}
+    emitted = set()
+    while any(todo.values()):
+        moved = False
+        for e in "VSPGY":
+            while todo[e] and all(d in emitted for d in deps[todo[e][0]] | extra[todo[e][0]]):
+                i = todo[e].pop(0)
+                ws = []
+                dd = sorted(deps[i] | extra[i], key=lambda d: -fin[d])
+                for d in dd:
+                    s, c = end[d]
+                    if K[e].get(s, -1) >= c:
+                        continue
+                    ws.append(d)
+                    for a, b in clk[d].items():
+                        K[e][a] = max(K[e].get(a, -1), b)
+                fw = {}
+                for d in ws:
+                    s, c = end[d]
+                    if s not in fw or end[fw[s]][1] < c:
+                        fw[s] = d
+                waits[i] = list(fw.values())
+                c = dict(K[e])
+                c[end[i][0]] = max(c.get(end[i][0], -1), end[i][1])
+                clk[i] = c
+                emitted.add(i)
+                moved = True
+        assert moved
+    return dict(ops=ops, size=an["size"], order=order, waits=waits, end=end, bank_of=sc["bank_of"], cnt=cnt, ndma=ndma, span=sc["span"])
+
+
+PLAN = plan()
+_s = PLAN["size"]
+SCRATCH = {
+    "pxs": ("sbuf", [128, 4096], "bfloat16"), "vws": ("sbuf", [128, 2048], "int32"), "vtab": ("sbuf", [128, 4096 + n], "int32"),
+    "t613": ("sbuf", [128, 4096], "float32"), "code": ("sbuf", [128, 4096], "bfloat16"),
+}
+for _k in "FHJU":
+    SCRATCH[_k + "pool"] = ("sbuf", [128, _s[_k]], DT[_k])
+for _k in ["ps%d" % _b for _b in range(6)] + ["vps0", "vps1"]:
+    SCRATCH[_k] = ("psum", [128, 512], "float32")
+SEMAPHORES = ["eV", "eS", "eP", "eG", "sent"] + ["d%d" % k for k in range(PLAN["ndma"])]
+
+
+def rank_program(g, core, T, topo):
+    rank = T.rank_of(core)
+    if rank is None:
+        return
+    p = PLAN
+    ops, bank_of, end = p["ops"], p["bank_of"], p["end"]
+    q = {"V": g.vector, "S": g.scalar, "P": g.tensor, "G": g, "Y": g.sync}
+    esem = {e: T.sem["e" + e] for e in "VSPG"}
+    dst = T.cores[(rank + 3) % 8]
+    rid, pid, _ = topo.addr(dst)
+    mask, neng = topo.mask(core, dst), len(topo.engines(core, dst))
+
+    def A(a):
+        if not isinstance(a, tuple):
+            return a
+        if a[0] == "I":
+            return A(a[1]).indirect(A(a[2]))
+        buf = a[1]
+        if isinstance(buf, tuple):
+            t = T["ps%d" % bank_of[buf]]
+        elif buf in DT:
+            t = T[buf + "pool"]
+        else:
+            t = T[buf]
+        if pat(a) > 1:
+            return t[a[2]:a[3]:a[7], a[4]:a[5]]
+        return t[a[2]:a[3], a[4]:a[5]] if a[6] == 1 else t[a[2]:a[3], a[4]:a[5]:a[6]]
+
+    def op(s):
+        return {"add": OP.add, "subtract": OP.subtract, "mult": OP.mult, "min": OP.min, "max": OP.max, "is_ge": OP.is_ge, "is_le": OP.is_le,
+                "is_lt": OP.is_lt, "is_equal": OP.is_equal, "not_equal": OP.not_equal, "bitwise_and": OP.bitwise_and,
+                "arith_shift_right": OP.arith_shift_right, "logical_shift_right": OP.logical_shift_right}[s]
+
+    fun = {"Copy": AF.Copy, "Abs": AF.Abs, "Relu": AF.Relu, "Identity": AF.Identity}
+    nsent = 0
+    total = {}
+    for e in "VSPGY":
+        for i in p["order"][e]:
+            o = ops[i]
+            for d in p["waits"][i]:
+                s, c = end[d]
+                if s in esem:
+                    q[e].wait_ge(esem[s], c)
+                else:
+                    q[e].wait_ge(T.sem["d%d" % s[1]], neng if ops[d].get("remote") else 16)
+            for s in o["ins"]:
+                k = s[0]
+                if k == "dma":
+                    x = q[e].dma_start(A(s[1]), A(s[2]))
+                    x.then_inc(T.sem["d%d" % end[i][0][1]], 16)
+                    total[end[i][0][1]] = 16
+                    continue
+                if k == "rd":
+                    g.remote_dma(out_ap=A(s[1]), in_ap=A(s[2]), remote_sem=T.sem["d%d" % end[i][0][1]], local_sem=T.sem.sent, pid=pid, routing_id=rid, dma_engine_mask=mask)
+                    nsent += neng
+                    total[end[i][0][1]] = neng
+                    continue
+                if k == "tt":
+                    x = g.vector.tensor_tensor(out=A(s[1]), in0=A(s[2]), in1=A(s[3]), op=op(s[4]))
+                elif k == "ts":
+                    if s[6] is None:
+                        x = g.vector.tensor_scalar(out=A(s[1]), in0=A(s[2]), scalar1=A(s[3]), scalar2=None, op0=op(s[5]))
+                    else:
+                        x = g.vector.tensor_scalar(out=A(s[1]), in0=A(s[2]), scalar1=A(s[3]), scalar2=A(s[4]), op0=op(s[5]), op1=op(s[6]))
+                elif k == "cp":
+                    x = g.vector.tensor_copy(out=A(s[1]), in_=A(s[2]))
+                elif k == "tr":
+                    x = g.vector.transpose(out=A(s[1]), in_=A(s[2]))
+                elif k == "ms":
+                    x = g.vector.memset(A(s[1]), s[2])
+                elif k == "scan":
+                    x = g.vector.tensor_tensor_scan(out=A(s[1]), data0=A(s[2]), data1=A(s[3]), initial=s[4], op0=op(s[5]), op1=op(s[6]))
+                elif k == "act":
+                    x = g.scalar.activation(out=A(s[1]), in_=A(s[2]), func=fun[s[3]], bias=A(s[4]), scale=A(s[5]))
+                elif k == "mm":
+                    x = g.tensor.matmul(out=A(s[1]), lhsT=A(s[2]), rhs=A(s[3]), start=s[4], stop=s[5])
+                elif k == "iota":
+                    if s[1][1] in ("F", "H", "t613"):
+                        x = g.iota(out=A(s[1]), pattern=s[2], base=s[3], channel_multiplier=s[4], allow_small_or_imprecise_dtypes=True)
+                    else:
+                        x = g.iota(out=A(s[1]), pattern=s[2], base=s[3], channel_multiplier=s[4])
+                elif k == "asel":
+                    x = g.affine_select(out=A(s[1]), in_=A(s[2]), pattern=s[3], compare_op=op(s[4]), fill=s[5], base=s[6], channel_multiplier=s[7])
+                x.then_inc(esem[e], 1)
+    for e in "VSPG":
+        g.wait_ge(esem[e], p["cnt"][e])
+    for k in sorted(total):
+        g.wait_ge(T.sem["d%d" % k], total[k])
+    g.wait_ge(T.sem.sent, nsent)

@@ -4,9 +4,10 @@ import numpy as np
 
 NB, n = 2, 96
 M6, BIGM = 6, 12582912.0
-DT = {"F": "float32", "H": "bfloat16", "J": "int32", "U": "uint16"}
-EPE = True
-ABS_E, ABS_H = "SSS", "SSS"
+DT = {"F": "float32", "H": "bfloat16", "J": "int32", "U": "uint16", "E": "float16"}
+V16 = True
+XE, KPE, WF, PK = (0,), False, False, False
+GATH = {("E", 0): "SSS", ("H", 0): "VVV", ("E", 1): "VVS", ("H", 1): "SVS"}
 
 
 def ap(buf, c0, c1, st=1, r0=0, r1=128):
@@ -26,7 +27,7 @@ def width(a):
 
 
 def build():
-    ops, size, tiles, psn = [], {"F": 0, "H": 0, "J": 0, "U": 0}, {}, [0]
+    ops, size, tiles, psn = [], {k: 0 for k in DT}, {}, [0]
     cur = [None, -1, "setup"]
 
     def tile(pool, key, w):
@@ -36,9 +37,9 @@ def build():
             size[pool] += -(-w // 16) * 16
         return tiles[k]
 
-    def ps():
+    def ps(w=512):
         psn[0] += 1
-        return ap(("ps", psn[0]), 0, 512)
+        return ap(("ps", psn[0]), 0, w)
 
     def add(e, ins, rd, wr, **kw):
         o = dict(e=e, ins=ins, x=cur[0], t=cur[1], sec=cur[2], rd=[r for r in rd if isinstance(r, tuple)], wr=wr, i=len(ops))
@@ -48,14 +49,17 @@ def build():
     def two(x):
         return list(x[1:]) if x[0] == "I" else [x]
 
+    def outs(x):
+        return ([x[2]], [x[1]]) if x[0] == "I" else ([], [x])
+
     def tt(out, a, b, op):
-        add("V", [("tt", out, a, b, op)], two(a) + [b], two(out))
+        add("V", [("tt", out, a, b, op)], two(a) + [b], [out])
 
     def ts(out, a, s1, s2, op0, op1=None):
-        add("V", [("ts", out, a, s1, s2, op0, op1)], two(a) + [s1, s2], two(out))
+        add("V", [("ts", out, a, s1, s2, op0, op1)], two(a) + [s1, s2], [out])
 
     def cp(out, a):
-        add("V", [("cp", out, a)], two(a) + ([out[2]] if out[0] == "I" else []), [out[1]] if out[0] == "I" else [out])
+        add("V", [("cp", out, a)], two(a) + outs(out)[0], outs(out)[1])
 
     def ms(out, v):
         add("V", [("ms", out, v)], [], [out])
@@ -70,9 +74,19 @@ def build():
         add("S", [("act", out, a, func, bias, scale)], two(a) + [bias, scale], [out])
 
     def mm(group):
-        k = len(group)
-        add("P", [("mm", o, l, r, j == 0, j == k - 1) for j, (o, l, r) in enumerate(group)],
-            [x for _, l, r in group for x in (l, r)], [group[0][0]])
+        parts, all_ = [[]], [m for m in group if m]
+        for m in group:
+            if m:
+                parts[-1].append(m)
+            else:
+                parts.append([])
+        for p in parts:
+            add("P", [("mm", *m, m is all_[0], m is all_[-1]) for m in p], [x for _, l, r in p for x in (l, r)], [all_[0][0]], more=p is not parts[0])
+
+    def mmo(group, w=n):
+        P = ps(w)
+        mm([m and (P, *m) for m in group])
+        return P
 
     def iota(out, pattern, base, cm):
         add("G", [("iota", out, pattern, base, cm)], [], [out])
@@ -83,340 +97,303 @@ def build():
     def dma(out, a, eng="Y"):
         add(eng, [("dma", out, a)], [a], [out], dma=1)
 
-    def send(out, a, key):
-        add("G", [("rd", out, a, key)], [a], [out], dma=1, remote=1)
+    def send(out, a):
+        add("G", [("rd", out, a)], [a], [out], dma=1, remote=1)
+
+    def lane_rows(a, r):
+        return ("ap", a[1], r, 128, a[4], a[5], 1, 16)
 
     D = lambda nm, c1, r1=128: ap(nm, 0, c1, 1, 0, r1)
-    px, vw, vtab, T613, code = ap("pxs", 0, 4096), ap("vws", 0, 2048), ap("vtab", 0, 4096 + n), ap("t613", 0, 4096), ap("code", 0, 4096)
+    px, vw, vtab = ap("pxs", 0, 4096), ap("vws", 0, 2048), ap("vtab", 0, 4096 + n)
     v0i, d0i, f0i = tile("J", "v0i", 192), tile("J", "d0i", 192), tile("J", "f0i", 192)
     wi, ki, z0s = tile("J", "wi", 1), tile("J", "ki", 1), tile("H", "z0s", 192)
     ms(v0i, 0)
     ms(d0i, 0)
-    dma(("ap", "J", 0, 128, v0i[4], v0i[5], 1, 16), D("v0", 192, 8))
-    dma(z0s, D("z0", 192), "S")
+    dma(lane_rows(v0i, 0), D("v0", 192, 8))
     dma(px, D("px", 4096))
-    dma(("ap", "J", 0, 128, d0i[4], d0i[5], 1, 16), D("d0", 192, 8), "S")
+    dma(z0s, D("z0", 192), "S")
     dma(wi, D("wt", 1), "S")
     dma(ki, D("kap", 1), "S")
     dma(f0i, D("f0", 192), "S")
-    dma(vw, D("vw", 2048))
+    dma(lane_rows(d0i, 2), D("d0", 192, 8), "S")
+    dma(lane_rows(d0i, 6), D("d0", 192, 8), "S")
+    for c in range(2):
+        dma(sub(vw, 1024 * c, 1024 * c + 1024), ap("vw", 1024 * c, 1024 * c + 1024))
+        ops[-1]["behind"] = 4096 + 2048 * c
     ones, B, I = tile("H", "ones", 512), tile("H", "B", 128), tile("H", "I", 128)
     ms(ones, 1.0)
     pi = tile("J", "pi", 1)
     iota(pi, [[0, 1]], 0, 1)
-    kkf = tile("F", "kkf", n)
-    iota(kkf, [[0, 6], [1, 16]], 0, 0)
-    iota(sub(T613, 0, 64), [[25856, 8], [19616, 8]], 0, 0)
+    kkf, sf = tile("F", "kkf", n), tile("F", "sf", n)
     t = tile("H", "Bt", 128)
     asel(t, sub(ones, 0, 128), [[-16, 8], [0, 16]], "is_ge", 0.0, 0, 1)
     asel(B, t, [[16, 8], [0, 16]], "is_ge", 0.0, 15, -1)
+    iota(kkf, [[0, M6], [1, 16]], 0, 0)
     asel(I, sub(ones, 0, 128), [[-1, 128]], "is_equal", 0.0, 0, 1)
-    r6 = tile("F", "r6", 6)
-    iota(r6, [[16, 6]], 0, 0)
+    iota(sf, [[1, n]], 0, 0)
     EXP = tile("H", "EXP", 512)
     for c in range(3):
         asel(rows(EXP, 32 * c, 32 * c + 32), rows(ones, 32 * c, 32 * c + 32), [[-1, 32], [0, 16]], "is_equal", 0.0, 0, 1)
-    for j in range(6, 12):
-        act(sub(T613, 1 << j, 2 << j), sub(T613, 0, 1 << j), "Copy", float(3232 << j))
-    lane_i, lane = tile("J", "lane", 1), tile("F", "lane", 1)
-    ts(lane_i, pi, 15, None, "bitwise_and")
+
+    def col(key, a, s1, s2, op0, op1=None, pool="F"):
+        o = tile(pool, key, 1)
+        ts(o, a, s1, s2, op0, op1)
+        return o
+
+    def scaled(base, s, key, pool="H"):
+        o = tile(pool, key, width(base))
+        if pool == "E":
+            ts(o, base, s, None, "mult")
+        else:
+            act(o, base, "Copy", 0.0, s)
+        return o
+
+    lane_i = col("lane_i", pi, 15, None, "bitwise_and", pool="J")
+    lane = tile("F", "lane", 1)
     cp(lane, lane_i)
-    MASK, RST, RSTM = tile("F", "MASK", n), tile("F", "RST", n), tile("F", "RSTM", n)
+    MASK, HOLD = tile("F", "MASK", n), tile("F", "HOLD", n)
     ts(MASK, kkf, lane, None, "is_equal")
-    ts(RSTM, kkf, 0.0, None, "not_equal")
-    B32 = tile("F", "B32", 128)
-    cp(B32, B)
+    CAP = scaled(MASK, 1048576.0, "CAP", "F")
+    ms(sub(HOLD, 0, 1), 0.0)
+    ts(sub(HOLD, 1, n), sub(MASK, 0, n - 1), -8192.0, None, "mult")
+    tt(HOLD, HOLD, CAP, "add")
+    unhold = col("unhold", lane, 15.0, 8192.0, "is_lt", "mult")
+    B32 = scaled(B, 1.0, "B32", "F")
     v0f = tile("F", "v0f", 192)
     cp(v0f, v0i)
-    vL, vLf = {}, {}
+    vpool, voff = ("E", 2048.0) if V16 else ("F", 7.0)
+    vL, vS = {}, {}
 
-    def pack_v(x, t_next, P):
-        a, b = tile("F", ("pv", x, t_next), n), tile("F", ("pw", x, t_next), n)
-        tt(a, MASK, P, "mult")
-        scan(b, RSTM, a, 0.0, "mult", "add")
-        return sub(b, 15, n, 16)
+    def users(P, lst, rep):
+        b = tile("F", ("pw", cur[0]), n)
+        scan(b, HOLD, P, 0.0, "add", "min")
+        ts(lst, sub(b, 15, n, 16), unhold, None, "add")
+        if V16:
+            ts(rep, P, -voff, None, "add")
+        else:
+            act(rep, P, "Copy", -voff)
 
-    def list_v(x, t, v):
-        vL[x], vLf[x] = tile("U", ("vL", x, t), M6), v
-        cp(vL[x], v)
-
-    for x in range(NB):
-        P = ps()
-        mm([(sub(P, 0, n), B32, sub(v0f, x * n, x * n + n))])
-        list_v(x, 0, pack_v(x, 0, sub(P, 0, n)))
-    def scaled(base, s, key):
-        o = tile("H", key, width(base))
-        ts(o, base, float(s), None, "mult")
-        return o
-    SEL, LAST, GR = tile("H", "SEL", 2048), tile("F", "LAST", 128), tile("H", "GR", 1024)
-    nI, Ih, I8, In8, IBIG, In16, In64, I16, I8192 = [scaled(I, s, ("Is", s)) for s in (-1, .5, 8, -8, 131072, -16, -64, 16, 8192)]
-    B2 = scaled(B, 2, "B2")
-    wf, kf, wB = tile("F", "wf", 1), tile("F", "kf", 1), tile("H", "wB", 128)
+    order = (1, 0)
+    for x in order:
+        cur[0] = x
+        vL[x], vS[x] = tile("U", ("vL0", x), M6), tile(vpool, ("vS0", x), n)
+        users(mmo([(B32, sub(v0f, x * n, x * n + n))]), vL[x], vS[x])
+    cur[0] = None
+    nI, Ih, nIh, I7, I8k, nI8k, I16k = [scaled(I, s, ("Is", s)) for s in (-1.0, .5, -.5, 7.5, 8192.0, -8192.0, 16384.0)]
+    Iv, I613 = scaled(I, 1.0, "Iv", vpool), scaled(I, 613.0, "I613", vpool)
+    wf, kf = tile("F", "wf", 1), col("kf", ki, 1 / 32, None, "mult")
     cp(wf, wi)
-    cp(kf, ki)
-    ts(wB, B, wf, None, "mult")
-    Fin, Z, AD = {}, {}, {}
-    d0f = tile("H", "d0f", 192)
-    cp(d0f, d0i)
-    for x in range(NB):
+    wB = scaled(B, wf, "wB")
+    SELW = tile("H", "SELW", 144)
+    ms(SELW, 0.0)
+    cp(sub(SELW, 15, 143, 16), sub(B, 0, 128, 16))
+    SEL = lambda q: sub(SELW, 15 - q, 143 - q)
+    M = lambda j: sub(MASK, j, j + 1)
+    c0 = col("c0", M(0), -2048.0, None, "mult")
+    c1 = col("c1", M(1), 0.5, c0, "mult", "add")
+    CU = scaled(sub(ones, 0, n), c1, "CU")
+    CX = tile("H", "CX", n)
+    ms(CX, 1792.0)
+    floff = -261888.484375 if V16 else -261949.484375
+    Fin, Z, ME = {}, {}, {}
+    me0 = tile("H", "me0", 192)
+    ts(me0, d0i, M(6), 0.0, "subtract", "max")
+    for x in order:
         Fin[x] = tile("F", ("f0", x), n)
         cp(Fin[x], sub(f0i, x * n, x * n + n))
-        Z[x] = sub(z0s, x * n, x * n + n)
-        AD[x] = tile("H", ("ad0", x), 2 * n)
-        ms(sub(AD[x], 0, n), 0.0)
-        P = ps()
-        mm([(sub(P, 0, n), B, sub(d0f, x * n, x * n + n))])
-        act(sub(AD[x], n, 2 * n), sub(P, 0, n), "Copy")
-    c0, c1, FL = tile("F", "c0", 1), tile("F", "c1", 1), tile("F", "FL", 16)
-    ts(c0, lane, 12.0, -1.0, "is_lt", "mult")
-    ts(c1, lane, 12.0, None, "is_equal")
-    tt(sub(code, 0, 1), c0, c1, "add")
-    ts(FL, sub(MASK, 0, 16), -2.0, 1.0, "mult", "add")
-    for j in range(12):
-        if j < 10:
-            ts(sub(code, 1 << j, 2 << j), sub(code, 0, 1 << j), sub(FL, j, j + 1), None, "mult")
-        else:
-            act(sub(code, 1 << j, 2 << j), sub(code, 0, 1 << j), "Copy", 0.0, sub(FL, j, j + 1))
-    p16, mo, me = tile("J", "p16", 1), tile("F", "mo", 1), tile("F", "me", 1)
-    ts(p16, pi, 4, 1, "logical_shift_right", "bitwise_and")
-    cp(mo, p16)
-    ts(me, mo, -1.0, 1.0, "mult", "add")
-    m12, m12n = tile("F", "m12", 1), tile("F", "m12n", 1)
-    ts(m12, c1, 64.0, None, "mult")
-    ts(m12n, c1, -64.0, None, "mult")
-    kcol = tile("F", "kcol", 16)
-    for q in range(4):
-        ts(sub(kcol, q, q + 1), lane, -2.0, 2.0 * q + 1, "mult", "add")
-    sc, S16, dmp = tile("F", "sc", 6), tile("H", "S16", 6), tile("F", "dmp", 6)
-    ts(sc, r6, lane, None, "add")
-    ts(S16, sc, 16.0, None, "mult")
-    ts(dmp, sc, 4096.0, None, "add")
+        Z[x], ME[x] = sub(z0s, x * n, x * n + n), sub(me0, x * n, x * n + n)
+    r_i = col("r_i", pi, 3, None, "bitwise_and", pool="J")
+    j_i = col("j_i", pi, 2, 3, "logical_shift_right", "bitwise_and", pool="J")
+    e0c, e1c, e2c = [col(("e", q), r_i, float(q), None, "is_equal") for q in range(3)]
+    Mo = scaled(I, col("cO", e1c, 16.0, -8.0, "mult", "add"), "Mo")
+    Mn = scaled(I, col("cN", e2c, 8.0, e0c, "mult", "subtract"), "Mn")
+    mb = col("mb", j_i, -1.0, col("mb0", e0c, 8.0, -7.0, "mult", "add"), "mult", "add")
+    cA = col("cA", lane, 2.0, None, "is_lt")
+    Mm, Ms = tile("H", "Mm", 128), tile("H", "Ms", 128)
+    ms(Mm, 0.0)
+    ms(Ms, 0.0)
+    act(sub(Mm, 0, 128, 4), sub(B, 0, 128, 4), "Copy", 0.0, cA)
+    act(sub(Mm, 2, 128, 4), sub(B, 2, 128, 4), "Copy", 0.0, M(2))
+    act(sub(Ms, 1, 128, 4), sub(B, 1, 128, 4), "Copy", 0.0, cA)
+    Mi = scaled(B, col("cI", M(2), M(6), None, "subtract"), "Mi")
+    klane = col("klane", lane, 1 / 16, None, "mult")
+    if KPE:
+        CK = scaled(sub(ones, 0, n), klane, "CK")
+    RST, LAST = tile("F", "RST", n), scaled(B32, M(15), "LAST", "F")
     ts(RST, kkf, 0.0, 1e6, "is_equal", "mult")
-    C80, C1, Cq = tile("H", "C80", n), tile("H", "C1", n), tile("H", "Cq", n)
-    ms(C80, 80.0)
-    ms(C1, 1.0)
-    ms(Cq, -0.25)
-    ts(sub(vtab, 0, 2048), vw, 4095, None, "bitwise_and")
-    ts(sub(vtab, 2048, 4096), vw, 12, None, "logical_shift_right")
-    ms(SEL, 0.0)
-    for b in range(16):
-        cp(sub(SEL, b * 128 + b, b * 128 + 128, 16), sub(B, b, 128, 16))
-    NSEL = tile("H", "NSEL", 2048)
-    act(NSEL, SEL, "Copy", 0.0, -1.0)
-    ts(LAST, B32, sub(MASK, 15, 16), None, "mult")
-    ms(GR, 0.0)
-    for q in range(8):
-        ms(sub(GR, q * 144, q * 144 + 16), 1.0)
-    mat = lambda A, b: sub(A, b * 128, b * 128 + 128)
+    OFFM, CS, DMP = tile("H", "OFFM", n), tile("H", "CS", n), tile("F", "DMP", n)
+    act(OFFM, MASK, "Copy", 32768.0, -32768.0)
+    tt(CS, OFFM, sf, "add")
+    act(DMP, mmo([(scaled(I, 1.0, "I32", "F"), sf), (nI, OFFM)]), "Copy", 4096.0 + 8192.0 - voff)
+    B8k = scaled(B, 8192.0, "B8k")
+    nl = col("nl", lane, -1.0, None, "mult")
+    CT = []
+    for q in range(4):
+        CT.append(tile("H", ("CT", q), n))
+        act(CT[q], sub(ones, 0, n), "Identity", nl, float(q))
+    r2 = col("r2", r_i, 2.0, None, "is_lt")
+    p1 = col("p1", j_i, 1.0, 2.0, "is_equal", "mult")
+    p2 = col("p2", j_i, 2.0, -2.0, "is_equal", "mult")
+    p3 = col("p3", p1, p2, r2, "add", "mult")
+    Mp = scaled(B, col("cP", p3, cA, None, "subtract"), "Mp")
+    Mc = scaled(B, col("cC", cA, 16.0, M(2), "mult", "add"), "Mc")
+    cur[2] = "unpack"
+    for c in range(2):
+        ts(sub(vtab, 1024 * c, 1024 * c + 1024), sub(vw, 1024 * c, 1024 * c + 1024), 4095, None, "bitwise_and")
+        ts(sub(vtab, 2048 + 1024 * c, 3072 + 1024 * c), sub(vw, 1024 * c, 1024 * c + 1024), 12, None, "logical_shift_right")
     outz, outf, outv, outc = [tile("F", k, 192) for k in ("oz", "of", "ov", "oc")]
+    even, odd = (lambda a: sub(a, 0, n, 2)), (lambda a: sub(a, 1, n, 2))
 
-    Csave = {}
     for t in range(4):
-        L, Cx, NLx, over, y, xb, Elist, e0, h, hm, en, src, W, vfs, nxT, nqT, OH1, OH2 = [{} for _ in range(18)]
-        for x in range(NB):
+        en, off = {}, {}
+        for x in order:
             cur[:] = [x, t, "like"]
-            sent = ("zad", "zland", "vland", "ff", "fland")
+            sent = ("zm", "zland", "vl", "vland", "ff", "fland", "vs", "sland")
             k = lambda s: (s, x, t if s in sent else t & 1)
-            z = Z[x]
-            y[x], xb[x] = sub(ps(), 0, n), tile("H", k("x"), n)
-            act(xb[x], ("I", px, vL[x]), "Copy")
-            mm([(y[x], nI, z), (y[x], I, xb[x])])
-            a, b = tile("H", k("c1"), n), tile("H", k("c2"), n)
-            ts(a, y[x], 60.0, None, "is_le")
-            ts(b, y[x], -60.0, None, "is_ge")
-            P = ps()
-            grp = []
-            if t == 1:
-                grp = [(sub(P, 0, n), nI, sub(AD[x], 0, n))]
-            elif t > 1:
-                for q in (1.0, 3.0)[:t - 1]:
-                    par = tile("H", k(("par", q)), n)
-                    ts(par, sub(AD[x], 0, n), q, None, "is_equal")
-                    grp.append((sub(P, 0, n), nI, par))
-            mm(grp + [(sub(P, 0, n), B, a), (sub(P, 0, n), B, b)])
-            L[x] = tile("H", k("L"), n)
-            ts(L[x], sub(P, 0, n), 24.0, None, "is_ge")
+            z, me, f, vs, vl = Z[x], ME[x], Fin[x], vS[x], vL[x]
+            T0, T1, T2, T3, T4 = [ap("vps%d" % x, n * q, n * q + n) for q in range(5)]
+            xb, ay, a, NL, NLy = [tile("H", k(s), n) for s in ("x", "ay", "a", "NL", "NLy")]
+            act(xb, ("I", px, vl), "Copy")
+            y = mmo([(nI, z), None, (I, xb)])
+            act(ay, y, "Abs")
+            ts(a, ay, 60.0, None, "is_le")
+            ts(NL, mmo(([(Mp, me), None] if t else []) + [(B, a)]), 8.0, None, "is_lt")
+            tt(NLy, y, NL, "mult")
             cur[2] = "hash"
-            U = ps()
-            mm([(sub(U, 0, n), wB, z)])
-            ui, uj, uh, us = [tile("J", k(("u", q)), n) for q in range(4)]
-            up = tile("F", k("up"), n)
-            cp(ui, sub(U, 0, n))
-            ts(uj, ui, 4095, None, "bitwise_and")
-            ts(up, uj, kf, -15728640.0, "mult", "add")
-            tt(uh, ("I", T613, vL[x]), up, "add")
-            ts(us, uh, 5, 4095, "arith_shift_right", "bitwise_and")
-            vp = "vps%d" % x
-            hf, m = ap(vp, 384, 384 + n), ap(vp, 0, n)
-            tt(hf, Fin[x], us, "subtract")
-            tt(m, hf, L[x], "mult")
-            h[x] = tile("F", k("h"), n)
-            tt(h[x], us, m, "add")
-            Hl = tile("U", k("Hl"), n)
-            cp(Hl, h[x])
+            R, fl, hp, h, Hl = tile("H", k("R"), n), tile("J", k("fl"), n), tile("J", k("hp"), n), tile("J", k("h"), n), tile("U", k("Hl"), n)
+            ts(R, mmo([(B, CU), (wB, z)]), BIGM * 4096, BIGM * 4096, "add", "subtract")
+            ts(fl, mmo([(wB, z), None, (nI, R)]), kf, floff, "mult", "add")
+            if PK:
+                us = tile("J", k("us"), n)
+                tt(hp, fl, mmo(([(I, CX)] if V16 else []) + [(I613, vs)]), "add")
+                ts(us, hp, 4095, None, "bitwise_and")
+                tt(T1, us, f, "subtract")
+                cur[2] = "pick"
+                tt(T1, T1, NL, "mult")
+                tt(h, T1, f, "add")
+            else:
+                tt(T0, fl, mmo(([(I, CX)] if V16 else []) + [(I613, vs)]), "add")
+                tt(T1, T0, f, "subtract")
+                cur[2] = "pick"
+                tt(T1, T1, NL, "mult")
+                tt(hp, T1, f, "add")
+                ts(h, hp, 4095, None, "bitwise_and")
+            cp(Hl, h)
             cur[2] = "E"
-            Elist[x] = tile("U", k("El"), n)
-            cp(Elist[x], ("I", vtab, vL[x]))
-            e0[x] = ap(vp, 96, 96 + n)
-            cp(e0[x], Elist[x])
+            El = tile("U", k("El"), n)
+            cp(El, ("I", vtab, vl))
+            cp(T2, El)
             cur[2] = "q"
-            Ly = tile("H", k("Ly"), n)
-            tt(Ly, y[x], L[x], "mult")
-            P = ps()
-            mm([(rows(sub(P, 0, 128), 0, n), z, I), (rows(sub(P, 0, 128), 0, n), Ly, I)])
-            nqT[x] = tile("H", k("nqT"), 128)
-            act(rows(nqT[x], 0, n), rows(sub(P, 0, 128), 0, n), "Copy", 0.0, -1.0)
-            P = ps()
-            mm([(rows(sub(P, 0, 128), 0, n), xb[x], I)])
-            nxT[x] = tile("H", k("nxT"), 128)
-            act(rows(nxT[x], 0, n), rows(sub(P, 0, 128), 0, n), "Copy", 0.0, -1.0)
-            da, de = tile("H", ("da", x), 16 * n), tile("H", ("de", x), 16 * n)
-            for which, lst, nT, dist, eng, abse in (("E", Elist[x], nxT[x], de, "V", ABS_E), ("H", Hl, nqT[x], da, "S", ABS_H)):
+            P, nqT = rows(ps(128), 0, n), tile("H", k("nqT"), 128)
+            mm([(P, xb, nI), None, (P, NLy, I)])
+            act(rows(nqT, 0, n), P, "Copy")
+            nxT = nqT
+            if x in XE:
+                cur[2] = "xT"
+                P, nxT = rows(ps(128), 0, n), tile("H", k("nxT"), 128)
+                mm([(P, xb, nI)])
+                act(rows(nxT, 0, n), P, "Copy")
+            dist = {}
+            for which, lst, nqT in (("E", El, nxT), ("H", Hl, nqT)):
                 cur[2] = which
-                raw = tile("H", ("raw", which, x), 16 * n)
+                raw, dist[which] = tile("H", ("raw", which, x), 16 * n), tile("H", ("d", which, x), 16 * n)
                 for c in range(3):
-                    r, dd = sub(raw, 512 * c, 512 * c + 512), sub(dist, 512 * c, 512 * c + 512)
+                    r, dd = sub(raw, 512 * c, 512 * c + 512), sub(dist[which], 512 * c, 512 * c + 512)
                     win = ("I", px, sub(lst, 32 * c, 32 * c + 32))
-                    if eng == "V":
+                    if GATH[which, x][c] == "V":
                         cp(r, win)
                     else:
                         act(r, win, "Copy")
-                    P = ps()
-                    mm([(P, I, r), (P, rows(nT, 32 * c, 32 * c + 32), rows(EXP, 32 * c, 32 * c + 32))])
-                    act(dd, P, "Abs")
-            Dp = ps()
-            mm([(sub(Dp, 0, n), I8192, L[x])] + [(sub(Dp, 0, n), mat(SEL, q), sub(de, q, 16 * n, 16)) for q in range(16)])
-            Ds = tile("F", k("Ds"), n)
-            act(Ds, sub(Dp, 0, n), "Copy", -8192.0)
-            Dh = ps()
-            mm([(sub(Dh, 0, n), mat(SEL, q), sub(da, q, 16 * n, 16)) for q in range(16)])
-            cur[2] = "count"
-            P = ps()
-            mm([(sub(P, 0, 2 * n), I, AD[x]), (sub(P, 0, n), I, L[x]), (sub(P, n, 2 * n), In16, L[x]), (sub(P, n, 2 * n), I, C1)])
-            AD1 = tile("H", k("AD1"), 2 * n)
-            act(AD1, sub(P, 0, 2 * n), "Relu")
-            P = ps()
-            mm([(sub(P, 0, n), I, sub(AD1, n, 2 * n)), (sub(P, 0, n, 2), I8, sub(L[x], 1, n, 2)), (sub(P, 1, n, 2), I8, sub(L[x], 0, n, 2))])
-            over[x] = tile("H", k("ov"), n)
-            ts(over[x], sub(P, 0, n), 10.0, None, "is_ge")
-            P = ps()
-            mm([(sub(P, 0, 6), I, S16)] + [(sub(P, 0, 6), mat(NSEL if q & 1 else SEL, q), sub(over[x], q, n, 16)) for q in range(16)])
-            src[x] = tile("U", k("src"), 6)
-            ts(src[x], sub(P, 0, 6), 0.0625, None, "mult")
-            P = ps()
-            mm([(sub(P, 0, n), I, Cq), (sub(P, 0, n), I, z), (sub(P, 0, n), Ih, Ly)])
-            z1 = tile("H", k("z1"), n)
-            ts(z1, sub(P, 0, n), BIGM, BIGM, "add", "subtract")
-            zad = tile("H", k("zad"), 3 * n)
-            if t < 3:
-                act(sub(zad, 0, n), ("I", z1, src[x]), "Copy")
-            else:
-                act(sub(outz, x * n, x * n + n), ("I", z1, src[x]), "Copy")
-            act(sub(zad, n, 2 * n), ("I", sub(AD1, 0, n), src[x]), "Copy")
-            act(sub(zad, 2 * n, 3 * n), ("I", sub(AD1, n, 2 * n), src[x]), "Copy")
-            if t < 3:
-                land = tile("H", k("zland"), 3 * n)
-                send(land, zad, ("z", x, t))
-                Z[x], AD[x] = sub(land, 0, n), sub(land, n, 3 * n)
-            else:
-                P = ps()
-                mm([(sub(P, 0, n), I16, sub(zad, n, 2 * n)), (sub(P, 0, n), I, sub(zad, 2 * n, 3 * n))])
-                act(sub(outc, x * n, x * n + n), sub(P, 0, n), "Copy")
-            cur[2] = "place"
-            P = ps()
-            mm([(sub(P, 0, n), B2, z1), (sub(P, 0, n), nI, L[x])])
-            wi_, w31 = tile("J", k("wi"), n), tile("J", k("w31"), n)
-            ts(wi_, sub(P, 0, n), sub(kcol, t, t + 1), None, "add")
-            ts(w31, wi_, 31, None, "bitwise_and")
-            OH1[x], OH2[x] = ap(vp, 192, 192 + n), ap(vp, 288, 288 + n)
-            ts(OH1[x], w31, 0.0, None, "is_equal")
-            P = ps()
-            mm([(sub(P, 0, n), I, C80), (sub(P, 0, n, 2), In64, sub(over[x], 1, n, 2)), (sub(P, 1, n, 2), In64, sub(over[x], 0, n, 2))])
-            tt(OH2[x], w31, sub(P, 0, n), "is_equal")
-            cur[2] = "e"
-            hmx = tile("F", k("hm"), n)
-            tt(hmx, h[x], e0[x], "subtract")
-            cc, chm = ap(vp, 0, n), tile("F", k("chm"), n)
-            tt(cc, sub(Dh, 0, n), Ds, "is_lt")
-            tt(chm, hmx, cc, "mult")
-            en[x] = tile("F", k("en"), n)
-            tt(en[x], chm, e0[x], "add")
-            W1, W2, W3 = [tile("F", k(("W", q)), n) for q in range(3)]
-            cur[2] = "least"
+                    act(dd, mmo([(rows(nqT, 32 * c, 32 * c + 32), rows(EXP, 32 * c, 32 * c + 32)), None, (I, r)], 512), "Abs")
+            cur[2] = "sum"
+            De = mmo([(nI8k, NL)] + [(SEL(q), sub(dist["E"], q, 16 * n, 16)) for q in range(16)])
             key, k1, k2, k3 = [tile("F", k(("key", q)), n) for q in range(4)]
-            ts(key, sub(Dh, 0, n), 16.0, lane, "mult", "add")
-            tr(k1, key)
+            if KPE:
+                P = mmo([(I, CK)] + [(SEL(q), sub(dist["H"], q, 16 * n, 16)) for q in range(16)])
+                cur[2] = "least"
+                tr(k1, P)
+                cur[2] = "sum"
+                act(key, P, "Copy")
+            else:
+                act(key, mmo([(SEL(q), sub(dist["H"], q, 16 * n, 16)) for q in range(16)]), "Identity", klane)
+                cur[2] = "least"
+                tr(k1, key)
+            cur[2] = "count"
+            over, sw, src = tile("H", k("ov"), n), tile("F", k("sw"), n), tile("U", k("src"), M6)
+            P = ps(n)
+            mm([(P, Mi, me), (P, I, NL), (even(P), nI, odd(NL)), (odd(P), nI, even(NL))])
+            act(over, P, "Relu", -1.0)
+            P = ps(n)
+            mm([(P, I, CS), (even(P), I, even(over)), (odd(P), nI, odd(over))])
+            scan(sw, CAP, P, 0.0, "add", "min")
+            cp(src, sub(sw, 15, n, 16))
+            zm = tile("H", k("zm"), 2 * n)
+            z2, me2, z1 = sub(zm, 0, n), sub(zm, n, 2 * n), tile("F", k("z1"), n)
+            P = ps(n)
+            mm([(P, Mm, me), (P, Mn, NL), (even(P), Ms, odd(me)), (odd(P), Ms, even(me)), (P, Mo, over)])
+            act(me2, P, "Relu", mb)
+            act(z1, mmo([(Ih, z), (Ih, xb), (nIh, NLy)]), "Copy", BIGM, 1 - 2.0 ** -10)
+            act(z2, ("I", z1, src), "Copy", -BIGM)
+            if t < 3:
+                land = tile("H", k("zland"), 2 * n)
+                send(land, zm)
+                Z[x], ME[x] = sub(land, 0, n), sub(land, n, 2 * n)
+            else:
+                cp(sub(outz, x * n, x * n + n), z2)
+                act(sub(outc, x * n, x * n + n), mmo([(Mc, me2)]), "Copy")
+            cur[2] = "place"
+            P, R16 = mmo([(I, CT[t]), (Ih, NL), (I7, over), None, (B, z2)]), tile("F", k("R16"), n)
+            ts(R16, P, BIGM * 16, BIGM * 16, "add", "subtract")
+            if WF:
+                T3 = tile("H", k("OH"), n)
+            tt(T3, R16, P, "is_equal")
+            cur[2] = "e"
+            hm, chm = tile("F", k("hm"), n), tile("F", k("chm"), n)
+            en[x] = tile("F", k("en"), n)
+            tt(hm, h, T2, "subtract")
+            tt(T0, key, De, "is_lt")
+            tt(chm, hm, T0, "mult")
+            tt(en[x], chm, T2, "add")
+            f2 = tile("F", k("ff"), n) if t < 3 else sub(outf, x * n, x * n + n)
+            act(f2, ("I", en[x], src), "Copy")
+            W1, W3 = tile("F", k("W1"), n), tile("F", k("W3"), n)
+            tt(W1, ("I", en[x], src) if WF else f2, T3, "mult")
+            cur[2] = "least"
             scan(k2, RST, k1, 1e6, "add", "min")
             tr(k3, k2)
-            P = ps()
-            mm([(sub(P, 0, n), IBIG, L[x]), (sub(P, 0, n), IBIG, over[x]), (sub(P, 0, n), LAST, k3)])
-            oh3 = ap(vp, 0, n)
-            tt(oh3, key, sub(P, 0, n), "is_equal")
-            tt(W3, h[x], oh3, "mult")
-            tt(W1, OH1[x], en[x], "mult")
-            tt(sub(W2, 0, n, 2), sub(OH2[x], 1, n, 2), sub(en[x], 1, n, 2), "mult")
-            tt(sub(W2, 1, n, 2), sub(OH2[x], 0, n, 2), sub(en[x], 0, n, 2), "mult")
-            P = ps()
-            mm([(sub(P, 0, n), B32, w) for w in (W1, W2, W3)])
-            vold, vfold = vL[x], vLf[x]
+            tt(T1, key, mmo([(I8k, sub(ones, 0, n)), (nI8k, NL), (I8k, over), None, (LAST, k3)]), "is_equal")
+            tt(W3, h, T1, "mult")
+            cur[2] = "v"
+            P = mmo([(B32, W1), None, (B32, W3)])
             if t < 3:
-                ff, land = sub(tile("F", k("ff"), n + 16), 0, n + M6), sub(tile("F", k("fland"), n + 16), 0, n + M6)
-                act(sub(ff, 0, n), ("I", en[x], src[x]), "Copy")
-                cp(sub(ff, n, n + M6), pack_v(x, t + 1, sub(P, 0, n)))
-                send(land, ff, ("f", x, t))
-                Fin[x] = sub(land, 0, n)
-                list_v(x, t + 1, sub(land, n, n + M6))
+                lst, rep = tile("U", k("vl"), M6), tile(vpool, k("vs"), n)
+                users(P, lst, rep)
+                vL[x], vS[x], Fin[x] = tile("U", k("vland"), M6), tile(vpool, k("sland"), n), tile("F", k("fland"), n)
+                send(vL[x], lst)
+                send(Fin[x], f2)
+                send(vS[x], rep)
             else:
-                act(sub(outv, x * n, x * n + n), sub(P, 0, n), "Copy")
-                act(sub(outf, x * n, x * n + n), ("I", en[x], src[x]), "Copy")
+                act(sub(outv, x * n, x * n + n), P, "Copy")
             cur[2] = "write"
-            C, Ce, Co = [tile("H", k(("C", q)), n) for q in range(3)]
-            nl = ap(vp, 384, 384 + n)
-            act(C, ("I", code, vold), "Copy")
-            ts(Ce, C, me, None, "mult")
-            ts(Co, C, mo, None, "mult")
-            ts(nl, L[x], m12, m12n, "mult", "add")
-            Cn = tile("H", k("Cn"), n)
-            tt(Cn, C, nl, "add")
-            Csave[x] = (Cn,)
-            cnt = []
-            for x2 in range(x + 1):
-                E = tile("H", k(("E", x2)), 8 * n)
-                for pb in range(4):
-                    P = ps()
-                    o = rows(sub(P, 0, 2 * n), 0, n)
-                    same = x2 == x
-                    grp = []
-                    for q in range(2):
-                        oo = rows(sub(P, n * q, n * q + n), 0, n)
-                        r = rows(Co if q else Ce, 32 * pb, 32 * pb + 32)
-                        for w, l in enumerate(Csave[x2]):
-                            grp.append(("mm", oo, rows(l, 32 * pb, 32 * pb + 32), r, True, True))
-                    add("P", grp, [Ce, Co] + list(Csave[x2]), [o])
-                    act(rows(sub(E, 2 * n * pb, 2 * n * pb + 2 * n), 0, n), o, "Relu", -12.0)
-                if same:
-                    asel(rows(E, 0, n), rows(E, 0, n), [[0, 8], [1, n]], "is_ge", 0.0, -1, -1)
-                cnt += [(rows(mat(GR, q), 0, n), rows(sub(E, n * q, n * q + n), 0, n)) for q in range(8)]
-            P = ps()
-            mm([(sub(P, 0, n), In8, L[x])] + [(sub(P, 0, n), l, r) for l, r in cnt])
-            win = tile("H", k("win"), n)
-            ts(win, sub(P, 0, n), -7.5, 0.0625, "is_lt", "mult")
-            P = ps()
-            mm([(sub(P, 0, 6), mat(SEL, q), sub(win, q, n, 16)) for q in range(16)])
-            vmd, tq, off = [tile("F", k(("o", q)), 6) for q in range(3)]
-            tt(vmd, vfold, dmp, "subtract")
-            tt(tq, vmd, sub(P, 0, 6), "mult")
-            tt(off, tq, dmp, "add")
-            W[x] = tile("U", k("off"), 6)
-            cp(W[x], off)
-        for x in range(NB):
-            cur[:] = [x, t, "write"]
-            cp(("I", vtab, W[x]), en[x])
+            eq1, eq2, ow = tile("H", k("eq1"), n), tile("H", k("eq2"), n), tile("F", k("ow"), n)
+            grp = [(I, OFFM), (Iv, vs), (I16k, NL)]
+            scan(T4, CAP, mmo(grp), -4096.0, "add", "min")
+            tt(eq1, vs, T4, "is_equal")
+            tt(sub(eq2, 16, n), sub(vs, 16, n), sub(T4, 0, n - 16), "is_equal")
+            P = ps(n)
+            mm([(P, l, r) for l, r in grp] + [None, (sub(P, 16, n), B8k, sub(eq2, 16, n)), (P, B8k, eq1)])
+            scan(ow, DMP, P, -32768.0, "max", "min")
+            off[x] = tile("U", k("off"), M6)
+            ts(off[x], sub(ow, 15, n, 16), voff - 8192.0, None, "add")
+        for x in order:
+            cur[:] = [x, t, "scatter"]
+            for c in (2, 1, 0):
+                cp(("I", vtab, sub(off[x], 2 * c, 2 * c + 2)), sub(en[x], 32 * c, 32 * c + 32))
     cur[:] = [None, 4, "out"]
     for o, nm in ((outz, "yz"), (outf, "yf")):
         dma(D(nm, 192), o)
     for o, nm in ((outv, "yv"), (outc, "yc")):
-        dma(D(nm, 192, 8), ("ap", "F", 0, 128, o[4], o[5], 1, 16))
+        dma(D(nm, 192, 8), lane_rows(o, 0))
     for c in range(4):
         q = ap("vps%d" % (c & 1), 0, 512)
         o = tile("F", ("yw", c), 512)
@@ -443,30 +420,25 @@ def cost(o):
             c += .06
         elif k == "rd":
             c += .8
+        elif i[1][0] == "I":
+            c += .05 + 3.8 * width(i[1][2]) * 16 * .83e-3
+        elif k != "ms" and i[2][0] == "I":
+            c += (.065 if k == "act" else .05) + 1.56 * width(i[2][2]) * 16 * .83e-3
         else:
-            out = i[1][1] if i[1][0] == "I" else i[1]
-            w = width(i[2][2]) * 16 if k != "ms" and i[2][0] == "I" else width(out)
-            b16 = lambda a: a[0] != "I" and a[1] in ("H", "U", "code")
-            if i[1][0] == "I":
-                w = 3.5 * width(i[1][2]) * 16
-            elif k != "ms" and i[2][0] == "I":
-                w = 1.5 * w
-            elif k == "tt":
+            w = width(i[1])
+            b16 = lambda a: a[1] in ("H", "U", "E")
+            if k == "tt":
                 ps_ = any(isinstance(a[1], tuple) or a[1] in ("vps0", "vps1") for a in i[2:4])
                 w = w * (1 if ps_ else 2)
             elif k in ("cp", "ts") and b16(i[1]) and b16(i[2]) or k == "ms" and b16(i[1]):
                 w = w * .5
-            c += max(64, w) * .83e-3 + (.01 if i[2:] else 0)
+            c += max(64, w) * .83e-3 + .01
     return c
 
 
 WAKE, OWN, NET, LOADT = .12, .06, 2.6, 2.0
 SCALE = 1.2
-SECT = {("E", 0): 2.6, ("H", 0): 2.9, ("count", 0): 7.3, ("e", 0): 3.0, ("hash", 0): 3.0, ("least", 0): 1.9, ("like", 0): 3.0, ("place", 0): 4.3,
-        ("q", 0): 3.0, ("write", 0): 3.0, ("hash", 1): -0.5, ("E", 1): -2.5, ("H", 1): -2.0, ("out", None): -20.2, ("q", 1): 0.7, ("like", 1): 4.2,
-        ("place", 1): 4.6, ("count", 1): 0.5}
-SEEDS = [(977194, 0.004, 8.0), (73801, 0.004, 8.0), (621379, 0.03, 3.0), (792181, 0.004, 1.0), (493328, 0.004, 3.0), (139368, 0.01, 1.0),
-         (828585, 0.01, 3.0), (445549, 0.03, 1.0), (186910, 0.03, 1.0), (256747, 0.004, 3.0), (625478, 0.01, 1.0), (890177, 0.01, 1.0)]
+BANKS, LAG, STEPS, SEED = 6, 5.0, 3000, 1
 
 
 def analyse():
@@ -475,8 +447,6 @@ def analyse():
     hist = {}
     deps = [set() for _ in range(N)]
     tile_ops = {}
-    for o in ops:
-        i = o["i"] = ops.index(o) if ops[o["i"]] is not o else o["i"]
     for o in ops:
         i = o["i"]
         for kind, lst in (("r", o["rd"]), ("w", o["wr"])):
@@ -487,7 +457,7 @@ def analyse():
                     if i not in tile_ops[buf]:
                         tile_ops[buf].append(i)
                 for (lo, hi, k2, j, st) in hist.setdefault(buf, []):
-                    if j != i and (k2 == "w" or kind == "w") and lo < a[5] and a[4] < hi:
+                    if j != i and (k2 == "w" or kind == "w" or isinstance(buf, tuple) and ops[j]["e"] != o["e"]) and lo < a[5] and a[4] < hi:
                         if st == a[6] > 1 and (lo - a[4]) % st:
                             continue
                         deps[i].add(j)
@@ -495,7 +465,7 @@ def analyse():
             for a in lst:
                 hh = hist[a[1]]
                 if kind == "w":
-                    hist[a[1]] = hh = [e for e in hh if not (a[6] == 1 and a[2] == 0 and a[3] == 128 and pat(a) == 1 and a[4] <= e[0] and e[1] <= a[5] and a[1] != "vtab")]
+                    hist[a[1]] = hh = [e for e in hh if not (a[6] == 1 and a[2] == 0 and a[3] == 128 and pat(a) == 1 and a[4] <= e[0] and e[1] <= a[5])]
                 hh.append((a[4], a[5], kind, i, a[6]))
     pool = [o["i"] for o in ops if o["e"] == "G" and not o.get("dma")]
     for a, b in zip(pool, pool[1:]):
@@ -506,8 +476,8 @@ def analyse():
         if o.get("remote"):
             lat.append(NET)
         elif o.get("dma"):
-            w = max(width(a) for a in o["wr"])
-            lat.append(LOADT + w * 1.1e-3)
+            w = max(width(a) for a in o["wr"]) * (1 if o["wr"][0][1] in ("H", "pxs") else 2)
+            lat.append(LOADT + (w + o.get("behind", 0)) * .8e-3)
         else:
             lat.append(0.0)
     prio = [0.0] * N
@@ -517,92 +487,180 @@ def analyse():
             succ[j].append(i)
     for i in range(N - 1, -1, -1):
         prio[i] = cst[i] + lat[i] + max([prio[s] + .1 for s in succ[i]] + [0.0])
-    for i in range(N):
-        prio[i] += SECT.get((ops[i]["sec"], ops[i]["x"]), 0.0)
-    return dict(ops=ops, size=size, deps=deps, succ=succ, tile_ops=tile_ops, cst=cst, lat=lat, prio=prio)
-
-
-def nudge(prio, seeds):
-    prio = list(prio)
-    for s, frac, sig in seeds:
-        r = np.random.default_rng(s)
-        hit, by = r.random(len(prio)) < frac, r.normal(size=len(prio)) * sig
-        prio = [float(p + b) if h else p for p, h, b in zip(prio, hit, by)]
-    return prio
+    eng = [o["e"] for o in ops]
+    opens = [None if o.get("more") else next((a[1] for a in o["wr"] if isinstance(a[1], tuple)), None) for o in ops]
+    touch = [set(a[1] for a in o["rd"] + o["wr"] if isinstance(a[1], tuple)) for o in ops]
+    gap = [[(q, 0.0 if ops[q].get("more") and q == i + 1 else OWN if eng[q] == eng[i] and not ops[i].get("dma") else WAKE) for q in succ[i]] for i in range(N)]
+    return dict(ops=ops, size=size, eng=eng, opens=opens, touch=touch, gap=gap, deps=deps, succ=succ, tile_ops=tile_ops, cst=cst, lat=lat, prio=prio)
 
 
 def schedule(an, prio):
-    ops, deps, succ, tile_ops, cst, lat = an["ops"], an["deps"], an["succ"], an["tile_ops"], an["cst"], an["lat"]
-    N = len(ops)
-    ptile = [next((a[1] for a in o["wr"] if isinstance(a[1], tuple)), None) for o in ops]
-    ptouch = [set(a[1] for a in o["rd"] + o["wr"] if isinstance(a[1], tuple)) for o in ops]
-    eng = [o["e"] for o in ops]
-    isdma = [bool(o.get("dma")) for o in ops]
-    bank_tiles = [[] for _ in range(6)]
+    tile_ops, cst, lat, eng, opens, touch, gap = [an[k] for k in ("tile_ops", "cst", "lat", "eng", "opens", "touch", "gap")]
+    N = len(cst)
+    last, bfree = [None] * BANKS, [0.0] * BANKS
     bank_of, left = {}, {b: len(v) for b, v in tile_ops.items()}
-    fin, free = [None] * N, {}
-    start = [None] * N
-    order = {e: [] for e in "VSPGY"}
-    ndep = [len(d) for d in deps]
-    ready = [i for i in range(N) if ndep[i] == 0]
-    rt = {i: 0.0 for i in ready}
-    extra = [set() for _ in range(N)]
-    done = 0
-    while done < N:
-        best = None
-        for i in ready:
-            s = max(free.get(eng[i], 0.0), rt[i])
-            bk = None
-            if best is not None and round(s / .04) > best[0][0]:
-                continue
-            if ptile[i] is not None and ptile[i] not in bank_of:
-                cand = []
-                for b in range(6):
-                    bt = bank_tiles[b]
-                    if not bt or left[bt[-1]] == 0:
-                        f = max([fin[j] for j in tile_ops[bt[-1]]]) + WAKE if bt else 0.0
-                        cand.append((f, b))
-                if not cand:
-                    continue
-                f, bk = min(cand)
-                s = max(s, f)
-            key = (round(s / .04), -prio[i], i)
-            if best is None or key < best[0]:
-                best = (key, s, i, bk)
-        key, s, i, bk = best
-        o = ops[i]
-        ready.remove(i)
-        if bk is not None:
-            tb = ptile[i]
-            if bank_tiles[bk]:
-                extra[i] |= set(tile_ops[bank_tiles[bk][-1]])
-            bank_tiles[bk].append(tb)
-            bank_of[tb] = bk
-        for tb in ptouch[i]:
+    left[None] = 0
+    fin, start, rt, extra = [None] * N, [None] * N, [0.0] * N, [()] * N
+    free, order, ready = [{e: v() for e in "VSPGY"} for v in (float, list, list)]
+    ndep = [len(d) for d in an["deps"]]
+    for i in range(N):
+        if ndep[i] == 0:
+            ready[eng[i]].append(i)
+    for _ in range(N):
+        bf, bk = 1e9, None
+        for b in range(BANKS):
+            if bfree[b] < bf and not left[last[b]]:
+                bf, bk = bfree[b], b
+        first, e = 1e9, None
+        for q, lst in ready.items():
+            if lst and free[q] < first:
+                s = max(free[q], min([bf if opens[i] and bf > rt[i] else rt[i] for i in lst] if q == "P" else [rt[i] for i in lst]))
+                if s < first:
+                    first, e = s, q
+        if e is None:
+            return None
+        lim = first + .02
+        i = max([i for i in ready[e] if rt[i] <= lim and (bf <= lim or not opens[i])], key=lambda j: prio[j])
+        s = max(rt[i], free[e], bf if opens[i] else 0.0)
+        ready[e].remove(i)
+        if opens[i]:
+            if last[bk] is not None:
+                extra[i] = tile_ops[last[bk]]
+            last[bk], bank_of[opens[i]] = opens[i], bk
+        start[i], free[e] = s, s + cst[i]
+        f = fin[i] = s + cst[i] + lat[i]
+        for tb in touch[i]:
             left[tb] -= 1
-        start[i], fin[i] = s, s + cst[i] + lat[i]
-        free[o["e"]] = s + cst[i]
-        order[o["e"]].append(i)
-        done += 1
-        for q in succ[i]:
-            w = OWN if eng[q] == eng[i] and not isdma[i] else WAKE
-            rt[q] = max(rt.get(q, 0.0), fin[i] + w)
+            if f + WAKE > bfree[bank_of[tb]]:
+                bfree[bank_of[tb]] = f + WAKE
+        order[e].append(i)
+        for q, w in gap[i]:
+            if f + w > rt[q]:
+                rt[q] = f + w
             ndep[q] -= 1
-            if ndep[q] == 0:
-                ready.append(q)
+            if not ndep[q]:
+                ready[eng[q]].append(q)
     return dict(order=order, start=start, fin=fin, extra=extra, bank_of=bank_of, span=max(fin))
+
+
+def tune(an, steps):
+    seen, cls = {}, []
+    for o in an["ops"]:
+        k = (o["x"], o["t"], o["sec"], o["e"])
+        seen[k] = seen.get(k, -1) + 1
+        cls.append((o["x"], o["sec"], o["e"], seen[k], 0 <= o["t"] < 4))
+    keys = sorted(set(cls), key=str)
+    of = np.array([keys.index(c) for c in cls])
+    sections = [[j for j, k in enumerate(keys) if k[:2] == s] for s in sorted(set(k[:2] for k in keys), key=str)]
+    base, rng = np.array(an["prio"]), np.random.default_rng(SEED)
+    shift = np.array([-LAG if k[0] == 0 else 0.0 for k in keys])
+    cur = best = schedule(an, list(base + shift[of]))
+    for step in range(steps):
+        new = shift.copy()
+        if rng.random() < .25:
+            new[sections[rng.integers(len(sections))]] += rng.normal() * 2
+        else:
+            new[rng.integers(len(keys), size=(1, 1, 2, 4)[rng.integers(4)])] += rng.normal() * (.5, 2, 5)[rng.integers(3)]
+        sc = schedule(an, list(base + new[of]))
+        if sc and sc["span"] < cur["span"] + .3 * (1 - step / steps) * rng.exponential():
+            cur, shift = sc, new
+            if sc["span"] < best["span"]:
+                best = sc
+    return best
+
+
+def play(an, order):
+    tile_ops, cst, lat, eng, opens, touch, gap = [an[k] for k in ("tile_ops", "cst", "lat", "eng", "opens", "touch", "gap")]
+    N = len(cst)
+    last, bfree, bby = [None] * BANKS, [0.0] * BANKS, [None] * BANKS
+    bank_of, left = {}, {b: len(v) for b, v in tile_ops.items()}
+    left[None] = 0
+    fin, start, rt, extra, why = [0.0] * N, [0.0] * N, [0.0] * N, [()] * N, [None] * N
+    ndep = [len(d) for d in an["deps"]]
+    qs = [order[e] + [None] for e in "VSPGY"]
+    pos, free, prev = [0] * 5, [0.0] * 5, [None] * 5
+    for _ in range(N):
+        s, e = 1e9, None
+        for q in range(5):
+            i = qs[q][pos[q]]
+            if i is None or ndep[i]:
+                continue
+            c = rt[i] if rt[i] > free[q] else free[q]
+            if opens[i]:
+                bf, bk = 1e9, None
+                for b in range(BANKS):
+                    if bfree[b] < bf and not left[last[b]]:
+                        bf, bk = bfree[b], b
+                if bf > c:
+                    c = bf
+            if c < s:
+                s, e = c, q
+        if e is None:
+            return None
+        i = qs[e][pos[e]]
+        pos[e] += 1
+        if s > rt[i]:
+            why[i] = prev[e] if s == free[e] else bby[bk]
+        if opens[i]:
+            if last[bk] is not None:
+                extra[i] = tile_ops[last[bk]]
+            last[bk], bank_of[opens[i]] = opens[i], bk
+        start[i], free[e], prev[e] = s, s + cst[i], i
+        f = fin[i] = s + cst[i] + lat[i]
+        for tb in touch[i]:
+            left[tb] -= 1
+            b = bank_of[tb]
+            if f + WAKE > bfree[b]:
+                bfree[b], bby[b] = f + WAKE, i
+        for q, w in gap[i]:
+            if f + w > rt[q]:
+                rt[q], why[q] = f + w, i
+            ndep[q] -= 1
+    return dict(order=order, start=start, fin=fin, extra=extra, bank_of=bank_of, span=max(fin), why=why)
+
+
+def refine(an, sc, steps):
+    rng, eng, deps = np.random.default_rng(SEED), an["eng"], an["deps"]
+    pick = lambda a: a[rng.integers(len(a))]
+    cur = best = play(an, sc["order"])
+    path = None
+    for step in range(steps):
+        if path is None:
+            i, path = cur["fin"].index(cur["span"]), []
+            while cur["why"][i] is not None:
+                if cur["why"][i] not in deps[i]:
+                    path.append((cur["why"][i], i))
+                i = cur["why"][i]
+        u, v = pick(path)
+        order = dict(cur["order"])
+        if rng.random() < .5:
+            a, d = v if eng[u] == eng[v] else u, -pick((1, 1, 2, 3, 5))
+        elif eng[u] != eng[v]:
+            a, d = order["P"][max(0, order["P"].index(v) - pick(range(1, 8)))], pick((1, 2, 4, 8))
+        else:
+            k = pick((0, 0, 0, 1, 2))
+            a, d = order[eng[u]][max(0, order[eng[u]].index(u) - k)], k + pick((1, 1, 2, 3, 5))
+        lst = order[eng[a]] = list(order[eng[a]])
+        p = lst.index(a)
+        lst.insert(max(0, p + d), lst.pop(p))
+        new = play(an, order)
+        if new and new["span"] < cur["span"] + .05 * (1 - step / steps) * rng.exponential():
+            cur, path = new, None
+            if new["span"] < best["span"]:
+                best = new
+    return best
 
 
 def plan():
     an = analyse()
-    sc = schedule(an, nudge(an["prio"], SEEDS))
+    sc = refine(an, tune(an, STEPS), 5 * STEPS)
+    sc["extra"] = [set(x) for x in sc["extra"]]
     ops, deps, order, extra, fin = an["ops"], an["deps"], sc["order"], sc["extra"], sc["fin"]
     N = len(ops)
     cnt = {e: 0 for e in "VSPG"}
     end, K, clk, waits = {}, {e: {} for e in "VSPGY"}, [None] * N, [None] * N
     ndma = 0
     for e in "VSPGY":
-        pos = {i: p for p, i in enumerate(order[e])}
         for i in order[e]:
             if ops[i].get("dma"):
                 end[i] = (("d", ndma), 0)
@@ -621,7 +679,7 @@ def plan():
                 dd = sorted(deps[i] | extra[i], key=lambda d: -fin[d])
                 for d in dd:
                     s, c = end[d]
-                    if K[e].get(s, -1) >= c:
+                    if K[e].get(s, -1) >= c or ops[i].get("more") and d == i - 1:
                         continue
                     ws.append(d)
                     for a, b in clk[d].items():
@@ -638,17 +696,17 @@ def plan():
                 emitted.add(i)
                 moved = True
         assert moved
-    return dict(ops=ops, size=an["size"], order=order, waits=waits, end=end, bank_of=sc["bank_of"], cnt=cnt, ndma=ndma, span=sc["span"])
+    return dict(ops=ops, size=an["size"], start=sc["start"], order=order, waits=waits, end=end, bank_of=sc["bank_of"], cnt=cnt, ndma=ndma, span=sc["span"])
 
 
 PLAN = plan()
 _s = PLAN["size"]
 SCRATCH = {
     "pxs": ("sbuf", [128, 4096], "bfloat16"), "vws": ("sbuf", [128, 2048], "int32"), "vtab": ("sbuf", [128, 4096 + n], "int32"),
-    "t613": ("sbuf", [128, 4096], "float32"), "code": ("sbuf", [128, 4096], "bfloat16"),
 }
-for _k in "FHJU":
-    SCRATCH[_k + "pool"] = ("sbuf", [128, _s[_k]], DT[_k])
+for _k in DT:
+    if _s[_k]:
+        SCRATCH[_k + "pool"] = ("sbuf", [128, _s[_k]], DT[_k])
 for _k in ["ps%d" % _b for _b in range(6)] + ["vps0", "vps1"]:
     SCRATCH[_k] = ("psum", [128, 512], "float32")
 SEMAPHORES = ["eV", "eS", "eP", "eG", "sent"] + ["d%d" % k for k in range(PLAN["ndma"])]
@@ -731,7 +789,7 @@ def rank_program(g, core, T, topo):
                 elif k == "mm":
                     x = g.tensor.matmul(out=A(s[1]), lhsT=A(s[2]), rhs=A(s[3]), start=s[4], stop=s[5])
                 elif k == "iota":
-                    if s[1][1] in ("F", "H", "t613"):
+                    if s[1][1] in ("F", "H"):
                         x = g.iota(out=A(s[1]), pattern=s[2], base=s[3], channel_multiplier=s[4], allow_small_or_imprecise_dtypes=True)
                     else:
                         x = g.iota(out=A(s[1]), pattern=s[2], base=s[3], channel_multiplier=s[4])

@@ -1,13 +1,14 @@
 from concourse.mybir import AluOpType as OP, ActivationFunctionType as AF
 
+import math
 import numpy as np
 
 NB, n = 2, 96
 M6, BIGM = 6, 12582912.0
 DT = {"F": "float32", "H": "bfloat16", "J": "int32", "U": "uint16", "E": "float16"}
-V16 = True
-XE, KPE, WF, PK = (0,), False, False, False
-GATH = {("E", 0): "SSS", ("H", 0): "VVV", ("E", 1): "VVS", ("H", 1): "SVS"}
+XE, KPE, MSG, RE, FY, FT, VF, HI, WM = (), False, 2, (), True, False, False, False, False
+GATH = {("E", 0): "???", ("H", 0): "???", ("E", 1): "???", ("H", 1): "???"}
+CUTS = {("E", 0): (0, 32, 64, 96), ("H", 0): (0, 32, 64, 96), ("E", 1): (0, 32, 64, 96), ("H", 1): (0, 32, 64, 96)}
 
 
 def ap(buf, c0, c1, st=1, r0=0, r1=128):
@@ -70,8 +71,20 @@ def build():
     def tr(out, a):
         add("V", [("tr", out, a)], [a], [out])
 
-    def act(out, a, func, bias=0.0, scale=1.0):
-        add("S", [("act", out, a, func, bias, scale)], two(a) + [bias, scale], [out])
+    def act(out, a, func, bias=0.0, scale=1.0, on="S"):
+        alt = {"S": [("act", out, a, func, bias, scale)]}
+        if func == "Relu" and scale == 1.0:
+            alt["V"] = [("ts", out, a, bias, 0.0, "add", "max")]
+        elif func == "Relu" and bias == 0.0:
+            alt["V"] = [("ts", out, a, 0.0, scale, "max", "mult")]
+        elif func == "Sigmoid":
+            alt["V"] = [("ts", out, a, -bias / scale, None, "is_lt", None)]
+        elif func in ("Copy", "Identity"):
+            alt["V"] = [("cp", out, a)] if (bias, scale) == (0.0, 1.0) else [("ts", out, a, scale, bias, "mult", "add")]
+        add(on, alt[on], two(a) + [bias, scale], [out], alt=alt)
+
+    def below(out, a, c):
+        act(out, a, "Sigmoid", 256.0 * (c - .5), -256.0)
 
     def mm(group):
         parts, all_ = [[]], [m for m in group if m]
@@ -110,7 +123,8 @@ def build():
     ms(v0i, 0)
     ms(d0i, 0)
     dma(lane_rows(v0i, 0), D("v0", 192, 8))
-    dma(px, D("px", 4096))
+    if not VF:
+        dma(px, D("px", 4096))
     dma(z0s, D("z0", 192), "S")
     dma(wi, D("wt", 1), "S")
     dma(ki, D("kap", 1), "S")
@@ -119,21 +133,40 @@ def build():
     dma(lane_rows(d0i, 6), D("d0", 192, 8), "S")
     for c in range(2):
         dma(sub(vw, 1024 * c, 1024 * c + 1024), ap("vw", 1024 * c, 1024 * c + 1024))
-        ops[-1]["behind"] = 4096 + 2048 * c
+        ops[-1]["behind"] = (0 if VF else 8192) + 4096 * c
+    if VF:
+        dma(px, D("px", 4096))
+        ops[-1]["behind"] = 8192
     ones, B, I = tile("H", "ones", 512), tile("H", "B", 128), tile("H", "I", 128)
     ms(ones, 1.0)
     pi = tile("J", "pi", 1)
     iota(pi, [[0, 1]], 0, 1)
-    kkf, sf = tile("F", "kkf", n), tile("F", "sf", n)
+    kkf, sf = tile("F", "kkf", 2 * n), tile("H", "sf", n)
+    iota(kkf, [[0, 2 * M6], [1, 16]], 0, 0)
     t = tile("H", "Bt", 128)
     asel(t, sub(ones, 0, 128), [[-16, 8], [0, 16]], "is_ge", 0.0, 0, 1)
     asel(B, t, [[16, 8], [0, 16]], "is_ge", 0.0, 15, -1)
-    iota(kkf, [[0, M6], [1, 16]], 0, 0)
     asel(I, sub(ones, 0, 128), [[-1, 128]], "is_equal", 0.0, 0, 1)
-    iota(sf, [[1, n]], 0, 0)
+    zero = tile("H", "zero", 128 * 3 + 144)
+    ms(zero, 0.0)
+
+    def diag(s):
+        o = tile("H", ("diag", s), 128)
+        asel(o, sub(zero, 0, 128), [[-1, 128]], "not_equal", s, 0, 1)
+        return o
+
+    nI, Ih = diag(-1.0), diag(.5)
     EXP = tile("H", "EXP", 512)
     for c in range(3):
         asel(rows(EXP, 32 * c, 32 * c + 32), rows(ones, 32 * c, 32 * c + 32), [[-1, 32], [0, 16]], "is_equal", 0.0, 0, 1)
+    iota(sf, [[1, n]], 0, 0)
+    nIh, nI8k, I8k, I16k, I7 = [diag(s) for s in (-.5, -8192.0, 8192.0, 16384.0, 7.5)]
+    one = sub(ones, 0, n)
+
+    def lin(key, a, scale, bias):
+        o = tile("F", key, 1)
+        act(o, a, "Identity" if isinstance(bias, tuple) else "Copy", bias, scale)
+        return o
 
     def col(key, a, s1, s2, op0, op1=None, pool="F"):
         o = tile(pool, key, 1)
@@ -142,103 +175,95 @@ def build():
 
     def scaled(base, s, key, pool="H"):
         o = tile(pool, key, width(base))
-        if pool == "E":
-            ts(o, base, s, None, "mult")
-        else:
-            act(o, base, "Copy", 0.0, s)
+        act(o, base, "Copy", 0.0, s)
         return o
 
     lane_i = col("lane_i", pi, 15, None, "bitwise_and", pool="J")
     lane = tile("F", "lane", 1)
     cp(lane, lane_i)
-    MASK, HOLD = tile("F", "MASK", n), tile("F", "HOLD", n)
+    MASK, HOLD = tile("F", "MASK", 2 * n), tile("F", "HOLD", 2 * n)
     ts(MASK, kkf, lane, None, "is_equal")
+    act(HOLD, MASK, "Copy", -8192.0, 1048576.0)
+    MASK = sub(MASK, 0, n)
     CAP = scaled(MASK, 1048576.0, "CAP", "F")
-    ms(sub(HOLD, 0, 1), 0.0)
-    ts(sub(HOLD, 1, n), sub(MASK, 0, n - 1), -8192.0, None, "mult")
-    tt(HOLD, HOLD, CAP, "add")
-    unhold = col("unhold", lane, 15.0, 8192.0, "is_lt", "mult")
+    M = lambda j: sub(MASK, j, j + 1)
+    unhold = lin("unhold", lane, -8192.0, 15 * 8192.0)
     B32 = scaled(B, 1.0, "B32", "F")
     v0f = tile("F", "v0f", 192)
     cp(v0f, v0i)
-    vpool, voff = ("E", 2048.0) if V16 else ("F", 7.0)
-    vL, vS = {}, {}
+    vpool, voff = "E", 2048.0
 
-    def users(P, lst, rep):
-        b = tile("F", ("pw", cur[0]), n)
-        scan(b, HOLD, P, 0.0, "add", "min")
-        ts(lst, sub(b, 15, n, 16), unhold, None, "add")
-        if V16:
-            ts(rep, P, -voff, None, "add")
-        else:
-            act(rep, P, "Copy", -voff)
+    unhold2 = lin("unhold2", lane, -8192.0, 15 * 8192.0 - voff)
+
+    def users(P, lst, rep, unhold):
+        b = tile("F", ("pw", cur[0]), width(P))
+        scan(b, sub(HOLD, 0, width(P)), P, 0.0, "add", "min")
+        ts(lst, sub(b, 15, width(P), 16), unhold, None, "add")
+        act(rep, P, "Copy", -voff)
 
     order = (1, 0)
-    for x in order:
-        cur[0] = x
-        vL[x], vS[x] = tile("U", ("vL0", x), M6), tile(vpool, ("vS0", x), n)
-        users(mmo([(B32, sub(v0f, x * n, x * n + n))]), vL[x], vS[x])
-    cur[0] = None
-    nI, Ih, nIh, I7, I8k, nI8k, I16k = [scaled(I, s, ("Is", s)) for s in (-1.0, .5, -.5, 7.5, 8192.0, -8192.0, 16384.0)]
-    Iv, I613 = scaled(I, 1.0, "Iv", vpool), scaled(I, 613.0, "I613", vpool)
+    vL, vS = tile("U", "vL0", 2 * M6), tile(vpool, "vS0", 2 * n)
+    users(mmo([(B32, v0f)], 2 * n), vL, vS, unhold)
+    vL, vS = {x: sub(vL, M6 * x, M6 * x + M6) for x in order}, {x: sub(vS, n * x, n * x + n) for x in order}
+    Iv, nIv, I613, I2047 = [scaled(I, s, ("Iv", s), vpool) for s in (1.0, -1.0, 613.0, 2047.0)]
     wf, kf = tile("F", "wf", 1), col("kf", ki, 1 / 32, None, "mult")
     cp(wf, wi)
     wB = scaled(B, wf, "wB")
-    SELW = tile("H", "SELW", 144)
-    ms(SELW, 0.0)
-    cp(sub(SELW, 15, 143, 16), sub(B, 0, 128, 16))
+    if not HI:
+        CU = scaled(one, lin("c1", M(1), 0.5, lin("c0", M(0), -2048.0, 0.0)), "CU")
+    one16 = scaled(one, 1.0, "one16", "E")
+    SELW = sub(zero, 384, 528)
+    act(sub(SELW, 15, 143, 16), sub(B, 0, 128, 16), "Copy")
     SEL = lambda q: sub(SELW, 15 - q, 143 - q)
-    M = lambda j: sub(MASK, j, j + 1)
-    c0 = col("c0", M(0), -2048.0, None, "mult")
-    c1 = col("c1", M(1), 0.5, c0, "mult", "add")
-    CU = scaled(sub(ones, 0, n), c1, "CU")
-    CX = tile("H", "CX", n)
-    ms(CX, 1792.0)
-    floff = -261888.484375 if V16 else -261949.484375
+    if RE:
+        NSELW = scaled(SELW, -1.0, "NSELW")
+        NSEL = lambda q: sub(NSELW, 15 - q, 143 - q)
     Fin, Z, ME = {}, {}, {}
-    me0 = tile("H", "me0", 192)
+    me0, f0f = tile("H", "me0", 192), tile("E", "f0f", 192)
     ts(me0, d0i, M(6), 0.0, "subtract", "max")
+    ts(f0f, f0i, -2047.0, None, "add")
     for x in order:
-        Fin[x] = tile("F", ("f0", x), n)
-        cp(Fin[x], sub(f0i, x * n, x * n + n))
-        Z[x], ME[x] = sub(z0s, x * n, x * n + n), sub(me0, x * n, x * n + n)
+        Z[x], ME[x], Fin[x] = [sub(a, x * n, x * n + n) for a in (z0s, me0, f0f)]
     r_i = col("r_i", pi, 3, None, "bitwise_and", pool="J")
     j_i = col("j_i", pi, 2, 3, "logical_shift_right", "bitwise_and", pool="J")
     e0c, e1c, e2c = [col(("e", q), r_i, float(q), None, "is_equal") for q in range(3)]
-    Mo = scaled(I, col("cO", e1c, 16.0, -8.0, "mult", "add"), "Mo")
+    Mo = scaled(I, lin("cO", e1c, 16.0, -8.0), "Mo")
     Mn = scaled(I, col("cN", e2c, 8.0, e0c, "mult", "subtract"), "Mn")
-    mb = col("mb", j_i, -1.0, col("mb0", e0c, 8.0, -7.0, "mult", "add"), "mult", "add")
-    cA = col("cA", lane, 2.0, None, "is_lt")
-    Mm, Ms = tile("H", "Mm", 128), tile("H", "Ms", 128)
-    ms(Mm, 0.0)
-    ms(Ms, 0.0)
+    mb = col("mb", j_i, -1.0, lin("mb0", e0c, 8.0, -7.0), "mult", "add")
+    cA = tile("F", "cA", 1)
+    below(cA, lane, 2)
+    ops[-1].pop("alt")
+    ops[-1]["table"] = 1.3
+    Mm, Ms = sub(zero, 128, 256), sub(zero, 256, 384)
     act(sub(Mm, 0, 128, 4), sub(B, 0, 128, 4), "Copy", 0.0, cA)
     act(sub(Mm, 2, 128, 4), sub(B, 2, 128, 4), "Copy", 0.0, M(2))
     act(sub(Ms, 1, 128, 4), sub(B, 1, 128, 4), "Copy", 0.0, cA)
-    Mi = scaled(B, col("cI", M(2), M(6), None, "subtract"), "Mi")
-    klane = col("klane", lane, 1 / 16, None, "mult")
+    Mi = scaled(B, lin("cI", M(6), -1.0, M(2)), "Mi")
+    klane = lin("klane", lane, 1 / 16, 0.0)
     if KPE:
         CK = scaled(sub(ones, 0, n), klane, "CK")
     RST, LAST = tile("F", "RST", n), scaled(B32, M(15), "LAST", "F")
-    ts(RST, kkf, 0.0, 1e6, "is_equal", "mult")
-    OFFM, CS, DMP = tile("H", "OFFM", n), tile("H", "CS", n), tile("F", "DMP", n)
+    act(RST, sub(kkf, 0, n), "Relu", 1e6, -1e6)
+    OFFM, DMP = tile("H", "OFFM", n), tile("F", "DMP", n)
     act(OFFM, MASK, "Copy", 32768.0, -32768.0)
-    tt(CS, OFFM, sf, "add")
-    act(DMP, mmo([(scaled(I, 1.0, "I32", "F"), sf), (nI, OFFM)]), "Copy", 4096.0 + 8192.0 - voff)
-    B8k = scaled(B, 8192.0, "B8k")
-    nl = col("nl", lane, -1.0, None, "mult")
-    CT = []
+    act(DMP, mmo([(I, sf), (nI, OFFM)]), "Copy", 4096.0 + 8192.0 - voff)
+    B8k, CS, nl = scaled(B, 8192.0, "B8k"), tile("H", "CS", n), lin("nl", lane, -1.0, 0.0)
+    act(CS, mmo([(I, sf), (I, OFFM)]), "Copy")
+    CT = [tile("H", ("CT", q), n) for q in range(4)]
     for q in range(4):
-        CT.append(tile("H", ("CT", q), n))
-        act(CT[q], sub(ones, 0, n), "Identity", nl, float(q))
-    r2 = col("r2", r_i, 2.0, None, "is_lt")
-    p1 = col("p1", j_i, 1.0, 2.0, "is_equal", "mult")
-    p2 = col("p2", j_i, 2.0, -2.0, "is_equal", "mult")
-    p3 = col("p3", p1, p2, r2, "add", "mult")
-    Mp = scaled(B, col("cP", p3, cA, None, "subtract"), "Mp")
-    Mc = scaled(B, col("cC", cA, 16.0, M(2), "mult", "add"), "Mc")
+        act(CT[q], one, "Identity", nl, float(q))
+    p1 = col("p1", M(4), M(5), 2.0, "add", "mult")
+    p2 = col("p2", M(8), M(9), -2.0, "add", "mult")
+    Mp = scaled(B, col("cP", p1, p2, cA, "add", "subtract"), "Mp")
+    Mc = scaled(B, lin("cC", cA, 16.0, M(2)), "Mc")
     cur[2] = "unpack"
-    for c in range(2):
+    for c in range(4 if FT else 0):
+        w, hb, P = sub(vw, 512 * c, 512 * c + 512), tile("F", ("hb", c), 512), ps()
+        ts(hb, w, -(4096 * 2047 + 2047.5), BIGM * 4096, "add", "add")
+        act(P, hb, "Copy", (2047 - BIGM) * 4096)
+        act(sub(vtab, 2048 + 512 * c, 2560 + 512 * c), hb, "Copy", 2047 - BIGM, 2.0 ** -12)
+        tt(sub(vtab, 512 * c, 512 * c + 512), w, P, "subtract")
+    for c in range(0 if FT else 2):
         ts(sub(vtab, 1024 * c, 1024 * c + 1024), sub(vw, 1024 * c, 1024 * c + 1024), 4095, None, "bitwise_and")
         ts(sub(vtab, 2048 + 1024 * c, 3072 + 1024 * c), sub(vw, 1024 * c, 1024 * c + 1024), 12, None, "logical_shift_right")
     outz, outf, outv, outc = [tile("F", k, 192) for k in ("oz", "of", "ov", "oc")]
@@ -248,65 +273,73 @@ def build():
         en, off = {}, {}
         for x in order:
             cur[:] = [x, t, "like"]
-            sent = ("zm", "zland", "vl", "vland", "ff", "fland", "vs", "sland")
+            sent = ("zm", "zland", "msg", "land")
             k = lambda s: (s, x, t if s in sent else t & 1)
             z, me, f, vs, vl = Z[x], ME[x], Fin[x], vS[x], vL[x]
+            if t:
+                vl = tile("U", k("vlu"), M6)
+                ts(vl, vL[x], voff, None, "add")
+            hm = tile("F", k("hm"), n)
+            out_ = sub(tile("E", k("msg"), 4 * n + 16), 0, 4 * n + M6)
             T0, T1, T2, T3, T4 = [ap("vps%d" % x, n * q, n * q + n) for q in range(5)]
             xb, ay, a, NL, NLy = [tile("H", k(s), n) for s in ("x", "ay", "a", "NL", "NLy")]
-            act(xb, ("I", px, vl), "Copy")
-            y = mmo([(nI, z), None, (I, xb)])
-            act(ay, y, "Abs")
-            ts(a, ay, 60.0, None, "is_le")
-            ts(NL, mmo(([(Mp, me), None] if t else []) + [(B, a)]), 8.0, None, "is_lt")
+            if FY:
+                y = xb
+                tt(y, ("I", px, vl), z, "subtract")
+                ts(a, y, 60.0, None, "is_le")
+                ts(ay, y, -60.0, None, "is_ge")
+                below(NL, mmo(([(Mp, me), None] if t else []) + [(B, a), (B, ay)]), 24)
+                xs = [z, y]
+            else:
+                act(xb, ("I", px, vl), "Copy")
+                y = mmo([(nI, z), None, (I, xb)])
+                act(ay, y, "Abs")
+                below(a, ay, 61)
+                below(NL, mmo(([(Mp, me), None] if t else []) + [(B, a)]), 8)
+                xs = [xb]
             tt(NLy, y, NL, "mult")
             cur[2] = "hash"
             R, fl, hp, h, Hl = tile("H", k("R"), n), tile("J", k("fl"), n), tile("J", k("hp"), n), tile("J", k("h"), n), tile("U", k("Hl"), n)
-            ts(R, mmo([(B, CU), (wB, z)]), BIGM * 4096, BIGM * 4096, "add", "subtract")
-            ts(fl, mmo([(wB, z), None, (nI, R)]), kf, floff, "mult", "add")
-            if PK:
-                us = tile("J", k("us"), n)
-                tt(hp, fl, mmo(([(I, CX)] if V16 else []) + [(I613, vs)]), "add")
-                ts(us, hp, 4095, None, "bitwise_and")
-                tt(T1, us, f, "subtract")
-                cur[2] = "pick"
-                tt(T1, T1, NL, "mult")
-                tt(h, T1, f, "add")
-            else:
-                tt(T0, fl, mmo(([(I, CX)] if V16 else []) + [(I613, vs)]), "add")
-                tt(T1, T0, f, "subtract")
-                cur[2] = "pick"
-                tt(T1, T1, NL, "mult")
-                tt(hp, T1, f, "add")
+            if HI:
+                cp(hp, mmo([(wB, z)]))
                 ts(h, hp, 4095, None, "bitwise_and")
+                ts(fl, h, kf, -262143.484375, "mult", "add")
+            else:
+                ts(R, mmo([(B, CU), (wB, z)]), BIGM * 4096, BIGM * 4096, "add", "subtract")
+                ts(fl, mmo([(wB, z), None, (nI, R)]), kf, -262143.484375, "mult", "add")
+            tt(T1, fl, mmo([(nIv, f), (I613, vs)]), "add")
+            cur[2] = "pick"
+            tt(hm, T1, NL, "mult")
+            tt(hp, hm, mmo([(I2047, one16), (Iv, f)]), "add")
+            ts(h, hp, 4095, None, "bitwise_and")
             cp(Hl, h)
             cur[2] = "E"
             El = tile("U", k("El"), n)
             cp(El, ("I", vtab, vl))
-            cp(T2, El)
             cur[2] = "q"
             P, nqT = rows(ps(128), 0, n), tile("H", k("nqT"), 128)
-            mm([(P, xb, nI), None, (P, NLy, I)])
+            mm([(P, u, nI) for u in xs] + [None, (P, NLy, I)])
             act(rows(nqT, 0, n), P, "Copy")
             nxT = nqT
             if x in XE:
                 cur[2] = "xT"
                 P, nxT = rows(ps(128), 0, n), tile("H", k("nxT"), 128)
-                mm([(P, xb, nI)])
+                mm([(P, u, nI) for u in xs])
                 act(rows(nxT, 0, n), P, "Copy")
             dist = {}
             for which, lst, nqT in (("E", El, nxT), ("H", Hl, nqT)):
                 cur[2] = which
                 raw, dist[which] = tile("H", ("raw", which, x), 16 * n), tile("H", ("d", which, x), 16 * n)
+                cuts = CUTS[which, x]
+                for c0, c1 in zip(cuts, cuts[1:]):
+                    act(sub(raw, 16 * c0, 16 * c1), ("I", px, sub(lst, c0, c1)), "Copy")
                 for c in range(3):
                     r, dd = sub(raw, 512 * c, 512 * c + 512), sub(dist[which], 512 * c, 512 * c + 512)
-                    win = ("I", px, sub(lst, 32 * c, 32 * c + 32))
-                    if GATH[which, x][c] == "V":
-                        cp(r, win)
-                    else:
-                        act(r, win, "Copy")
-                    act(dd, mmo([(rows(nqT, 32 * c, 32 * c + 32), rows(EXP, 32 * c, 32 * c + 32)), None, (I, r)], 512), "Abs")
+                    act(dd, mmo([(rows(nqT, 32 * c, 32 * c + 32), rows(EXP, 32 * c, 32 * c + 32)), None, (I, r)], 512), *(("Relu", 0.0, 2.0) if which == "E" and x in RE else ("Abs",)))
+                if which == "E":
+                    minus = [(B, u) for u in xs] + [(NSEL(q), sub(raw, q, 16 * n, 16)) for q in range(16)] + [None] if x in RE else []
             cur[2] = "sum"
-            De = mmo([(nI8k, NL)] + [(SEL(q), sub(dist["E"], q, 16 * n, 16)) for q in range(16)])
+            De = mmo([(nI8k, NL)] + minus + [(SEL(q), sub(dist["E"], q, 16 * n, 16)) for q in range(16)])
             key, k1, k2, k3 = [tile("F", k(("key", q)), n) for q in range(4)]
             if KPE:
                 P = mmo([(I, CK)] + [(SEL(q), sub(dist["H"], q, 16 * n, 16)) for q in range(16)])
@@ -327,51 +360,56 @@ def build():
             mm([(P, I, CS), (even(P), I, even(over)), (odd(P), nI, odd(over))])
             scan(sw, CAP, P, 0.0, "add", "min")
             cp(src, sub(sw, 15, n, 16))
-            zm = tile("H", k("zm"), 2 * n)
+            zm = tile("H", k("zm"), 2 * n) if MSG == 2 else sub(out_, 0, 2 * n)
             z2, me2, z1 = sub(zm, 0, n), sub(zm, n, 2 * n), tile("F", k("z1"), n)
             P = ps(n)
-            mm([(P, Mm, me), (P, Mn, NL), (even(P), Ms, odd(me)), (odd(P), Ms, even(me)), (P, Mo, over)])
+            mm([(P, Mm, me), (P, Mn, NL)] + ([(even(P), Ms, odd(me)), (odd(P), Ms, even(me))] if t else []) + [(P, Mo, over)])
             act(me2, P, "Relu", mb)
-            act(z1, mmo([(Ih, z), (Ih, xb), (nIh, NLy)]), "Copy", BIGM, 1 - 2.0 ** -10)
+            act(z1, mmo([(I if FY else Ih, z), (Ih, xb), (nIh, NLy)]), "Copy", BIGM, 1 - 2.0 ** -10)
             act(z2, ("I", z1, src), "Copy", -BIGM)
-            if t < 3:
+            if t < 3 and MSG == 2:
                 land = tile("H", k("zland"), 2 * n)
                 send(land, zm)
                 Z[x], ME[x] = sub(land, 0, n), sub(land, n, 2 * n)
-            else:
-                cp(sub(outz, x * n, x * n + n), z2)
+            if t == 3:
+                act(sub(outz, x * n, x * n + n), z2, "Copy")
                 act(sub(outc, x * n, x * n + n), mmo([(Mc, me2)]), "Copy")
             cur[2] = "place"
-            P, R16 = mmo([(I, CT[t]), (Ih, NL), (I7, over), None, (B, z2)]), tile("F", k("R16"), n)
+            P, R16 = mmo([(I, CT[t])] + [(Ih, NL), (I7, over), None, (B, z2)]), tile("F", k("R16"), n)
             ts(R16, P, BIGM * 16, BIGM * 16, "add", "subtract")
-            if WF:
-                T3 = tile("H", k("OH"), n)
+            T3 = tile("H", k("OH"), n)
             tt(T3, R16, P, "is_equal")
             cur[2] = "e"
-            hm, chm = tile("F", k("hm"), n), tile("F", k("chm"), n)
             en[x] = tile("F", k("en"), n)
-            tt(hm, h, T2, "subtract")
-            tt(T0, key, De, "is_lt")
-            tt(chm, hm, T0, "mult")
-            tt(en[x], chm, T2, "add")
-            f2 = tile("F", k("ff"), n) if t < 3 else sub(outf, x * n, x * n + n)
-            act(f2, ("I", en[x], src), "Copy")
+            tt(hm, ("I", vtab, vl), h, "subtract")
+            tt(T0, key, De, "is_ge")
+            tt(T2, hm, T0, "mult")
+            tt(en[x], T2, h, "add")
+            if t < 3:
+                act(sub(out_, 2 * n, 3 * n), ("I", en[x], src), "Copy", -2047.0)
+            else:
+                act(sub(outf, x * n, x * n + n), ("I", en[x], src), "Copy")
             W1, W3 = tile("F", k("W1"), n), tile("F", k("W3"), n)
-            tt(W1, ("I", en[x], src) if WF else f2, T3, "mult")
+            tt(W1, ("I", en[x], src), T3, "mult")
             cur[2] = "least"
             scan(k2, RST, k1, 1e6, "add", "min")
             tr(k3, k2)
             tt(T1, key, mmo([(I8k, sub(ones, 0, n)), (nI8k, NL), (I8k, over), None, (LAST, k3)]), "is_equal")
-            tt(W3, h, T1, "mult")
+            tt(T1 if WM else W3, h, T1, "mult")
             cur[2] = "v"
-            P = mmo([(B32, W1), None, (B32, W3)])
+            if WM:
+                tt(W3, W1, T1, "add")
+                P = mmo([(B32, W3)])
+            else:
+                P = mmo([(B32, W1), None, (B32, W3)])
             if t < 3:
-                lst, rep = tile("U", k("vl"), M6), tile(vpool, k("vs"), n)
-                users(P, lst, rep)
-                vL[x], vS[x], Fin[x] = tile("U", k("vland"), M6), tile(vpool, k("sland"), n), tile("F", k("fland"), n)
-                send(vL[x], lst)
-                send(Fin[x], f2)
-                send(vS[x], rep)
+                users(P, sub(out_, 4 * n, 4 * n + M6), sub(out_, 3 * n, 4 * n), unhold2)
+                land = sub(tile("E", k("land"), 4 * n + 16), 0, 4 * n + M6)
+                c0 = 2 * n if MSG == 2 else 0
+                send(sub(land, c0, 4 * n + M6), sub(out_, c0, 4 * n + M6))
+                Fin[x], vS[x], vL[x] = sub(land, 2 * n, 3 * n), sub(land, 3 * n, 4 * n), sub(land, 4 * n, 4 * n + M6)
+                if MSG == 1:
+                    Z[x], ME[x] = sub(land, 0, n), sub(land, n, 2 * n)
             else:
                 act(sub(outv, x * n, x * n + n), P, "Copy")
             cur[2] = "write"
@@ -394,12 +432,16 @@ def build():
         dma(D(nm, 192), o)
     for o, nm in ((outv, "yv"), (outc, "yc")):
         dma(D(nm, 192, 8), lane_rows(o, 0))
-    for c in range(4):
-        q = ap("vps%d" % (c & 1), 0, 512)
-        o = tile("F", ("yw", c), 512)
-        ts(q, sub(vtab, 2048 + 512 * c, 2560 + 512 * c), 4096.0, None, "mult")
-        tt(o, sub(vtab, 512 * c, 512 * c + 512), q, "add")
-        dma(ap("yw", 512 * c, 512 * c + 512), o, "YS"[c & 1])
+    cuts = (0, 256, 768, 1280, 1792, 2048)
+    for c, (c0, c1) in enumerate(zip(cuts, cuts[1:])):
+        q, o = ap("vps%d" % (c & 1), 0, c1 - c0), tile("F", ("yw", c), c1 - c0)
+        if FT:
+            q = ps(c1 - c0)
+            act(q, sub(vtab, 2048 + c0, 2048 + c1), "Copy", 0.0, 4096.0)
+        else:
+            ts(q, sub(vtab, 2048 + c0, 2048 + c1), 4096.0, None, "mult")
+        tt(o, sub(vtab, c0, c1), q, "add")
+        dma(ap("yw", c0, c1), o, "YS"[c & 1])
     return ops, size
 
 
@@ -407,9 +449,9 @@ def pat(a):
     return a[7] if len(a) > 7 else 1
 
 
-def cost(o):
+def cost(ins, GATHER, SCATTER, ISSUE):
     c = 0.0
-    for i in o["ins"]:
+    for i in ins:
         k = i[0]
         if k == "mm":
             f = 4 if i[2][1] == "F" else 1
@@ -419,11 +461,11 @@ def cost(o):
         elif k == "dma":
             c += .06
         elif k == "rd":
-            c += .8
+            c += ISSUE
         elif i[1][0] == "I":
-            c += .05 + 3.8 * width(i[1][2]) * 16 * .83e-3
+            c += .05 + SCATTER * width(i[1][2]) * 16 * .83e-3
         elif k != "ms" and i[2][0] == "I":
-            c += (.065 if k == "act" else .05) + 1.56 * width(i[2][2]) * 16 * .83e-3
+            c += (.065 if k == "act" else .05) + GATHER * width(i[2][2]) * 16 * .83e-3
         else:
             w = width(i[1])
             b16 = lambda a: a[1] in ("H", "U", "E")
@@ -432,13 +474,14 @@ def cost(o):
                 w = w * (1 if ps_ else 2)
             elif k in ("cp", "ts") and b16(i[1]) and b16(i[2]) or k == "ms" and b16(i[1]):
                 w = w * .5
-            c += max(64, w) * .83e-3 + .01
+            c += max(48, w) * .83e-3 + .05
     return c
 
 
-WAKE, OWN, NET, LOADT = .12, .06, 2.6, 2.0
-SCALE = 1.2
-BANKS, LAG, STEPS, SEED = 6, 5.0, 3000, 1
+SPEEDS = [(1.4, 1.6, 1.9, 5.0, 1.0, 2.0, .1, .2, 3e-3, .5e-3, .7, 1.0), (1.15, 2.0, 1.56, 3.8, .8, 1.6, .1, .2, 2e-3, .4e-3, .5, .6),
+          (1.05, 1.05, 1.56, 3.8, .8, 1.6, .1, .2, 2e-3, .4e-3, .5, 1.2)]
+LOADT, TEMP, HOLD0 = 2.0, .12, .5
+BANKS, LAG, STEPS, SEED = 6, 5.0, 2000, 1
 
 
 def analyse():
@@ -457,7 +500,8 @@ def analyse():
                     if i not in tile_ops[buf]:
                         tile_ops[buf].append(i)
                 for (lo, hi, k2, j, st) in hist.setdefault(buf, []):
-                    if j != i and (k2 == "w" or kind == "w" or isinstance(buf, tuple) and ops[j]["e"] != o["e"]) and lo < a[5] and a[4] < hi:
+                    two_ = isinstance(buf, tuple) and (ops[j]["e"] != o["e"] or "alt" in o or "alt" in ops[j])
+                    if j != i and (k2 == "w" or kind == "w" or two_) and lo < a[5] and a[4] < hi:
                         if st == a[6] > 1 and (lo - a[4]) % st:
                             continue
                         deps[i].add(j)
@@ -470,16 +514,22 @@ def analyse():
     pool = [o["i"] for o in ops if o["e"] == "G" and not o.get("dma")]
     for a, b in zip(pool, pool[1:]):
         deps[b].add(a)
-    cst = [cost(o) * (1.0 if o.get("dma") else SCALE) for o in ops]
-    lat = []
-    for o in ops:
-        if o.get("remote"):
-            lat.append(NET)
-        elif o.get("dma"):
-            w = max(width(a) for a in o["wr"]) * (1 if o["wr"][0][1] in ("H", "pxs") else 2)
-            lat.append(LOADT + (w + o.get("behind", 0)) * .8e-3)
-        else:
-            lat.append(0.0)
+    more = []
+    for scale, tensor, gather, scatter, issue, net, own, wake, link, load, rows_, weight in SPEEDS:
+        both = [{e: cost(ins, gather, scatter, issue) * (1.0 if o.get("dma") else tensor if e == "P" else scale) + o.get("table", 0.0) for e, ins in o.get("alt", {o["e"]: o["ins"]}).items()} for o in ops]
+        lat, wire = [0.0] * N, [0.0] * N
+        for i, o in enumerate(ops):
+            if o.get("dma"):
+                a = o["wr"][0]
+                size_ = width(a) * (2 if a[1] in ("H", "U", "E", "pxs") else 4) * (a[3] - a[2]) // pat(a) / 128
+                if o["t"] < 0:
+                    lat[i] = LOADT + (size_ + o.get("behind", 0)) * load
+                else:
+                    lat[i], wire[i] = (net, rows_ + size_ * link) if o.get("remote") else (LOADT, size_ * load)
+        more.append((both, lat, wire, own, wake, weight))
+    both, lat, wire, OWN, WAKE, _ = more.pop(0)
+    cst = [b[o["e"]] for b, o in zip(both, ops)]
+    pred = [[(d, 0 if ops[i].get("more") and d == i - 1 else 2 if ops[d].get("dma") else 1) for d in deps[i]] for i in range(N)]
     prio = [0.0] * N
     succ = [[] for _ in range(N)]
     for i in range(N):
@@ -490,22 +540,29 @@ def analyse():
     eng = [o["e"] for o in ops]
     opens = [None if o.get("more") else next((a[1] for a in o["wr"] if isinstance(a[1], tuple)), None) for o in ops]
     touch = [set(a[1] for a in o["rd"] + o["wr"] if isinstance(a[1], tuple)) for o in ops]
-    gap = [[(q, 0.0 if ops[q].get("more") and q == i + 1 else OWN if eng[q] == eng[i] and not ops[i].get("dma") else WAKE) for q in succ[i]] for i in range(N)]
-    return dict(ops=ops, size=size, eng=eng, opens=opens, touch=touch, gap=gap, deps=deps, succ=succ, tile_ops=tile_ops, cst=cst, lat=lat, prio=prio)
+    gap = [[(q, 0.0 if ops[q].get("more") and q == i + 1 else WAKE if ops[i].get("dma") else OWN) for q in succ[i]] for i in range(N)]
+    return dict(ops=ops, size=size, eng=eng, opens=opens, touch=touch, gap=gap, deps=deps, tile_ops=tile_ops, both=both, lat=lat, wire=wire, wired=[i for i in range(N) if wire[i]], prio=prio, more=more, pred=pred, wake=WAKE)
 
 
-def schedule(an, prio):
-    tile_ops, cst, lat, eng, opens, touch, gap = [an[k] for k in ("tile_ops", "cst", "lat", "eng", "opens", "touch", "gap")]
-    N = len(cst)
+def schedule(an, prio, hold):
+    tile_ops, lat, opens, touch, gap, WAKE, both = [an[k] for k in ("tile_ops", "lat", "opens", "touch", "gap", "wake", "both")]
+    N, eng, wire, busy = len(both), list(an["eng"]), an["wire"], 0.0
     last, bfree = [None] * BANKS, [0.0] * BANKS
     bank_of, left = {}, {b: len(v) for b, v in tile_ops.items()}
     left[None] = 0
-    fin, start, rt, extra = [None] * N, [None] * N, [0.0] * N, [()] * N
-    free, order, ready = [{e: v() for e in "VSPGY"} for v in (float, list, list)]
+    fin, start, rt = [None] * N, [None] * N, [0.0] * N
+    free, order, ready = [{e: v() for e in "VSPGY"} for v in (float, list, dict)]
     ndep = [len(d) for d in an["deps"]]
+
+    def offer(i):
+        if len(both[i]) > 1:
+            ready["V"][i], ready["S"][i] = rt[i] + max(hold[i], 0.0), rt[i] + max(-hold[i], 0.0)
+        else:
+            ready[eng[i]][i] = rt[i]
+
     for i in range(N):
         if ndep[i] == 0:
-            ready[eng[i]].append(i)
+            offer(i)
     for _ in range(N):
         bf, bk = 1e9, None
         for b in range(BANKS):
@@ -514,33 +571,37 @@ def schedule(an, prio):
         first, e = 1e9, None
         for q, lst in ready.items():
             if lst and free[q] < first:
-                s = max(free[q], min([bf if opens[i] and bf > rt[i] else rt[i] for i in lst] if q == "P" else [rt[i] for i in lst]))
+                s = max(free[q], min([bf if opens[i] and bf > r else r for i, r in lst.items()]))
                 if s < first:
                     first, e = s, q
         if e is None:
             return None
         lim = first + .02
-        i = max([i for i in ready[e] if rt[i] <= lim and (bf <= lim or not opens[i])], key=lambda j: prio[j])
-        s = max(rt[i], free[e], bf if opens[i] else 0.0)
-        ready[e].remove(i)
+        i = max([i for i, r in ready[e].items() if r <= lim and (bf <= lim or not opens[i])], key=lambda j: prio[j])
+        s = max(ready[e][i], free[e], bf if opens[i] else 0.0)
+        for q in both[i]:
+            del ready[q][i]
         if opens[i]:
-            if last[bk] is not None:
-                extra[i] = tile_ops[last[bk]]
             last[bk], bank_of[opens[i]] = opens[i], bk
-        start[i], free[e] = s, s + cst[i]
-        f = fin[i] = s + cst[i] + lat[i]
+        start[i], free[e], eng[i] = s, s + both[i][e], e
+        f = fin[i] = free[e] + lat[i]
+        if wire[i]:
+            busy = max(free[e], busy) + wire[i]
+            f = fin[i] = busy + lat[i]
         for tb in touch[i]:
             left[tb] -= 1
             if f + WAKE > bfree[bank_of[tb]]:
                 bfree[bank_of[tb]] = f + WAKE
         order[e].append(i)
         for q, w in gap[i]:
-            if f + w > rt[q]:
-                rt[q] = f + w
+            w = f + (w if eng[q] == e else WAKE)
+            if w > rt[q]:
+                rt[q] = w
             ndep[q] -= 1
             if not ndep[q]:
-                ready[eng[q]].append(q)
-    return dict(order=order, start=start, fin=fin, extra=extra, bank_of=bank_of, span=max(fin))
+                offer(q)
+    order["Y"].sort(key=lambda i: (an["ops"][i]["t"] >= 0, start[i] if an["ops"][i]["t"] >= 0 else i))
+    return dict(order=order, eng=eng, span=max(fin))
 
 
 def tune(an, steps):
@@ -554,32 +615,49 @@ def tune(an, steps):
     sections = [[j for j, k in enumerate(keys) if k[:2] == s] for s in sorted(set(k[:2] for k in keys), key=str)]
     base, rng = np.array(an["prio"]), np.random.default_rng(SEED)
     shift = np.array([-LAG if k[0] == 0 else 0.0 for k in keys])
-    cur = best = schedule(an, list(base + shift[of]))
+    free = sorted(set(of[i] for i, b in enumerate(an["both"]) if len(b) > 1))
+    hold = np.full(len(keys), HOLD0)
+    for (which, x), on in GATH.items():
+        for c, e in enumerate(on):
+            hold[keys.index((x, which, "S", c, True))] = {"S": 9.0, "V": -9.0, "?": HOLD0}[e]
+    cur = best = schedule(an, list(base + shift[of]), list(hold[of]))
+    while not cur:
+        shift = shift + rng.normal(size=len(keys))
+        cur = best = schedule(an, list(base + shift[of]), list(hold[of]))
     for step in range(steps):
-        new = shift.copy()
-        if rng.random() < .25:
+        new, ho, r = shift.copy(), hold.copy(), rng.random()
+        if r < .2:
             new[sections[rng.integers(len(sections))]] += rng.normal() * 2
+        elif r < .45:
+            ho[free[rng.integers(len(free))]] += rng.normal() * 1.5
         else:
             new[rng.integers(len(keys), size=(1, 1, 2, 4)[rng.integers(4)])] += rng.normal() * (.5, 2, 5)[rng.integers(3)]
-        sc = schedule(an, list(base + new[of]))
+        sc = schedule(an, list(base + new[of]), list(ho[of]))
         if sc and sc["span"] < cur["span"] + .3 * (1 - step / steps) * rng.exponential():
-            cur, shift = sc, new
+            cur, shift, hold = sc, new, ho
             if sc["span"] < best["span"]:
                 best = sc
     return best
 
 
-def play(an, order):
-    tile_ops, cst, lat, eng, opens, touch, gap = [an[k] for k in ("tile_ops", "cst", "lat", "eng", "opens", "touch", "gap")]
-    N = len(cst)
-    last, bfree, bby = [None] * BANKS, [0.0] * BANKS, [None] * BANKS
-    bank_of, left = {}, {b: len(v) for b, v in tile_ops.items()}
-    left[None] = 0
-    fin, start, rt, extra, why = [0.0] * N, [0.0] * N, [0.0] * N, [()] * N, [None] * N
-    ndep = [len(d) for d in an["deps"]]
+def play(an, order, eng, old=None, same=0):
+    tile_ops, lat, opens, touch, gap, both, WAKE = [an[k] for k in ("tile_ops", "lat", "opens", "touch", "gap", "both", "wake")]
+    N, wire = len(eng), an["wire"]
+    if old:
+        kept = old["kept"][:same // 64 + 1]
+        last, bfree, bby, bank_of, left, rt, why, ndep, pos, free, prev = [a.copy() for a in kept.pop()]
+        fin, start, extra, step = [old[k].copy() for k in ("fin", "start", "extra", "step")]
+    else:
+        kept, last, bfree, bby = [], [None] * BANKS, [0.0] * BANKS, [None] * BANKS
+        bank_of, left = {}, {b: len(v) for b, v in tile_ops.items()}
+        left[None] = 0
+        fin, start, rt, extra, why, step = [0.0] * N, [0.0] * N, [0.0] * N, [()] * N, [None] * N, [0] * N
+        ndep = [len(d) for d in an["deps"]]
+        pos, free, prev = [0] * 5, [0.0] * 6, [None] * 5
     qs = [order[e] + [None] for e in "VSPGY"]
-    pos, free, prev = [0] * 5, [0.0] * 5, [None] * 5
-    for _ in range(N):
+    for now in range(64 * len(kept), N):
+        if not now & 63:
+            kept.append([a.copy() for a in (last, bfree, bby, bank_of, left, rt, why, ndep, pos, free, prev)])
         s, e = 1e9, None
         for q in range(5):
             i = qs[q][pos[q]]
@@ -602,61 +680,118 @@ def play(an, order):
         if s > rt[i]:
             why[i] = prev[e] if s == free[e] else bby[bk]
         if opens[i]:
-            if last[bk] is not None:
-                extra[i] = tile_ops[last[bk]]
+            extra[i] = tile_ops.get(last[bk], ())
             last[bk], bank_of[opens[i]] = opens[i], bk
-        start[i], free[e], prev[e] = s, s + cst[i], i
-        f = fin[i] = s + cst[i] + lat[i]
+        start[i], free[e], prev[e], step[i] = s, s + both[i][eng[i]], i, now
+        f = fin[i] = free[e] + lat[i]
+        if wire[i]:
+            free[5] = max(free[e], free[5]) + wire[i]
+            f = fin[i] = free[5] + lat[i]
         for tb in touch[i]:
             left[tb] -= 1
             b = bank_of[tb]
             if f + WAKE > bfree[b]:
                 bfree[b], bby[b] = f + WAKE, i
         for q, w in gap[i]:
-            if f + w > rt[q]:
-                rt[q], why[q] = f + w, i
+            w = f + (w if eng[q] == eng[i] else WAKE)
+            if w > rt[q]:
+                rt[q], why[q] = w, i
             ndep[q] -= 1
-    return dict(order=order, start=start, fin=fin, extra=extra, bank_of=bank_of, span=max(fin), why=why)
+    return dict(order=order, start=start, fin=fin, extra=extra, bank_of=bank_of, span=max(fin), why=why, eng=eng, step=step, kept=kept)
+
+
+def again(an, run, old=None, same=0):
+    eng, extra, N = run["eng"], run["extra"], len(run["eng"])
+    seq = sorted(range(N), key=lambda i: run["step"][i])[same:]
+    before = [None] * N
+    for lst in run["order"].values():
+        for a, b in zip(lst, lst[1:]):
+            before[b] = a
+    run["more"], run["sum"] = [], run["span"]
+    for m, (both, lat, wire, own, wake, weight) in enumerate(an["more"]):
+        fin, why, done = [a.copy() for a in old["more"][m]] if old else ([0.0] * N, [None] * N, [0.0] * N)
+        busy = max([fin[i] - lat[i] for i in an["wired"] if wire[i] and run["step"][i] < same] + [0.0])
+        for i in seq:
+            y = before[i]
+            s = 0.0 if y is None else done[y]
+            for d, kind in an["pred"][i]:
+                w = fin[d] + (wake if eng[d] != eng[i] or kind == 2 else own * kind)
+                if w > s:
+                    s, y = w, d
+            for d in extra[i]:
+                if fin[d] + wake > s:
+                    s, y = fin[d] + wake, d
+            done[i] = s = s + both[i][eng[i]]
+            if wire[i]:
+                s = busy = max(s, busy) + wire[i]
+            fin[i], why[i] = s + lat[i], y
+        run["more"].append((fin, why, done))
+        run["sum"] += weight * max(fin)
+    return run
 
 
 def refine(an, sc, steps):
-    rng, eng, deps = np.random.default_rng(SEED), an["eng"], an["deps"]
-    pick = lambda a: a[rng.integers(len(a))]
-    cur = best = play(an, sc["order"])
-    path = None
+    rng, deps = np.random.default_rng(SEED), an["deps"]
+    cur = best = again(an, play(an, sc["order"], sc["eng"]))
+    paths = None
+    draws = rng.random((steps, 7)).tolist()
     for step in range(steps):
-        if path is None:
-            i, path = cur["fin"].index(cur["span"]), []
-            while cur["why"][i] is not None:
-                if cur["why"][i] not in deps[i]:
-                    path.append((cur["why"][i], i))
-                i = cur["why"][i]
-        u, v = pick(path)
-        order = dict(cur["order"])
-        if rng.random() < .5:
+        draw = draws[step]
+        pick = lambda a: a[int(draw.pop() * len(a))]
+        if paths is None:
+            paths = []
+            for fin, why, _ in [(cur["fin"], cur["why"], 0)] + cur["more"]:
+                i = fin.index(max(fin))
+                paths.append([])
+                while why[i] is not None:
+                    if why[i] not in deps[i]:
+                        paths[-1].append((why[i], i))
+                    i = why[i]
+        u, v = pick(pick(paths))
+        order, eng, r, same = dict(cur["order"]), cur["eng"], draw.pop(), 1 << 20
+        if r < .15:
+            a = order[eng[u]][max(0, order[eng[u]].index(u) - pick((0, 0, 1, 2, 3, 5)))]
+            if len(an["both"][a]) == 1:
+                continue
+            e = "V" if eng[a] == "S" else "S"
+            p = order[eng[a]].index(a)
+            same = min([cur["step"][i] for i in list(deps[a]) + order[eng[a]][max(0, p - 1):p]] + [cur["step"][a] if p else 0])
+            order[eng[a]] = order[eng[a]][:p] + order[eng[a]][p + 1:]
+            order[e] = sorted(order[e] + [a], key=lambda i: (cur["start"][i], i))
+            eng, d = list(eng), pick((-1, 0, 0, 1))
+            eng[a] = e
+        elif r < .55:
             a, d = v if eng[u] == eng[v] else u, -pick((1, 1, 2, 3, 5))
         elif eng[u] != eng[v]:
-            a, d = order["P"][max(0, order["P"].index(v) - pick(range(1, 8)))], pick((1, 2, 4, 8))
+            a, d = order[eng[v]][max(0, order[eng[v]].index(v) - pick(range(1, 8)))], pick((1, 2, 4, 8))
         else:
             k = pick((0, 0, 0, 1, 2))
             a, d = order[eng[u]][max(0, order[eng[u]].index(u) - k)], k + pick((1, 1, 2, 3, 5))
+        if eng[a] == "Y":
+            continue
         lst = order[eng[a]] = list(order[eng[a]])
         p = lst.index(a)
+        if any(i in deps[a] for i in lst[max(0, p + d):p]) or any(a in deps[i] for i in lst[p + 1:p + d + 1]):
+            continue
         lst.insert(max(0, p + d), lst.pop(p))
-        new = play(an, order)
-        if new and new["span"] < cur["span"] + .05 * (1 - step / steps) * rng.exponential():
-            cur, path = new, None
-            if new["span"] < best["span"]:
+        p = min(p, p + d) - 1
+        same = min(same, cur["step"][lst[p]]) if p >= 0 else 0
+        new = play(an, order, eng, cur, same)
+        if new and new["span"] < cur["span"] + 1 and again(an, new, cur, same)["sum"] < cur["sum"] - TEMP * (1 - step / steps) * math.log(draw.pop() + 1e-9):
+            cur, paths = new, None
+            if new["sum"] < best["sum"]:
                 best = new
     return best
 
 
 def plan():
     an = analyse()
-    sc = refine(an, tune(an, STEPS), 5 * STEPS)
+    sc = refine(an, tune(an, STEPS), 15 * STEPS)
     sc["extra"] = [set(x) for x in sc["extra"]]
     ops, deps, order, extra, fin = an["ops"], an["deps"], sc["order"], sc["extra"], sc["fin"]
     N = len(ops)
+    for o, e in zip(ops, sc["eng"]):
+        o["e"], o["ins"] = e, o.get("alt", {e: o["ins"]})[e]
     cnt = {e: 0 for e in "VSPG"}
     end, K, clk, waits = {}, {e: {} for e in "VSPGY"}, [None] * N, [None] * N
     ndma = 0
@@ -702,7 +837,7 @@ def plan():
 PLAN = plan()
 _s = PLAN["size"]
 SCRATCH = {
-    "pxs": ("sbuf", [128, 4096], "bfloat16"), "vws": ("sbuf", [128, 2048], "int32"), "vtab": ("sbuf", [128, 4096 + n], "int32"),
+    "pxs": ("sbuf", [128, 4096], "bfloat16"), "vws": ("sbuf", [128, 2048], "int32"), "vtab": ("sbuf", [128, 4096 + n], "float32" if FT else "int32"),
 }
 for _k in DT:
     if _s[_k]:
@@ -745,7 +880,7 @@ def rank_program(g, core, T, topo):
                 "is_lt": OP.is_lt, "is_equal": OP.is_equal, "not_equal": OP.not_equal, "bitwise_and": OP.bitwise_and,
                 "arith_shift_right": OP.arith_shift_right, "logical_shift_right": OP.logical_shift_right}[s]
 
-    fun = {"Copy": AF.Copy, "Abs": AF.Abs, "Relu": AF.Relu, "Identity": AF.Identity}
+    fun = {"Copy": AF.Copy, "Abs": AF.Abs, "Relu": AF.Relu, "Identity": AF.Identity, "Sigmoid": AF.Sigmoid}
     nsent = 0
     total = {}
     for e in "VSPGY":

from concourse.mybir import AluOpType as OP, ActivationFunctionType as AF

import math
import numpy as np

NB, n = 2, 96
M6, BIGM = 6, 12582912.0
DT = {"F": "float32", "H": "bfloat16", "J": "int32", "U": "uint16", "E": "float16"}
XE, KPE, MSG, RE, FY, FT, VF, HI, WM = (), False, 2, (), True, False, False, False, False
GATH = {("E", 0): "???", ("H", 0): "???", ("E", 1): "???", ("H", 1): "???"}
CUTS = {("E", 0): (0, 32, 64, 96), ("H", 0): (0, 32, 64, 96), ("E", 1): (0, 32, 64, 96), ("H", 1): (0, 32, 64, 96)}


def ap(buf, c0, c1, st=1, r0=0, r1=128):
    return ("ap", buf, r0, r1, c0, c1, st)


def sub(a, c0, c1, st=1):
    return ("ap", a[1], a[2], a[3], a[4] + c0, a[4] + c1, st)


def rows(a, r0, r1):
    return ("ap", a[1], r0, r1, a[4], a[5], a[6])


def width(a):
    return -(-(a[5] - a[4]) // a[6])


def build():
    ops, size, tiles, psn = [], {k: 0 for k in DT}, {}, [0]
    cur = [None, -1, "setup"]

    def tile(pool, key, w):
        k = (pool, key)
        if k not in tiles:
            tiles[k] = ap(pool, size[pool], size[pool] + w)
            size[pool] += -(-w // 16) * 16
        return tiles[k]

    def ps(w=512):
        psn[0] += 1
        return ap(("ps", psn[0]), 0, w)

    def add(e, ins, rd, wr, **kw):
        o = dict(e=e, ins=ins, x=cur[0], t=cur[1], sec=cur[2], rd=[r for r in rd if isinstance(r, tuple)], wr=wr, i=len(ops))
        o.update(kw)
        ops.append(o)

    def two(x):
        return list(x[1:]) if x[0] == "I" else [x]

    def outs(x):
        return ([x[2]], [x[1]]) if x[0] == "I" else ([], [x])

    def tt(out, a, b, op):
        add("V", [("tt", out, a, b, op)], two(a) + [b], [out])

    def ts(out, a, s1, s2, op0, op1=None):
        add("V", [("ts", out, a, s1, s2, op0, op1)], two(a) + [s1, s2], [out])

    def cp(out, a):
        add("V", [("cp", out, a)], two(a) + outs(out)[0], outs(out)[1])

    def ms(out, v):
        add("V", [("ms", out, v)], [], [out])

    def scan(out, d0, d1, init, op0, op1):
        add("V", [("scan", out, d0, d1, init, op0, op1)], [d0, d1], [out])

    def tr(out, a):
        add("V", [("tr", out, a)], [a], [out])

    def act(out, a, func, bias=0.0, scale=1.0, on="S"):
        alt = {"S": [("act", out, a, func, bias, scale)]}
        if func == "Relu" and scale == 1.0:
            alt["V"] = [("ts", out, a, bias, 0.0, "add", "max")]
        elif func == "Relu" and bias == 0.0:
            alt["V"] = [("ts", out, a, 0.0, scale, "max", "mult")]
        elif func == "Sigmoid":
            alt["V"] = [("ts", out, a, -bias / scale, None, "is_lt", None)]
        elif func in ("Copy", "Identity"):
            alt["V"] = [("cp", out, a)] if (bias, scale) == (0.0, 1.0) else [("ts", out, a, scale, bias, "mult", "add")]
        add(on, alt[on], two(a) + [bias, scale], [out], alt=alt)

    def below(out, a, c):
        act(out, a, "Sigmoid", 256.0 * (c - .5), -256.0)

    def mm(group):
        parts, all_ = [[]], [m for m in group if m]
        for m in group:
            if m:
                parts[-1].append(m)
            else:
                parts.append([])
        for p in parts:
            add("P", [("mm", *m, m is all_[0], m is all_[-1]) for m in p], [x for _, l, r in p for x in (l, r)], [all_[0][0]], more=p is not parts[0])

    def mmo(group, w=n):
        P = ps(w)
        mm([m and (P, *m) for m in group])
        return P

    def iota(out, pattern, base, cm):
        add("G", [("iota", out, pattern, base, cm)], [], [out])

    def asel(out, a, pattern, cmp, fill, base, cm):
        add("G", [("asel", out, a, pattern, cmp, fill, base, cm)], [a], [out])

    def dma(out, a, eng="Y"):
        add(eng, [("dma", out, a)], [a], [out], dma=1)

    def send(out, a):
        add("G", [("rd", out, a)], [a], [out], dma=1, remote=1)

    def lane_rows(a, r):
        return ("ap", a[1], r, 128, a[4], a[5], 1, 16)

    D = lambda nm, c1, r1=128: ap(nm, 0, c1, 1, 0, r1)
    px, vw, vtab = ap("pxs", 0, 4096), ap("vws", 0, 2048), ap("vtab", 0, 4096 + n)
    v0i, d0i, f0i = tile("J", "v0i", 192), tile("J", "d0i", 192), tile("J", "f0i", 192)
    wi, ki, z0s = tile("J", "wi", 1), tile("J", "ki", 1), tile("H", "z0s", 192)
    ms(v0i, 0)
    ms(d0i, 0)
    dma(lane_rows(v0i, 0), D("v0", 192, 8))
    if not VF:
        dma(px, D("px", 4096))
    dma(z0s, D("z0", 192), "S")
    dma(wi, D("wt", 1), "S")
    dma(ki, D("kap", 1), "S")
    dma(f0i, D("f0", 192), "S")
    dma(lane_rows(d0i, 2), D("d0", 192, 8), "S")
    dma(lane_rows(d0i, 6), D("d0", 192, 8), "S")
    for c in range(2):
        dma(sub(vw, 1024 * c, 1024 * c + 1024), ap("vw", 1024 * c, 1024 * c + 1024))
        ops[-1]["behind"] = (0 if VF else 8192) + 4096 * c
    if VF:
        dma(px, D("px", 4096))
        ops[-1]["behind"] = 8192
    ones, B, I = tile("H", "ones", 512), tile("H", "B", 128), tile("H", "I", 128)
    ms(ones, 1.0)
    pi = tile("J", "pi", 1)
    iota(pi, [[0, 1]], 0, 1)
    kkf, sf = tile("F", "kkf", 2 * n), tile("H", "sf", n)
    iota(kkf, [[0, 2 * M6], [1, 16]], 0, 0)
    t = tile("H", "Bt", 128)
    asel(t, sub(ones, 0, 128), [[-16, 8], [0, 16]], "is_ge", 0.0, 0, 1)
    asel(B, t, [[16, 8], [0, 16]], "is_ge", 0.0, 15, -1)
    asel(I, sub(ones, 0, 128), [[-1, 128]], "is_equal", 0.0, 0, 1)
    zero = tile("H", "zero", 128 * 3 + 144)
    ms(zero, 0.0)

    def diag(s):
        o = tile("H", ("diag", s), 128)
        asel(o, sub(zero, 0, 128), [[-1, 128]], "not_equal", s, 0, 1)
        return o

    nI, Ih = diag(-1.0), diag(.5)
    EXP = tile("H", "EXP", 512)
    for c in range(3):
        asel(rows(EXP, 32 * c, 32 * c + 32), rows(ones, 32 * c, 32 * c + 32), [[-1, 32], [0, 16]], "is_equal", 0.0, 0, 1)
    iota(sf, [[1, n]], 0, 0)
    nIh, nI8k, I8k, I16k, I7 = [diag(s) for s in (-.5, -8192.0, 8192.0, 16384.0, 7.5)]
    one = sub(ones, 0, n)

    def lin(key, a, scale, bias):
        o = tile("F", key, 1)
        act(o, a, "Identity" if isinstance(bias, tuple) else "Copy", bias, scale)
        return o

    def col(key, a, s1, s2, op0, op1=None, pool="F"):
        o = tile(pool, key, 1)
        ts(o, a, s1, s2, op0, op1)
        return o

    def scaled(base, s, key, pool="H"):
        o = tile(pool, key, width(base))
        act(o, base, "Copy", 0.0, s)
        return o

    lane_i = col("lane_i", pi, 15, None, "bitwise_and", pool="J")
    lane = tile("F", "lane", 1)
    cp(lane, lane_i)
    MASK, HOLD = tile("F", "MASK", 2 * n), tile("F", "HOLD", 2 * n)
    ts(MASK, kkf, lane, None, "is_equal")
    act(HOLD, MASK, "Copy", -8192.0, 1048576.0)
    MASK = sub(MASK, 0, n)
    CAP = scaled(MASK, 1048576.0, "CAP", "F")
    M = lambda j: sub(MASK, j, j + 1)
    unhold = lin("unhold", lane, -8192.0, 15 * 8192.0)
    B32 = scaled(B, 1.0, "B32", "F")
    v0f = tile("F", "v0f", 192)
    cp(v0f, v0i)
    vpool, voff = "E", 2048.0

    unhold2 = lin("unhold2", lane, -8192.0, 15 * 8192.0 - voff)

    def users(P, lst, rep, unhold):
        b = tile("F", ("pw", cur[0]), width(P))
        scan(b, sub(HOLD, 0, width(P)), P, 0.0, "add", "min")
        ts(lst, sub(b, 15, width(P), 16), unhold, None, "add")
        act(rep, P, "Copy", -voff)

    order = (1, 0)
    vL, vS = tile("U", "vL0", 2 * M6), tile(vpool, "vS0", 2 * n)
    users(mmo([(B32, v0f)], 2 * n), vL, vS, unhold)
    vL, vS = {x: sub(vL, M6 * x, M6 * x + M6) for x in order}, {x: sub(vS, n * x, n * x + n) for x in order}
    Iv, nIv, I613, I2047 = [scaled(I, s, ("Iv", s), vpool) for s in (1.0, -1.0, 613.0, 2047.0)]
    wf, kf = tile("F", "wf", 1), col("kf", ki, 1 / 32, None, "mult")
    cp(wf, wi)
    wB = scaled(B, wf, "wB")
    if not HI:
        CU = scaled(one, lin("c1", M(1), 0.5, lin("c0", M(0), -2048.0, 0.0)), "CU")
    one16 = scaled(one, 1.0, "one16", "E")
    SELW = sub(zero, 384, 528)
    act(sub(SELW, 15, 143, 16), sub(B, 0, 128, 16), "Copy")
    SEL = lambda q: sub(SELW, 15 - q, 143 - q)
    if RE:
        NSELW = scaled(SELW, -1.0, "NSELW")
        NSEL = lambda q: sub(NSELW, 15 - q, 143 - q)
    Fin, Z, ME = {}, {}, {}
    me0, f0f = tile("H", "me0", 192), tile("E", "f0f", 192)
    ts(me0, d0i, M(6), 0.0, "subtract", "max")
    ts(f0f, f0i, -2047.0, None, "add")
    for x in order:
        Z[x], ME[x], Fin[x] = [sub(a, x * n, x * n + n) for a in (z0s, me0, f0f)]
    r_i = col("r_i", pi, 3, None, "bitwise_and", pool="J")
    j_i = col("j_i", pi, 2, 3, "logical_shift_right", "bitwise_and", pool="J")
    e0c, e1c, e2c = [col(("e", q), r_i, float(q), None, "is_equal") for q in range(3)]
    Mo = scaled(I, lin("cO", e1c, 16.0, -8.0), "Mo")
    Mn = scaled(I, col("cN", e2c, 8.0, e0c, "mult", "subtract"), "Mn")
    mb = col("mb", j_i, -1.0, lin("mb0", e0c, 8.0, -7.0), "mult", "add")
    cA = tile("F", "cA", 1)
    below(cA, lane, 2)
    ops[-1].pop("alt")
    ops[-1]["table"] = 1.3
    Mm, Ms = sub(zero, 128, 256), sub(zero, 256, 384)
    act(sub(Mm, 0, 128, 4), sub(B, 0, 128, 4), "Copy", 0.0, cA)
    act(sub(Mm, 2, 128, 4), sub(B, 2, 128, 4), "Copy", 0.0, M(2))
    act(sub(Ms, 1, 128, 4), sub(B, 1, 128, 4), "Copy", 0.0, cA)
    Mi = scaled(B, lin("cI", M(6), -1.0, M(2)), "Mi")
    klane = lin("klane", lane, 1 / 16, 0.0)
    if KPE:
        CK = scaled(sub(ones, 0, n), klane, "CK")
    RST, LAST = tile("F", "RST", n), scaled(B32, M(15), "LAST", "F")
    act(RST, sub(kkf, 0, n), "Relu", 1e6, -1e6)
    OFFM, DMP = tile("H", "OFFM", n), tile("F", "DMP", n)
    act(OFFM, MASK, "Copy", 32768.0, -32768.0)
    act(DMP, mmo([(I, sf), (nI, OFFM)]), "Copy", 4096.0 + 8192.0 - voff)
    B8k, CS, nl = scaled(B, 8192.0, "B8k"), tile("H", "CS", n), lin("nl", lane, -1.0, 0.0)
    act(CS, mmo([(I, sf), (I, OFFM)]), "Copy")
    CT = [tile("H", ("CT", q), n) for q in range(4)]
    for q in range(4):
        act(CT[q], one, "Identity", nl, float(q))
    p1 = col("p1", M(4), M(5), 2.0, "add", "mult")
    p2 = col("p2", M(8), M(9), -2.0, "add", "mult")
    Mp = scaled(B, col("cP", p1, p2, cA, "add", "subtract"), "Mp")
    Mc = scaled(B, lin("cC", cA, 16.0, M(2)), "Mc")
    cur[2] = "unpack"
    for c in range(4 if FT else 0):
        w, hb, P = sub(vw, 512 * c, 512 * c + 512), tile("F", ("hb", c), 512), ps()
        ts(hb, w, -(4096 * 2047 + 2047.5), BIGM * 4096, "add", "add")
        act(P, hb, "Copy", (2047 - BIGM) * 4096)
        act(sub(vtab, 2048 + 512 * c, 2560 + 512 * c), hb, "Copy", 2047 - BIGM, 2.0 ** -12)
        tt(sub(vtab, 512 * c, 512 * c + 512), w, P, "subtract")
    for c in range(0 if FT else 2):
        ts(sub(vtab, 1024 * c, 1024 * c + 1024), sub(vw, 1024 * c, 1024 * c + 1024), 4095, None, "bitwise_and")
        ts(sub(vtab, 2048 + 1024 * c, 3072 + 1024 * c), sub(vw, 1024 * c, 1024 * c + 1024), 12, None, "logical_shift_right")
    outz, outf, outv, outc = [tile("F", k, 192) for k in ("oz", "of", "ov", "oc")]
    even, odd = (lambda a: sub(a, 0, n, 2)), (lambda a: sub(a, 1, n, 2))

    for t in range(4):
        en, off = {}, {}
        for x in order:
            cur[:] = [x, t, "like"]
            sent = ("zm", "zland", "msg", "land")
            k = lambda s: (s, x, t if s in sent else t & 1)
            z, me, f, vs, vl = Z[x], ME[x], Fin[x], vS[x], vL[x]
            if t:
                vl = tile("U", k("vlu"), M6)
                ts(vl, vL[x], voff, None, "add")
            hm = tile("F", k("hm"), n)
            out_ = sub(tile("E", k("msg"), 4 * n + 16), 0, 4 * n + M6)
            T0, T1, T2, T3, T4 = [ap("vps%d" % x, n * q, n * q + n) for q in range(5)]
            xb, ay, a, NL, NLy = [tile("H", k(s), n) for s in ("x", "ay", "a", "NL", "NLy")]
            if FY:
                y = xb
                tt(y, ("I", px, vl), z, "subtract")
                ts(a, y, 60.0, None, "is_le")
                ts(ay, y, -60.0, None, "is_ge")
                below(NL, mmo(([(Mp, me), None] if t else []) + [(B, a), (B, ay)]), 24)
                xs = [z, y]
            else:
                act(xb, ("I", px, vl), "Copy")
                y = mmo([(nI, z), None, (I, xb)])
                act(ay, y, "Abs")
                below(a, ay, 61)
                below(NL, mmo(([(Mp, me), None] if t else []) + [(B, a)]), 8)
                xs = [xb]
            tt(NLy, y, NL, "mult")
            cur[2] = "hash"
            R, fl, hp, h, Hl = tile("H", k("R"), n), tile("J", k("fl"), n), tile("J", k("hp"), n), tile("J", k("h"), n), tile("U", k("Hl"), n)
            if HI:
                cp(hp, mmo([(wB, z)]))
                ts(h, hp, 4095, None, "bitwise_and")
                ts(fl, h, kf, -262143.484375, "mult", "add")
            else:
                ts(R, mmo([(B, CU), (wB, z)]), BIGM * 4096, BIGM * 4096, "add", "subtract")
                ts(fl, mmo([(wB, z), None, (nI, R)]), kf, -262143.484375, "mult", "add")
            tt(T1, fl, mmo([(nIv, f), (I613, vs)]), "add")
            cur[2] = "pick"
            tt(hm, T1, NL, "mult")
            tt(hp, hm, mmo([(I2047, one16), (Iv, f)]), "add")
            ts(h, hp, 4095, None, "bitwise_and")
            cp(Hl, h)
            cur[2] = "E"
            El = tile("U", k("El"), n)
            cp(El, ("I", vtab, vl))
            cur[2] = "q"
            P, nqT = rows(ps(128), 0, n), tile("H", k("nqT"), 128)
            mm([(P, u, nI) for u in xs] + [None, (P, NLy, I)])
            act(rows(nqT, 0, n), P, "Copy")
            nxT = nqT
            if x in XE:
                cur[2] = "xT"
                P, nxT = rows(ps(128), 0, n), tile("H", k("nxT"), 128)
                mm([(P, u, nI) for u in xs])
                act(rows(nxT, 0, n), P, "Copy")
            dist = {}
            for which, lst, nqT in (("E", El, nxT), ("H", Hl, nqT)):
                cur[2] = which
                raw, dist[which] = tile("H", ("raw", which, x), 16 * n), tile("H", ("d", which, x), 16 * n)
                cuts = CUTS[which, x]
                for c0, c1 in zip(cuts, cuts[1:]):
                    act(sub(raw, 16 * c0, 16 * c1), ("I", px, sub(lst, c0, c1)), "Copy")
                for c in range(3):
                    r, dd = sub(raw, 512 * c, 512 * c + 512), sub(dist[which], 512 * c, 512 * c + 512)
                    act(dd, mmo([(rows(nqT, 32 * c, 32 * c + 32), rows(EXP, 32 * c, 32 * c + 32)), None, (I, r)], 512), *(("Relu", 0.0, 2.0) if which == "E" and x in RE else ("Abs",)))
                if which == "E":
                    minus = [(B, u) for u in xs] + [(NSEL(q), sub(raw, q, 16 * n, 16)) for q in range(16)] + [None] if x in RE else []
            cur[2] = "sum"
            De = mmo([(nI8k, NL)] + minus + [(SEL(q), sub(dist["E"], q, 16 * n, 16)) for q in range(16)])
            key, k1, k2, k3 = [tile("F", k(("key", q)), n) for q in range(4)]
            if KPE:
                P = mmo([(I, CK)] + [(SEL(q), sub(dist["H"], q, 16 * n, 16)) for q in range(16)])
                cur[2] = "least"
                tr(k1, P)
                cur[2] = "sum"
                act(key, P, "Copy")
            else:
                act(key, mmo([(SEL(q), sub(dist["H"], q, 16 * n, 16)) for q in range(16)]), "Identity", klane)
                cur[2] = "least"
                tr(k1, key)
            cur[2] = "count"
            over, sw, src = tile("H", k("ov"), n), tile("F", k("sw"), n), tile("U", k("src"), M6)
            P = ps(n)
            mm([(P, Mi, me), (P, I, NL), (even(P), nI, odd(NL)), (odd(P), nI, even(NL))])
            act(over, P, "Relu", -1.0)
            P = ps(n)
            mm([(P, I, CS), (even(P), I, even(over)), (odd(P), nI, odd(over))])
            scan(sw, CAP, P, 0.0, "add", "min")
            cp(src, sub(sw, 15, n, 16))
            zm = tile("H", k("zm"), 2 * n) if MSG == 2 else sub(out_, 0, 2 * n)
            z2, me2, z1 = sub(zm, 0, n), sub(zm, n, 2 * n), tile("F", k("z1"), n)
            P = ps(n)
            mm([(P, Mm, me), (P, Mn, NL)] + ([(even(P), Ms, odd(me)), (odd(P), Ms, even(me))] if t else []) + [(P, Mo, over)])
            act(me2, P, "Relu", mb)
            act(z1, mmo([(I if FY else Ih, z), (Ih, xb), (nIh, NLy)]), "Copy", BIGM, 1 - 2.0 ** -10)
            act(z2, ("I", z1, src), "Copy", -BIGM)
            if t < 3 and MSG == 2:
                land = tile("H", k("zland"), 2 * n)
                send(land, zm)
                Z[x], ME[x] = sub(land, 0, n), sub(land, n, 2 * n)
            if t == 3:
                act(sub(outz, x * n, x * n + n), z2, "Copy")
                act(sub(outc, x * n, x * n + n), mmo([(Mc, me2)]), "Copy")
            cur[2] = "place"
            P, R16 = mmo([(I, CT[t])] + [(Ih, NL), (I7, over), None, (B, z2)]), tile("F", k("R16"), n)
            ts(R16, P, BIGM * 16, BIGM * 16, "add", "subtract")
            T3 = tile("H", k("OH"), n)
            tt(T3, R16, P, "is_equal")
            cur[2] = "e"
            en[x] = tile("F", k("en"), n)
            tt(hm, ("I", vtab, vl), h, "subtract")
            tt(T0, key, De, "is_ge")
            tt(T2, hm, T0, "mult")
            tt(en[x], T2, h, "add")
            if t < 3:
                act(sub(out_, 2 * n, 3 * n), ("I", en[x], src), "Copy", -2047.0)
            else:
                act(sub(outf, x * n, x * n + n), ("I", en[x], src), "Copy")
            W1, W3 = tile("F", k("W1"), n), tile("F", k("W3"), n)
            tt(W1, ("I", en[x], src), T3, "mult")
            cur[2] = "least"
            scan(k2, RST, k1, 1e6, "add", "min")
            tr(k3, k2)
            tt(T1, key, mmo([(I8k, sub(ones, 0, n)), (nI8k, NL), (I8k, over), None, (LAST, k3)]), "is_equal")
            tt(T1 if WM else W3, h, T1, "mult")
            cur[2] = "v"
            if WM:
                tt(W3, W1, T1, "add")
                P = mmo([(B32, W3)])
            else:
                P = mmo([(B32, W1), None, (B32, W3)])
            if t < 3:
                users(P, sub(out_, 4 * n, 4 * n + M6), sub(out_, 3 * n, 4 * n), unhold2)
                land = sub(tile("E", k("land"), 4 * n + 16), 0, 4 * n + M6)
                c0 = 2 * n if MSG == 2 else 0
                send(sub(land, c0, 4 * n + M6), sub(out_, c0, 4 * n + M6))
                Fin[x], vS[x], vL[x] = sub(land, 2 * n, 3 * n), sub(land, 3 * n, 4 * n), sub(land, 4 * n, 4 * n + M6)
                if MSG == 1:
                    Z[x], ME[x] = sub(land, 0, n), sub(land, n, 2 * n)
            else:
                act(sub(outv, x * n, x * n + n), P, "Copy")
            cur[2] = "write"
            eq1, eq2, ow = tile("H", k("eq1"), n), tile("H", k("eq2"), n), tile("F", k("ow"), n)
            grp = [(I, OFFM), (Iv, vs), (I16k, NL)]
            scan(T4, CAP, mmo(grp), -4096.0, "add", "min")
            tt(eq1, vs, T4, "is_equal")
            tt(sub(eq2, 16, n), sub(vs, 16, n), sub(T4, 0, n - 16), "is_equal")
            P = ps(n)
            mm([(P, l, r) for l, r in grp] + [None, (sub(P, 16, n), B8k, sub(eq2, 16, n)), (P, B8k, eq1)])
            scan(ow, DMP, P, -32768.0, "max", "min")
            off[x] = tile("U", k("off"), M6)
            ts(off[x], sub(ow, 15, n, 16), voff - 8192.0, None, "add")
        for x in order:
            cur[:] = [x, t, "scatter"]
            for c in (2, 1, 0):
                cp(("I", vtab, sub(off[x], 2 * c, 2 * c + 2)), sub(en[x], 32 * c, 32 * c + 32))
    cur[:] = [None, 4, "out"]
    for o, nm in ((outz, "yz"), (outf, "yf")):
        dma(D(nm, 192), o)
    for o, nm in ((outv, "yv"), (outc, "yc")):
        dma(D(nm, 192, 8), lane_rows(o, 0))
    cuts = (0, 256, 768, 1280, 1792, 2048)
    for c, (c0, c1) in enumerate(zip(cuts, cuts[1:])):
        q, o = ap("vps%d" % (c & 1), 0, c1 - c0), tile("F", ("yw", c), c1 - c0)
        if FT:
            q = ps(c1 - c0)
            act(q, sub(vtab, 2048 + c0, 2048 + c1), "Copy", 0.0, 4096.0)
        else:
            ts(q, sub(vtab, 2048 + c0, 2048 + c1), 4096.0, None, "mult")
        tt(o, sub(vtab, c0, c1), q, "add")
        dma(ap("yw", c0, c1), o, "YS"[c & 1])
    return ops, size


def pat(a):
    return a[7] if len(a) > 7 else 1


def cost(ins, GATHER, SCATTER, ISSUE):
    c = 0.0
    for i in ins:
        k = i[0]
        if k == "mm":
            f = 4 if i[2][1] == "F" else 1
            c += f * max(64, width(i[3])) * .42e-3
        elif k in ("iota", "asel"):
            c += .15 + 1.7e-3 * width(i[1])
        elif k == "dma":
            c += .06
        elif k == "rd":
            c += ISSUE
        elif i[1][0] == "I":
            c += .05 + SCATTER * width(i[1][2]) * 16 * .83e-3
        elif k != "ms" and i[2][0] == "I":
            c += (.065 if k == "act" else .05) + GATHER * width(i[2][2]) * 16 * .83e-3
        else:
            w = width(i[1])
            b16 = lambda a: a[1] in ("H", "U", "E")
            if k == "tt":
                ps_ = any(isinstance(a[1], tuple) or a[1] in ("vps0", "vps1") for a in i[2:4])
                w = w * (1 if ps_ else 2)
            elif k in ("cp", "ts") and b16(i[1]) and b16(i[2]) or k == "ms" and b16(i[1]):
                w = w * .5
            c += max(48, w) * .83e-3 + .05
    return c


SPEEDS = [(1.4, 1.6, 1.9, 5.0, 1.0, 2.0, .1, .2, 3e-3, .5e-3, .7, 1.0), (1.15, 2.0, 1.56, 3.8, .8, 1.6, .1, .2, 2e-3, .4e-3, .5, .6),
          (1.05, 1.05, 1.56, 3.8, .8, 1.6, .1, .2, 2e-3, .4e-3, .5, 1.2)]
LOADT, TEMP, HOLD0 = 2.0, .12, .5
BANKS, LAG, STEPS, SEED = 6, 5.0, 2000, 1


def analyse():
    ops, size = build()
    N = len(ops)
    hist = {}
    deps = [set() for _ in range(N)]
    tile_ops = {}
    for o in ops:
        i = o["i"]
        for kind, lst in (("r", o["rd"]), ("w", o["wr"])):
            for a in lst:
                buf = a[1]
                if isinstance(buf, tuple):
                    tile_ops.setdefault(buf, [])
                    if i not in tile_ops[buf]:
                        tile_ops[buf].append(i)
                for (lo, hi, k2, j, st) in hist.setdefault(buf, []):
                    two_ = isinstance(buf, tuple) and (ops[j]["e"] != o["e"] or "alt" in o or "alt" in ops[j])
                    if j != i and (k2 == "w" or kind == "w" or two_) and lo < a[5] and a[4] < hi:
                        if st == a[6] > 1 and (lo - a[4]) % st:
                            continue
                        deps[i].add(j)
        for kind, lst in (("r", o["rd"]), ("w", o["wr"])):
            for a in lst:
                hh = hist[a[1]]
                if kind == "w":
                    hist[a[1]] = hh = [e for e in hh if not (a[6] == 1 and a[2] == 0 and a[3] == 128 and pat(a) == 1 and a[4] <= e[0] and e[1] <= a[5])]
                hh.append((a[4], a[5], kind, i, a[6]))
    pool = [o["i"] for o in ops if o["e"] == "G" and not o.get("dma")]
    for a, b in zip(pool, pool[1:]):
        deps[b].add(a)
    more = []
    for scale, tensor, gather, scatter, issue, net, own, wake, link, load, rows_, weight in SPEEDS:
        both = [{e: cost(ins, gather, scatter, issue) * (1.0 if o.get("dma") else tensor if e == "P" else scale) + o.get("table", 0.0) for e, ins in o.get("alt", {o["e"]: o["ins"]}).items()} for o in ops]
        lat, wire = [0.0] * N, [0.0] * N
        for i, o in enumerate(ops):
            if o.get("dma"):
                a = o["wr"][0]
                size_ = width(a) * (2 if a[1] in ("H", "U", "E", "pxs") else 4) * (a[3] - a[2]) // pat(a) / 128
                if o["t"] < 0:
                    lat[i] = LOADT + (size_ + o.get("behind", 0)) * load
                else:
                    lat[i], wire[i] = (net, rows_ + size_ * link) if o.get("remote") else (LOADT, size_ * load)
        more.append((both, lat, wire, own, wake, weight))
    both, lat, wire, OWN, WAKE, _ = more.pop(0)
    cst = [b[o["e"]] for b, o in zip(both, ops)]
    pred = [[(d, 0 if ops[i].get("more") and d == i - 1 else 2 if ops[d].get("dma") else 1) for d in deps[i]] for i in range(N)]
    prio = [0.0] * N
    succ = [[] for _ in range(N)]
    for i in range(N):
        for j in deps[i]:
            succ[j].append(i)
    for i in range(N - 1, -1, -1):
        prio[i] = cst[i] + lat[i] + max([prio[s] + .1 for s in succ[i]] + [0.0])
    eng = [o["e"] for o in ops]
    opens = [None if o.get("more") else next((a[1] for a in o["wr"] if isinstance(a[1], tuple)), None) for o in ops]
    touch = [set(a[1] for a in o["rd"] + o["wr"] if isinstance(a[1], tuple)) for o in ops]
    gap = [[(q, 0.0 if ops[q].get("more") and q == i + 1 else WAKE if ops[i].get("dma") else OWN) for q in succ[i]] for i in range(N)]
    return dict(ops=ops, size=size, eng=eng, opens=opens, touch=touch, gap=gap, deps=deps, tile_ops=tile_ops, both=both, lat=lat, wire=wire, wired=[i for i in range(N) if wire[i]], prio=prio, more=more, pred=pred, wake=WAKE)


def schedule(an, prio, hold):
    tile_ops, lat, opens, touch, gap, WAKE, both = [an[k] for k in ("tile_ops", "lat", "opens", "touch", "gap", "wake", "both")]
    N, eng, wire, busy = len(both), list(an["eng"]), an["wire"], 0.0
    last, bfree = [None] * BANKS, [0.0] * BANKS
    bank_of, left = {}, {b: len(v) for b, v in tile_ops.items()}
    left[None] = 0
    fin, start, rt = [None] * N, [None] * N, [0.0] * N
    free, order, ready = [{e: v() for e in "VSPGY"} for v in (float, list, dict)]
    ndep = [len(d) for d in an["deps"]]

    def offer(i):
        if len(both[i]) > 1:
            ready["V"][i], ready["S"][i] = rt[i] + max(hold[i], 0.0), rt[i] + max(-hold[i], 0.0)
        else:
            ready[eng[i]][i] = rt[i]

    for i in range(N):
        if ndep[i] == 0:
            offer(i)
    for _ in range(N):
        bf, bk = 1e9, None
        for b in range(BANKS):
            if bfree[b] < bf and not left[last[b]]:
                bf, bk = bfree[b], b
        first, e = 1e9, None
        for q, lst in ready.items():
            if lst and free[q] < first:
                s = max(free[q], min([bf if opens[i] and bf > r else r for i, r in lst.items()]))
                if s < first:
                    first, e = s, q
        if e is None:
            return None
        lim = first + .02
        i = max([i for i, r in ready[e].items() if r <= lim and (bf <= lim or not opens[i])], key=lambda j: prio[j])
        s = max(ready[e][i], free[e], bf if opens[i] else 0.0)
        for q in both[i]:
            del ready[q][i]
        if opens[i]:
            last[bk], bank_of[opens[i]] = opens[i], bk
        start[i], free[e], eng[i] = s, s + both[i][e], e
        f = fin[i] = free[e] + lat[i]
        if wire[i]:
            busy = max(free[e], busy) + wire[i]
            f = fin[i] = busy + lat[i]
        for tb in touch[i]:
            left[tb] -= 1
            if f + WAKE > bfree[bank_of[tb]]:
                bfree[bank_of[tb]] = f + WAKE
        order[e].append(i)
        for q, w in gap[i]:
            w = f + (w if eng[q] == e else WAKE)
            if w > rt[q]:
                rt[q] = w
            ndep[q] -= 1
            if not ndep[q]:
                offer(q)
    order["Y"].sort(key=lambda i: (an["ops"][i]["t"] >= 0, start[i] if an["ops"][i]["t"] >= 0 else i))
    return dict(order=order, eng=eng, span=max(fin))


def tune(an, steps):
    seen, cls = {}, []
    for o in an["ops"]:
        k = (o["x"], o["t"], o["sec"], o["e"])
        seen[k] = seen.get(k, -1) + 1
        cls.append((o["x"], o["sec"], o["e"], seen[k], 0 <= o["t"] < 4))
    keys = sorted(set(cls), key=str)
    of = np.array([keys.index(c) for c in cls])
    sections = [[j for j, k in enumerate(keys) if k[:2] == s] for s in sorted(set(k[:2] for k in keys), key=str)]
    base, rng = np.array(an["prio"]), np.random.default_rng(SEED)
    shift = np.array([-LAG if k[0] == 0 else 0.0 for k in keys])
    free = sorted(set(of[i] for i, b in enumerate(an["both"]) if len(b) > 1))
    hold = np.full(len(keys), HOLD0)
    for (which, x), on in GATH.items():
        for c, e in enumerate(on):
            hold[keys.index((x, which, "S", c, True))] = {"S": 9.0, "V": -9.0, "?": HOLD0}[e]
    cur = best = schedule(an, list(base + shift[of]), list(hold[of]))
    while not cur:
        shift = shift + rng.normal(size=len(keys))
        cur = best = schedule(an, list(base + shift[of]), list(hold[of]))
    for step in range(steps):
        new, ho, r = shift.copy(), hold.copy(), rng.random()
        if r < .2:
            new[sections[rng.integers(len(sections))]] += rng.normal() * 2
        elif r < .45:
            ho[free[rng.integers(len(free))]] += rng.normal() * 1.5
        else:
            new[rng.integers(len(keys), size=(1, 1, 2, 4)[rng.integers(4)])] += rng.normal() * (.5, 2, 5)[rng.integers(3)]
        sc = schedule(an, list(base + new[of]), list(ho[of]))
        if sc and sc["span"] < cur["span"] + .3 * (1 - step / steps) * rng.exponential():
            cur, shift, hold = sc, new, ho
            if sc["span"] < best["span"]:
                best = sc
    return best


def play(an, order, eng, old=None, same=0):
    tile_ops, lat, opens, touch, gap, both, WAKE = [an[k] for k in ("tile_ops", "lat", "opens", "touch", "gap", "both", "wake")]
    N, wire = len(eng), an["wire"]
    if old:
        kept = old["kept"][:same // 64 + 1]
        last, bfree, bby, bank_of, left, rt, why, ndep, pos, free, prev = [a.copy() for a in kept.pop()]
        fin, start, extra, step = [old[k].copy() for k in ("fin", "start", "extra", "step")]
    else:
        kept, last, bfree, bby = [], [None] * BANKS, [0.0] * BANKS, [None] * BANKS
        bank_of, left = {}, {b: len(v) for b, v in tile_ops.items()}
        left[None] = 0
        fin, start, rt, extra, why, step = [0.0] * N, [0.0] * N, [0.0] * N, [()] * N, [None] * N, [0] * N
        ndep = [len(d) for d in an["deps"]]
        pos, free, prev = [0] * 5, [0.0] * 6, [None] * 5
    qs = [order[e] + [None] for e in "VSPGY"]
    for now in range(64 * len(kept), N):
        if not now & 63:
            kept.append([a.copy() for a in (last, bfree, bby, bank_of, left, rt, why, ndep, pos, free, prev)])
        s, e = 1e9, None
        for q in range(5):
            i = qs[q][pos[q]]
            if i is None or ndep[i]:
                continue
            c = rt[i] if rt[i] > free[q] else free[q]
            if opens[i]:
                bf, bk = 1e9, None
                for b in range(BANKS):
                    if bfree[b] < bf and not left[last[b]]:
                        bf, bk = bfree[b], b
                if bf > c:
                    c = bf
            if c < s:
                s, e = c, q
        if e is None:
            return None
        i = qs[e][pos[e]]
        pos[e] += 1
        if s > rt[i]:
            why[i] = prev[e] if s == free[e] else bby[bk]
        if opens[i]:
            extra[i] = tile_ops.get(last[bk], ())
            last[bk], bank_of[opens[i]] = opens[i], bk
        start[i], free[e], prev[e], step[i] = s, s + both[i][eng[i]], i, now
        f = fin[i] = free[e] + lat[i]
        if wire[i]:
            free[5] = max(free[e], free[5]) + wire[i]
            f = fin[i] = free[5] + lat[i]
        for tb in touch[i]:
            left[tb] -= 1
            b = bank_of[tb]
            if f + WAKE > bfree[b]:
                bfree[b], bby[b] = f + WAKE, i
        for q, w in gap[i]:
            w = f + (w if eng[q] == eng[i] else WAKE)
            if w > rt[q]:
                rt[q], why[q] = w, i
            ndep[q] -= 1
    return dict(order=order, start=start, fin=fin, extra=extra, bank_of=bank_of, span=max(fin), why=why, eng=eng, step=step, kept=kept)


def again(an, run, old=None, same=0):
    eng, extra, N = run["eng"], run["extra"], len(run["eng"])
    seq = sorted(range(N), key=lambda i: run["step"][i])[same:]
    before = [None] * N
    for lst in run["order"].values():
        for a, b in zip(lst, lst[1:]):
            before[b] = a
    run["more"], run["sum"] = [], run["span"]
    for m, (both, lat, wire, own, wake, weight) in enumerate(an["more"]):
        fin, why, done = [a.copy() for a in old["more"][m]] if old else ([0.0] * N, [None] * N, [0.0] * N)
        busy = max([fin[i] - lat[i] for i in an["wired"] if wire[i] and run["step"][i] < same] + [0.0])
        for i in seq:
            y = before[i]
            s = 0.0 if y is None else done[y]
            for d, kind in an["pred"][i]:
                w = fin[d] + (wake if eng[d] != eng[i] or kind == 2 else own * kind)
                if w > s:
                    s, y = w, d
            for d in extra[i]:
                if fin[d] + wake > s:
                    s, y = fin[d] + wake, d
            done[i] = s = s + both[i][eng[i]]
            if wire[i]:
                s = busy = max(s, busy) + wire[i]
            fin[i], why[i] = s + lat[i], y
        run["more"].append((fin, why, done))
        run["sum"] += weight * max(fin)
    return run


def refine(an, sc, steps):
    rng, deps = np.random.default_rng(SEED), an["deps"]
    cur = best = again(an, play(an, sc["order"], sc["eng"]))
    paths = None
    draws = rng.random((steps, 7)).tolist()
    for step in range(steps):
        draw = draws[step]
        pick = lambda a: a[int(draw.pop() * len(a))]
        if paths is None:
            paths = []
            for fin, why, _ in [(cur["fin"], cur["why"], 0)] + cur["more"]:
                i = fin.index(max(fin))
                paths.append([])
                while why[i] is not None:
                    if why[i] not in deps[i]:
                        paths[-1].append((why[i], i))
                    i = why[i]
        u, v = pick(pick(paths))
        order, eng, r, same = dict(cur["order"]), cur["eng"], draw.pop(), 1 << 20
        if r < .15:
            a = order[eng[u]][max(0, order[eng[u]].index(u) - pick((0, 0, 1, 2, 3, 5)))]
            if len(an["both"][a]) == 1:
                continue
            e = "V" if eng[a] == "S" else "S"
            p = order[eng[a]].index(a)
            same = min([cur["step"][i] for i in list(deps[a]) + order[eng[a]][max(0, p - 1):p]] + [cur["step"][a] if p else 0])
            order[eng[a]] = order[eng[a]][:p] + order[eng[a]][p + 1:]
            order[e] = sorted(order[e] + [a], key=lambda i: (cur["start"][i], i))
            eng, d = list(eng), pick((-1, 0, 0, 1))
            eng[a] = e
        elif r < .55:
            a, d = v if eng[u] == eng[v] else u, -pick((1, 1, 2, 3, 5))
        elif eng[u] != eng[v]:
            a, d = order[eng[v]][max(0, order[eng[v]].index(v) - pick(range(1, 8)))], pick((1, 2, 4, 8))
        else:
            k = pick((0, 0, 0, 1, 2))
            a, d = order[eng[u]][max(0, order[eng[u]].index(u) - k)], k + pick((1, 1, 2, 3, 5))
        if eng[a] == "Y":
            continue
        lst = order[eng[a]] = list(order[eng[a]])
        p = lst.index(a)
        if any(i in deps[a] for i in lst[max(0, p + d):p]) or any(a in deps[i] for i in lst[p + 1:p + d + 1]):
            continue
        lst.insert(max(0, p + d), lst.pop(p))
        p = min(p, p + d) - 1
        same = min(same, cur["step"][lst[p]]) if p >= 0 else 0
        new = play(an, order, eng, cur, same)
        if new and new["span"] < cur["span"] + 1 and again(an, new, cur, same)["sum"] < cur["sum"] - TEMP * (1 - step / steps) * math.log(draw.pop() + 1e-9):
            cur, paths = new, None
            if new["sum"] < best["sum"]:
                best = new
    return best


def plan():
    an = analyse()
    sc = refine(an, tune(an, STEPS), 15 * STEPS)
    sc["extra"] = [set(x) for x in sc["extra"]]
    ops, deps, order, extra, fin = an["ops"], an["deps"], sc["order"], sc["extra"], sc["fin"]
    N = len(ops)
    for o, e in zip(ops, sc["eng"]):
        o["e"], o["ins"] = e, o.get("alt", {e: o["ins"]})[e]
    cnt = {e: 0 for e in "VSPG"}
    end, K, clk, waits = {}, {e: {} for e in "VSPGY"}, [None] * N, [None] * N
    ndma = 0
    for e in "VSPGY":
        for i in order[e]:
            if ops[i].get("dma"):
                end[i] = (("d", ndma), 0)
                ndma += 1
            else:
                cnt[e] += len(ops[i]["ins"])
                end[i] = (e, cnt[e])
    todo = {e: list(order[e]) for e in order}
    emitted = set()
    while any(todo.values()):
        moved = False
        for e in "VSPGY":
            while todo[e] and all(d in emitted for d in deps[todo[e][0]] | extra[todo[e][0]]):
                i = todo[e].pop(0)
                ws = []
                dd = sorted(deps[i] | extra[i], key=lambda d: -fin[d])
                for d in dd:
                    s, c = end[d]
                    if K[e].get(s, -1) >= c or ops[i].get("more") and d == i - 1:
                        continue
                    ws.append(d)
                    for a, b in clk[d].items():
                        K[e][a] = max(K[e].get(a, -1), b)
                fw = {}
                for d in ws:
                    s, c = end[d]
                    if s not in fw or end[fw[s]][1] < c:
                        fw[s] = d
                waits[i] = list(fw.values())
                c = dict(K[e])
                c[end[i][0]] = max(c.get(end[i][0], -1), end[i][1])
                clk[i] = c
                emitted.add(i)
                moved = True
        assert moved
    return dict(ops=ops, size=an["size"], start=sc["start"], order=order, waits=waits, end=end, bank_of=sc["bank_of"], cnt=cnt, ndma=ndma, span=sc["span"])


PLAN = plan()
_s = PLAN["size"]
SCRATCH = {
    "pxs": ("sbuf", [128, 4096], "bfloat16"), "vws": ("sbuf", [128, 2048], "int32"), "vtab": ("sbuf", [128, 4096 + n], "float32" if FT else "int32"),
}
for _k in DT:
    if _s[_k]:
        SCRATCH[_k + "pool"] = ("sbuf", [128, _s[_k]], DT[_k])
for _k in ["ps%d" % _b for _b in range(6)] + ["vps0", "vps1"]:
    SCRATCH[_k] = ("psum", [128, 512], "float32")
SEMAPHORES = ["eV", "eS", "eP", "eG", "sent"] + ["d%d" % k for k in range(PLAN["ndma"])]


def rank_program(g, core, T, topo):
    rank = T.rank_of(core)
    if rank is None:
        return
    p = PLAN
    ops, bank_of, end = p["ops"], p["bank_of"], p["end"]
    q = {"V": g.vector, "S": g.scalar, "P": g.tensor, "G": g, "Y": g.sync}
    esem = {e: T.sem["e" + e] for e in "VSPG"}
    dst = T.cores[(rank + 3) % 8]
    rid, pid, _ = topo.addr(dst)
    mask, neng = topo.mask(core, dst), len(topo.engines(core, dst))

    def A(a):
        if not isinstance(a, tuple):
            return a
        if a[0] == "I":
            return A(a[1]).indirect(A(a[2]))
        buf = a[1]
        if isinstance(buf, tuple):
            t = T["ps%d" % bank_of[buf]]
        elif buf in DT:
            t = T[buf + "pool"]
        else:
            t = T[buf]
        if pat(a) > 1:
            return t[a[2]:a[3]:a[7], a[4]:a[5]]
        return t[a[2]:a[3], a[4]:a[5]] if a[6] == 1 else t[a[2]:a[3], a[4]:a[5]:a[6]]

    def op(s):
        return {"add": OP.add, "subtract": OP.subtract, "mult": OP.mult, "min": OP.min, "max": OP.max, "is_ge": OP.is_ge, "is_le": OP.is_le,
                "is_lt": OP.is_lt, "is_equal": OP.is_equal, "not_equal": OP.not_equal, "bitwise_and": OP.bitwise_and,
                "arith_shift_right": OP.arith_shift_right, "logical_shift_right": OP.logical_shift_right}[s]

    fun = {"Copy": AF.Copy, "Abs": AF.Abs, "Relu": AF.Relu, "Identity": AF.Identity, "Sigmoid": AF.Sigmoid}
    nsent = 0
    total = {}
    for e in "VSPGY":
        for i in p["order"][e]:
            o = ops[i]
            for d in p["waits"][i]:
                s, c = end[d]
                if s in esem:
                    q[e].wait_ge(esem[s], c)
                else:
                    q[e].wait_ge(T.sem["d%d" % s[1]], neng if ops[d].get("remote") else 16)
            for s in o["ins"]:
                k = s[0]
                if k == "dma":
                    x = q[e].dma_start(A(s[1]), A(s[2]))
                    x.then_inc(T.sem["d%d" % end[i][0][1]], 16)
                    total[end[i][0][1]] = 16
                    continue
                if k == "rd":
                    g.remote_dma(out_ap=A(s[1]), in_ap=A(s[2]), remote_sem=T.sem["d%d" % end[i][0][1]], local_sem=T.sem.sent, pid=pid, routing_id=rid, dma_engine_mask=mask)
                    nsent += neng
                    total[end[i][0][1]] = neng
                    continue
                if k == "tt":
                    x = g.vector.tensor_tensor(out=A(s[1]), in0=A(s[2]), in1=A(s[3]), op=op(s[4]))
                elif k == "ts":
                    if s[6] is None:
                        x = g.vector.tensor_scalar(out=A(s[1]), in0=A(s[2]), scalar1=A(s[3]), scalar2=None, op0=op(s[5]))
                    else:
                        x = g.vector.tensor_scalar(out=A(s[1]), in0=A(s[2]), scalar1=A(s[3]), scalar2=A(s[4]), op0=op(s[5]), op1=op(s[6]))
                elif k == "cp":
                    x = g.vector.tensor_copy(out=A(s[1]), in_=A(s[2]))
                elif k == "tr":
                    x = g.vector.transpose(out=A(s[1]), in_=A(s[2]))
                elif k == "ms":
                    x = g.vector.memset(A(s[1]), s[2])
                elif k == "scan":
                    x = g.vector.tensor_tensor_scan(out=A(s[1]), data0=A(s[2]), data1=A(s[3]), initial=s[4], op0=op(s[5]), op1=op(s[6]))
                elif k == "act":
                    x = g.scalar.activation(out=A(s[1]), in_=A(s[2]), func=fun[s[3]], bias=A(s[4]), scale=A(s[5]))
                elif k == "mm":
                    x = g.tensor.matmul(out=A(s[1]), lhsT=A(s[2]), rhs=A(s[3]), start=s[4], stop=s[5])
                elif k == "iota":
                    if s[1][1] in ("F", "H"):
                        x = g.iota(out=A(s[1]), pattern=s[2], base=s[3], channel_multiplier=s[4], allow_small_or_imprecise_dtypes=True)
                    else:
                        x = g.iota(out=A(s[1]), pattern=s[2], base=s[3], channel_multiplier=s[4])
                elif k == "asel":
                    x = g.affine_select(out=A(s[1]), in_=A(s[2]), pattern=s[3], compare_op=op(s[4]), fill=s[5], base=s[6], channel_multiplier=s[7])
                x.then_inc(esem[e], 1)
    for e in "VSPG":
        g.wait_ge(esem[e], p["cnt"][e])
    for k in sorted(total):
        g.wait_ge(T.sem["d%d" % k], total[k])
    g.wait_ge(T.sem.sent, nsent)
